import numpy as np, ml_dtypes
CORES = [3,11,19,27,35,43,51,59]
N = 8
BF = ml_dtypes.bfloat16
V, T, BACK, HOPS = 3072, 192, 96, (1, 1, 1, 1)
def wanted(rng, pm, n, share, e):
    u = rng.random((N, 8, 16, n)); v = np.where(rng.random((N, 8, 16, n)) < share, V * u ** e, V * u).astype(np.int64)
    return pm[np.arange(8)[:, None, None], np.minimum(v, V - 1)]
def parts(rng, share=0.3, e=4.0):
    pm = np.argsort(rng.random((8, V)), axis=-1)
    return (rng.integers(0, 16, (N, 8, 16, V)), rng.integers(0, 16, (N, 8, 16, V)), wanted(rng, pm, V, share, e),
            rng.integers(0, 16, (N, 8, 16, T)), wanted(rng, pm, T, share, e), rng.integers(10, 45, (N, 8, 1)), pm)
def worst(x):
    return np.where(x < 8, 15, 0)
def apart(x, d):
    c = x.copy(); left = d.copy()
    for i in range(16):
        up = 15 - x[i] >= x[i]; m = np.minimum(left, np.where(up, 15 - x[i], x[i]))
        c[i] = np.where(up, x[i] + m, x[i] - m); left = left - m
    return c
def pack(x, y, ap, c, al, th):
    def b(a): return np.ascontiguousarray(a.reshape(N, 128, -1)).astype(np.float32).astype(BF)
    def w(a): return np.ascontiguousarray(a.reshape(N, 128, -1)).astype(np.int32)
    return {"fx": b(x), "hx": b(y), "ha": w(ap), "vx": b(c), "va": w(al), "th": th.astype(np.int32)}
def setup_inputs(rng):
    x, y, ap, c, al, th, pm = parts(rng)
    return pack(x, y, ap, c, al, th)
def setup_inputs_ties(rng):
    x, y, ap, c, al, th, pm = parts(rng, 0.5, 6.0); s = rng.integers(1, 4, (1, 8, 1, 1))
    x = (x & 1) * s; y = (y & 1) * s; c = (c & 1) * s; th = s[:, :, 0] * rng.integers(0, 5, (N, 8, 1))
    i = rng.integers(0, T // 2, T); c[:, ::2] = c[:, ::2][..., i]; al[:, ::2] = al[:, ::2][..., i]
    ap[:, :, 8:] = ap[:, :, :8]; al[:, 1::2, 8:] = al[:, 1::2, :8]
    return pack(x, y, ap, c, al, th)
def setup_inputs_crowd(rng):
    x, y, ap, c, al, th, pm = parts(rng)
    n = rng.permutation(np.array([1, 2, 3, 7, 16, 64, 256, V // 2]))
    for g in range(8):
        q = pm[g, :n[g]]
        y[:, g][:, :, q] = worst(x[:, g][:, :, q])
        ap[:, g] = q[rng.integers(0, n[g], (N, 16, V))]; al[:, g] = q[rng.integers(0, n[g], (N, 16, T))]
    i = rng.integers(0, T // 4, T); j = int(np.argmin(n)); c[:, ::2] = c[:, ::2][..., i]; c[:, j] = c[:, j][..., rng.permutation(i)]
    return pack(x, y, ap, c, al, rng.integers(0, 12, (N, 8, 1)))
def setup_inputs_ends(rng):
    x, y, ap, c, al, th, pm = parts(rng); o = rng.permutation(8); h = V // 2
    g = o[0]
    ap[:, g] = rng.integers(0, 2, (N, 16, V)) * (V - 1); al[:, g] = rng.integers(0, 2, (N, 16, T)) * (V - 1)
    y[:, g][:, :, [0, V - 1]] = worst(x[:, g][:, :, [0, V - 1]]); th[:, g] = rng.integers(0, 6, (N, 1))
    g = o[1]
    p = rng.integers(0, 2, (16, 1)) * 15; x[:, g] = p; y[:, g] = 15 - p; c[:, g] = p; th[:, g] = 240
    g = o[2]
    for q in range(N):
        f = rng.permutation(V)[:T]; d = rng.integers(60, 101, T); more = rng.permutation(np.arange(T) & 1)
        y[q, g][:, f] = apart(x[q, g][:, f], d); c[q, g] = apart(x[q, g][:, f], d - th[q, g, 0] - more); al[q, g] = f[None, :]
    g = o[3]
    p = rng.integers(0, 2, (16, 1)) * 15; x[:, g] = p; y[:, g] = 15 - p; c[:, g] = p; th[:, g] = 239
    g = o[4]
    x[:, g] = np.where(rng.random((N, 16, V)) < 0.5, 0, x[:, g]); y[:, g] = x[:, g]; y[:, g][:, :, :h] = worst(x[:, g][:, :, :h]); th[:, g] = rng.integers(0, 20, (N, 1))
    for a, n in ((ap, V), (al, T)):
        a[:, g] = rng.integers(h, V, (N, 16, n)); m = rng.random((N, n)) < 0.5; v = rng.integers(0, h, (N, n))
        a[:, g, 0] = np.where(m, v, a[:, g, 0]); a[:, g, 15] = np.where(m, a[:, g, 15], v)
    g = o[5]
    ap[:, g] = ap[:, g, :1]; al[:, g] = al[:, g, :1]
    g = o[6]
    y[:, g] = x[:, g]; th[:, g] = 0
    for q in range(N):
        f = rng.integers(0, V, T); m = rng.random(T) < 0.75
        al[q, g] = f[None, :]; c[q, g] = np.where(m[None, :], x[q, g][:, f], c[q, g])
    g = o[7]
    y[:, g] = x[:, g]; th[:, g] = rng.integers(0, 16, (N, 1)); R = len(HOPS); S = [sum(HOPS[:j]) for j in range(R)]
    o7 = rng.permutation(V); rest = o7[N + N * R:]
    ap[:, g] = rest[rng.integers(0, len(rest), (N, 16, V))]; al[:, g] = rest[rng.integers(0, len(rest), (N, 16, T))]
    for q in range(N):
        a = o7[q]; y[q, g][:, [a]] = apart(x[q, g][:, [a]], np.array([120]))
        for j in range(R):
            s = (q - S[j]) % N; t = q * R + j; home = apart(x[q, g][:, [a]], np.array([104 - 16 * j]))[:, 0]
            way = [(s + S[i]) % N for i in range(j)]; seen = [i for i in range(j) if way[i] == q]
            if not seen:
                c[s, g, :, t] = home; al[s, g, :, t] = a
            else:
                w = [way[m] for m in range(seen[-1] + 1, j) if way[m] not in way[:m]][0]; b = o7[N + t]
                x[w, g, :, b] = worst(home); y[w, g, :, b] = home; ap[w, g, :, b] = a
                c[s, g, :, t] = x[w, g, :, b]; al[s, g, :, t] = b
    return pack(x, y, ap, c, al, th)
def setup_inputs_full(rng):
    x, y, ap, c, al, th, pm = parts(rng); y = x.copy(); th = rng.integers(0, 60, (N, 8, 1)); z = rng.integers(0, 2, 8); q0 = int(rng.integers(0, N))
    for q in range(N):
        kinds = rng.permutation(np.array([0, 0, 1, 2, 3, 3, 4, 4]))
        for g in range(8):
            e = int(z[g] + q) % 2; kind = 0 if q == q0 else int(kinds[g])
            y[q, g][:, e::2] = worst(x[q, g][:, e::2]); far = e + 2 * rng.permutation(V // 2)
            f = far[:T]; d = rng.integers(0, 60, T)
            if kind == 1:
                n = min(T, V // 16); r = e + 2 * int(rng.integers(0, 8)); f = rng.permutation((r + 16 * rng.permutation(V // 16)[:n])[np.arange(T) % n])
            if kind == 2:
                f = e + 2 * (rng.permutation(T) + int(rng.integers(0, 2)) * (V // 2 - T))
            if kind == 3:
                tt = np.sort(rng.permutation(T).reshape(-1, 2), axis=1); f = np.zeros(T, np.int64); f[tt] = far[:T // 2][:, None]; d[tt] = rng.integers(0, 30, tt.shape) + np.array([30, 0])
            if kind == 4:
                a = far[0]; x[q, g, :, a] = 15 * rng.integers(0, 2, 16); y[q, g, :, a] = 15 - x[q, g, :, a]; th[q, g] = 0
                f = np.full(T, a); d = np.maximum(min(T, 240) - 1 - np.arange(T), 0)
            c[q, g] = apart(x[q, g][:, f], d); al[q, g] = f[None, :]
    return pack(x, y, ap, travel(c, -HOPS[0]), travel(al, -HOPS[0]), th)
def setup_inputs_spread(rng):
    x, y, ap, c, al, th, pm = parts(rng)
    def f(n): return np.minimum((np.exp2(4 * rng.random((N, 8, 1, n))) * rng.random((N, 8, 16, n)) + 0.5).astype(np.int64), 15)
    x = f(V); y = f(V); c = f(T); y = np.where(rng.random((N, 8, 1, V)) < 0.1, worst(x), y)
    ap = wanted(rng, pm, V, 0.8, np.exp2(4 * rng.random((N, 8, 1, V)))); al = wanted(rng, pm, T, 0.8, np.exp2(4 * rng.random((N, 8, 1, T))))
    th = (120 * rng.random((N, 8, 1)) ** 3).astype(np.int64); th[:, rng.integers(0, 8)] = 0
    return pack(x, y, ap, c, al, th)
def check_inputs(d):
    bad = []
    for k in ("fx", "hx", "vx"):
        v = np.asarray(d[k]).astype(np.float64)
        if not np.all((v >= 0) & (v <= 15) & (v == np.floor(v))): bad.append("whole numbers of " + k)
    for k, hi in (("ha", V - 1), ("va", V - 1), ("th", 240)):
        if np.min(d[k]) < 0 or np.max(d[k]) > hi: bad.append("range of " + k)
    return bad
def travel(a, h):
    b = np.roll(a, h, axis=0)
    if BACK: b[..., T - BACK:] = np.roll(a[..., T - BACK:], -h, axis=0)
    return b
def reference(fx, hx, ha, vx, va, th):
    x = fx.astype(np.float32).astype(np.int32).reshape(N, 8, 16, V)
    y = hx.astype(np.float32).astype(np.int32).reshape(N, 8, 16, V)
    ap = ha.astype(np.int64).reshape(N, 8, 16, V)
    hid = np.zeros((N, 8, V), np.int64) + np.arange(N)[:, None, None] * V + np.arange(V)
    c = vx.astype(np.float32).astype(np.int32).reshape(N, 8, 16, T)
    al = va.astype(np.int64).reshape(N, 8, 16, T)
    tid = np.zeros((N, 8, T), np.int64) + N * V + np.arange(N)[:, None, None] * T + np.arange(T)
    length = np.zeros((N, 8, T), np.int64); lim = th.astype(np.int64)
    ri = np.arange(N)[:, None, None]; gi = np.arange(8)[None, :, None]
    for h in HOPS:
        own = np.add.reduce(np.abs(x - y), axis=2)
        xa = np.take_along_axis(x, al.reshape(N, 8, 1, 16 * T), 3).reshape(N, 8, 16, 16, T)
        there = np.add.reduce(np.abs(xa - c[:, :, :, None, :]), axis=2)
        gain = np.take_along_axis(own, al.reshape(N, 8, 16 * T), 2).reshape(N, 8, 16, T).astype(np.int64) - there
        k = np.argmax(gain, axis=2)[:, :, None]
        best = np.take_along_axis(gain, k, 2)[:, :, 0]; fam = np.take_along_axis(al, k, 2)[:, :, 0]
        offer = best > lim
        key = np.where(offer, best * T + (T - 1 - np.arange(T)), -1)
        top = np.full((N, 8, V), -1, np.int64); np.maximum.at(top, (ri, gi, fam), key)
        n_, g_, t_ = np.nonzero(offer & (np.take_along_axis(top, fam, 2) == key)); f_ = fam[n_, g_, t_]
        old = y[n_, g_, :, f_]; y[n_, g_, :, f_] = c[n_, g_, :, t_]; c[n_, g_, :, t_] = old
        old = ap[n_, g_, :, f_]; ap[n_, g_, :, f_] = al[n_, g_, :, t_]; al[n_, g_, :, t_] = old
        old = hid[n_, g_, f_]; hid[n_, g_, f_] = tid[n_, g_, t_]; tid[n_, g_, t_] = old
        length[n_, g_, t_] += 1
        c = travel(c, h); al = travel(al, h); tid = travel(tid, h); length = travel(length, h)
    return {"yh": hid.astype(np.float32), "yt": tid.astype(np.float32), "yl": length.astype(np.float32)}

@@ -1,0 +1,425 @@
+from concourse.bass import DstId, RemoteDMATransfer
+from concourse.mybir import AluOpType as ALU, AxisListType as AX, ActivationFunctionType as AF
+
+V, NT, HALF, NR = 3072, 192, 96, 4
+W = V + NT
+F, B, I, U = "float32", "bfloat16", "int32", "uint16"
+
+SCRATCH = {}
+for _dt, _bufs in (
+    (F, dict(sw=[W], alL=[NR, 224], inf=[NR + 1, NT], outA=[NR - 1, NT], outI=[NR, NT], tt=[416], scn=[256], s8=[64], lose=[16],
+             f1=[16], f2=[16], f3=[16], f4=[16], pos=[16], zz=[16], ee=[256], leno=[NT], vv=[NT], pf=[8], j16=[12], g1=[12], g3=[12],
+             g6=[24], g7=[12], g8=[12], gcol=[128], thf=[4], tq=[6, 8], cols=[12], kcol=[256], em=[256], rm=[256],
+             scl=[160], idf=[128], wf=[2, 128], dt0=[16], lai=[12], rsi=[24], rs=[24], dc=[12])),
+    (B, dict(xw=[W], yw=[W], mx=[V], sg=[V], cL=[NR, 768], outC=[NR - 1, NT], dd=[16, 16], rb=[NT], le=[NT], lo=[NT], junk=[8, NT],
+             mst=[NT], crow=[512], wc=[6, 128], wab=[144], wm=[8], ws=[8], wsc=[128], ones=[256], kc=[256], m8=[256], s17=[96],
+             th8=[256], idb=[128])),
+    (I, dict(aw=[W], vai=[NT], rr=[160], pidx=[4], pi3=[8], g2=[12], g4=[12], g5=[24], thi=[4], lei=[16])),
+    (U, dict(off=[NT], lst=[12], gl=[12], la=[12], lel=[16])),
+):
+    for _k, _s in _bufs.items():
+        SCRATCH[_k] = ("sbuf", [128] + _s, _dt)
+for _b in range(8):
+    SCRATCH["pb%d" % _b] = ("psum", [128, 512], F)
+
+SEMAPHORES = (["cv", "ca", "cp", "cg", "sent"] + ["d%d" % _i for _i in range(24)]
+              + ["ra%d" % _i for _i in range(3)] + ["rc%d" % _i for _i in range(3)] + ["ri%d" % _i for _i in range(4)])
+
+S16 = 65536.0
+GS = 17 * 4096.0
+Z = 4096.0
+R_A, R_B, R_HI, R_LO, R_ID, R_LEN = 0, 1, 2, 3, 4, 5
+C_WE, C_WO, C_CE, C_CO, C_MR, C_CR, C_VB, C_ID, C_LEN = range(9)
+P_G, P_H, P_M, P_12, P_14, P_S1, P_S2 = range(7)
+
+
+def rank_program(g, core, T, topo):
+    rank = T.rank_of(core)
+    if rank is None:
+        return
+    n_ranks = len(T.cores)
+    nxt, prv = T.cores[(rank + 1) % n_ranks], T.cores[(rank - 1) % n_ranks]
+    queues = {"v": g.vector, "a": g.scalar, "p": g.tensor, "g": g, "s": g.sync}
+    csem = {"v": "cv", "a": "ca", "p": "cp", "g": "cg"}
+    count = {}
+    waited = {q: {} for q in queues}
+    lastw, readers = {}, {}
+    ndma = [0]
+
+    def need(q, toks):
+        top = {}
+        for (sem, val, owner) in toks:
+            if q == "p" and owner == "p":
+                continue
+            if val > top.get(sem, 0):
+                top[sem] = val
+        for sem, val in top.items():
+            if waited[q].get(sem, 0) < val:
+                queues[q].wait_ge(T.sem[sem], val)
+                waited[q][sem] = val
+
+    def order(q, rd, wr):
+        toks = []
+        for k in rd:
+            if k in lastw:
+                toks.append(lastw[k])
+            if k.startswith("pb"):
+                toks += [t for t in readers.get(k, []) if t[2] != q]
+        for k in wr:
+            if k in lastw:
+                toks.append(lastw[k])
+            toks += readers.get(k, [])
+        need(q, toks)
+
+    def done(tok, rd, wr):
+        for k in rd:
+            readers.setdefault(k, []).append(tok)
+        for k in wr:
+            lastw[k] = tok
+            readers[k] = []
+
+    def op(q, rd, wr, call):
+        if q == "g":
+            wr = wr + ["pool"]
+        order(q, rd, wr)
+        sem = csem[q]
+        count[sem] = count.get(sem, 0) + 1
+        call().then_inc(T.sem[sem], 1)
+        done((sem, count[sem], q), rd, wr)
+
+    def dma(q, rd, wr, out, in_, **kw):
+        order(q, rd, wr)
+        sem = "d%d" % ndma[0]
+        ndma[0] += 1
+        count[sem] = 16
+        queues[q].dma_start(out, in_, **kw).then_inc(T.sem[sem], 16)
+        done((sem, 16, "dma"), rd, wr)
+
+    def send(rd, src, dst, sem, key):
+        order("g", rd, [])
+        trs, sent = [], 0
+        for h, to in enumerate((nxt, prv)):
+            eng = topo.engines(core, to)
+            eng = eng[h * (len(eng) // 2):(h + 1) * (len(eng) // 2)]
+            rid, pid = topo.addr(to)[0:2]
+            trs.append(RemoteDMATransfer(dst_ids=[DstId(rid=rid, pnc=pid)], dma_engine_mask=sum(1 << e for e in eng),
+                                         remote_sem=T.sem[sem], src=src(h), dst=dst(h)))
+            sent += len(eng)
+        g.remote_dma_fused(trs, local_sem=T.sem.sent)
+        count["sent"] = count.get("sent", 0) + sent
+        count[sem] = len(topo.engines(prv, core)) // 2 + len(topo.engines(nxt, core)) // 2
+        lastw[key] = (sem, count[sem], "remote")
+
+    vec, act, pe = g.vector, g.scalar, g.tensor
+
+    def mset(ap, val, wr):
+        op("v", [], wr, lambda: vec.memset(ap, val))
+
+    def ts(out, in0, s1, s2, o0, o1, rd, wr):
+        if o1 is None:
+            op("v", rd, wr, lambda: vec.tensor_scalar(out, in0, s1, None, o0))
+        else:
+            op("v", rd, wr, lambda: vec.tensor_scalar(out, in0, s1, s2, o0, o1))
+
+    def tt(out, in0, in1, o, rd, wr):
+        op("v", rd, wr, lambda: vec.tensor_tensor(out, in0, in1, o))
+
+    def cp(out, in_, rd, wr):
+        op("v", rd, wr, lambda: vec.tensor_copy(out, in_))
+
+    def ac(out, in_, func, rd, wr, **kw):
+        op("a", rd, wr, lambda: act.activation(out, in_, func, **kw))
+
+    def aset(ap, src, val, wr):
+        ac(ap, src, AF.Identity, ["ones"], wr, scale=0.0, bias=val)
+
+    def mm(out, lhsT, rhs, start, stop, rd, wr):
+        op("p", rd, wr, lambda: pe.matmul(out, lhsT, rhs, start, stop))
+
+    def iota(out, pat, base, ch, wr, flag=True):
+        if flag:
+            op("g", [], wr, lambda: g.iota(out, pat, base, ch, allow_small_or_imprecise_dtypes=True))
+        else:
+            op("g", [], wr, lambda: g.iota(out, pat, base, ch))
+
+    def sel(out, in_, pat, cmp, fill, base, ch, rd, wr):
+        op("g", rd, wr, lambda: g.affine_select(out, in_, pat, cmp, fill, base, ch))
+
+    pb = [T["pb%d" % b] for b in range(8)]
+    X3, Y3 = ["x0", "x1", "x2", "x3"], ["y0", "y1", "y2", "y3"]
+    part = (0, 0, 1, 1, 2, 3)
+    S6 = ["s%d" % j for j in range(6)]
+    MX = ["mx%d" % k for k in range(16)]
+    SCL = ["scl%d" % j for j in range(6)]
+
+    def pc(j):
+        return T.pf[:, j:j + 1]
+
+    def col(j):
+        return T.cols[:, j:j + 1]
+
+    for j, (a, b) in enumerate(((0, 1024), (1024, 2048), (2048, 2560), (2560, V))):
+        dma("a", [], [Y3[j]], T.yw[:, a:b], T.hx[:, a:b])
+        dma("s", [], [X3[j]], T.xw[:, a:b], T.fx[:, a:b])
+        if j == 0:
+            dma("s", [], ["vai"], T.vai[:], T.va[:])
+    dma("a", [], ["c0"], T.cL[:, 0, 0:NT], T.vx[:])
+    dma("s", [Y3[3], X3[3]], ["aw"], T.aw[:, 0:V], T.ha[:])
+    dma("s", [], ["ad"], T.aw[:, V:W], T.va[:])
+    dma("s", [], ["yd"], T.yw[:, V:W], T.vx[:])
+
+    iota(T.pidx[:, 0:1], [[0, 1]], 0, 1, ["pidx"], flag=False)
+    mset(T.ones[:], 1.0, ["ones"])
+    mset(T.crow[0:64, :], 0.0, ["crow"])
+    mset(T.wc[0:96, :, :], 0.0, ["wc"])
+    iota(T.gcol[:], [[1, 8], [0, 16]], 0, 0, ["gcol"])
+    CR = ["cr%d" % j for j in range(10)]
+    WCK = ["wa%d" % j for j in range(8)]
+    for k in CR:
+        lastw[k] = lastw["crow"]
+    for k in WCK:
+        lastw[k] = lastw["wc"]
+    iota(T.crow[32:33, 0:64], [[1, 64]], 0, 0, [CR[0]])
+    iota(T.j16[:], [[16, 12]], 0, 0, ["j16"])
+    iota(T.wc[64:65, :, R_HI::16], [[8, 6], [0, 8]], -24, 0, [WCK[6]])
+    iota(T.wc[64:65, :, R_ID::16], [[512, 6], [0, 8]], V * rank, 0, [WCK[7]])
+    sel(T.idb[:], T.ones[:, 0:128], [[-1, 128]], ALU.is_equal, 0.0, 0, 1, ["ones"], ["idb"])
+    dma("g", [], ["thi"], T.thi[0:8, 0:1], T.th[:], allow_slow_non_contiguous=True)
+    for j in range(1, 8):
+        aset(T.crow[0:1, 64 * j:64 * (j + 1)], T.ones[0:1, 0:64], float(j), [CR[j]])
+        if j in (3, 5, 7):
+            w = 64 << (j // 2 - 1)
+            ac(T.crow[32:33, w:2 * w], T.crow[32:33, 0:w], AF.Copy, [CR[0]], [CR[0]])
+    mset(T.crow[64:65, :], 1.0, [CR[8]])
+    for j, (p, r, val) in enumerate(((0, R_HI, 1.0), (0, R_ID, 64.0), (32, R_LO, 1.0), (32, R_ID, 1.0), (64, R_A, -120.0), (64, R_LEN, 1.0))):
+        mset(T.wc[p:p + 1, :, r::16], val, [WCK[j]])
+    ts(T.pi3[:, 0:1], T.pidx[:, 0:1], 4, None, ALU.arith_shift_right, None, ["pidx"], ["pi0"])
+    ts(T.pi3[:, 1:2], T.pidx[:, 0:1], 4, 1, ALU.arith_shift_right, ALU.bitwise_and, ["pidx"], ["pi1"])
+    for j, m in ((P_M, 15), (P_12, 12), (P_14, 14)):
+        ts(T.pi3[:, j:j + 1], T.pidx[:, 0:1], m, None, ALU.bitwise_and, None, ["pidx"], ["pi%d" % j])
+    mset(T.wab[:], 0.0, ["wab"])
+    cp(T.pf[:, 0:5], T.pi3[:, 0:5], ["pi0", "pi1", "pi2", "pi3", "pi4"], ["pf"])
+    aset(T.alL[:, :, 0:16], T.ones[:, 0:64], 0.0, ["pad0"])
+    aset(T.alL[:, :, 208:224], T.ones[:, 0:64], 0.0, ["pad1"])
+    aset(T.ws[:], T.ones[:, 0:8], 0.0, ["ws"])
+    aset(T.tq[:], T.ones[:, 0:48], 0.0, ["tq"])
+    aset(T.s17[0:8, :], T.ones[0:8, 0:96], 17.0, ["s17"])
+    aset(T.rm[:], T.ones[:], 0.0, ["rm"])
+    for j in range(4):
+        aset(T.scl[:, j:64:4], T.ones[:, 0:16], 8.0 ** -j, ["scl%d" % j])
+    aset(T.rm[:, 0::16], T.ones[:, 0:16], -1.0e9, ["rm"])
+    aset(T.scl[:, 128:160], T.ones[:, 0:32], 1.0 / GS, ["scl5"])
+    ac(T.scl[:, 64:128], T.scl[:, 0:64], AF.Identity, SCL[0:4], ["scl4"], scale=0.125)
+    aset(T.zz[96:128, :], T.ones[96:128, 0:16], 0.0, ["zzp"])
+    aset(T.scn[96:128, :], T.ones[96:128, :], 0.0, ["scp"])
+    aset(T.xw[:, V:W], T.ones[:, 0:NT], 0.0, ["xd"])
+    ts(T.wab[:, 1:129:16], T.gcol[:, 0::16], pc(P_G), None, ALU.is_equal, None, ["gcol", "pf"], ["wab"])
+    ts(T.g1[:], T.j16[:], pc(P_M), None, ALU.add, None, ["j16", "pf"], ["g1"])
+    ts(pc(P_S1), pc(P_H), -416.0, 224.0, ALU.mult, ALU.add, ["pf"], ["pf1"])
+    ts(pc(P_S2), pc(P_H), 208.0, None, ALU.mult, None, ["pf"], ["pf2"])
+    ts(T.g2[:], T.g1[:], -5.5, 1.0 / 12.0, ALU.add, ALU.mult, ["g1"], ["g2"])
+    ts(T.wm[:], T.gcol[:, 0::16], pc(P_G), -2.0 * GS, ALU.is_equal, ALU.mult, ["gcol", "pf"], ["wm"])
+    ts(T.g3[:], T.g2[:], -12.0, None, ALU.mult, None, ["g2"], ["g3"])
+    ts(T.g8[:, 0:1], pc(P_12), 4.0, None, ALU.mult, None, ["pf"], ["g8a"])
+    tt(T.g4[:], T.g3[:], T.g1[:], ALU.add, ["g3", "g1"], ["g4"])
+    ts(T.wsc[:], T.gcol[:], pc(P_G), GS, ALU.is_equal, ALU.mult, ["gcol", "pf"], ["wsc"])
+    ts(T.g5[:, 0:12], T.g4[:], 1, None, ALU.arith_shift_right, None, ["g4"], ["g5a"])
+    ts(T.g5[:, 12:24], T.g4[:], 1, None, ALU.bitwise_and, None, ["g4"], ["g5b"])
+    ts(T.g8[:, 1:2], pc(P_14), 8.0, None, ALU.mult, None, ["pf"], ["g8b"])
+    ts(T.g6[:, 0:12], T.g5[:, 0:12], 32.0, None, ALU.mult, None, ["g5a"], ["g6a"])
+    ts(T.g6[:, 12:24], T.g5[:, 12:24], pc(P_S1), pc(P_S2), ALU.mult, ALU.add, ["g5b", "pf1", "pf2"], ["g6b"])
+    ts(T.dc[:], T.j16[:], pc(P_M), V + 15 * 8192.0, ALU.add, ALU.add, ["j16", "pf"], ["dc"])
+    tt(T.g7[:], T.g6[:, 0:12], T.g2[:], ALU.add, ["g6a", "g2"], ["g7"])
+    tt(T.g3[:], T.g7[:], T.g6[:, 12:24], ALU.add, ["g7", "g6b"], ["g3"])
+    cp(T.gl[:], T.g3[:], ["g3"], ["gl"])
+
+    def lists(n):
+        op("v", ["al%d" % n], ["tt1"], lambda: vec.transpose(T.tt[:, 0:192], T.alL[:, n, 16:208]))
+        op("v", ["al%d" % n, "pad0", "pad1"], ["tt2"], lambda: vec.transpose(T.tt[:, 192:416], T.alL[:, n, 0:224]))
+        cp(T.off[:], T.tt[:, 0:416].indirect(T.gl[:]), ["tt1", "tt2", "gl"], ["off"])
+
+    def copies(n):
+        sel(T.cL[:, n, 192:384], T.cL[:, n, 0:192], [[0, 192]], ALU.is_ge, 0.0, 0, 0, ["c%d" % n], ["c%db" % n])
+        sel(T.cL[:, n, 384:768], T.cL[:, n, 0:384], [[0, 384]], ALU.is_ge, 0.0, 0, 0, ["c%d" % n, "c%db" % n], ["c%dc" % n])
+
+    for j in range(6):
+        mm(pb[j][:], T.wc[0:65, j, :], T.crow[0:65, :], True, False, CR + WCK, ["pb%d" % j])
+
+    iota(T.kc[0:1, :], [[0, 16], [-4096, 16]], 28672, 0, ["kc"])
+    sel(T.m8[0:8, :], T.ones[0:8, :], [[0, 2], [-1, 8], [0, 16]], ALU.is_equal, 0.0, 0, 1, ["ones"], ["m8"])
+    iota(T.lai[:, 0:8], [[0, 2], [64, 4]], 15, 0, ["lai0"])
+    iota(T.lai[:, 8:10], [[128, 2]], 15, 0, ["lai1"])
+    iota(T.lei[:], [[1, 16]], 0, 0, ["lei"], flag=False)
+    iota(T.rsi[:], [[-6, 2], [1, 12]], 0, 0, ["rsi"])
+    iota(T.kcol[:], [[0, 16], [1, 16]], 0, 0, ["kcol"])
+    for r, val in ((R_A, 2.0 * GS), (R_B, -GS), (R_HI, 64.0), (R_LO, 1.0)):
+        sel(T.ws[:], T.ws[:], [[-16, 8]], ALU.not_equal, val, -r, 1, ["ws"], ["ws"])
+    copies(0)
+    steps = {0: ((0, 2 * S16 * Z), (4, 0.0), (10, -256 * Z), (11, -S16 * Z), (15, -Z), (16, 0.0)),
+             1: ((4, -S16 * Z), (8, Z), (9, 256 * Z), (10, 0.0)), 2: ((0, 1.0), (10, 0.0))}
+    for j in range(6):
+        lastw["tq%d" % j] = lastw["tq"]
+    for i in range(6):
+        for j in steps:
+            if i < len(steps[j]):
+                sel(T.tq[:, j, :], T.tq[:, j, :], [[16, 8]], ALU.is_ge, steps[j][i][1], steps[j][i][0] - 1, -1, ["tq%d" % j], ["tq%d" % j])
+    for j, r, val in ((3, R_A, -120.0), (4, R_ID, 1.0), (5, R_LEN, 1.0), (3, R_LEN, 1.0)):
+        sel(T.tq[:, j, :], T.tq[:, j, :], [[-16, 8]], ALU.not_equal, val, -r, 1, ["tq%d" % j], ["tq%d" % j])
+    iota(T.dd[:, :, 8::7], [[-HALF, 2], [0, 8], [0, 2]], NT - 1, -1, ["dtie"])
+    iota(T.inf[:, 0, :], [[1, NT]], n_ranks * V + NT * rank, 0, ["inf0"])
+    iota(T.dt0[:], [[HALF, 2], [0, 8]], V // 2, 1, ["dt0"])
+    sel(T.idf[:], T.ones[:, 0:128], [[-1, 128]], ALU.is_equal, 0.0, 0, 1, ["ones"], ["idf"])
+    iota(T.wf[:], [[0, 256]], 0, 0, ["wf"])
+    for j, r in ((0, R_HI), (1, R_ID), (0, R_LO)):
+        sel(T.wf[:, j, r::16], T.wf[:, j, r::16], [[-16, 8]], ALU.not_equal, 1.0, -r, 1, ["wf"], ["wf"])
+
+    fill = [
+        lambda: cp(T.alL[:, 0, 16:208], T.vai[:], ["vai"], ["al0"]),
+        lambda: lists(0),
+        lambda: cp(T.lel[:], T.lei[:], ["lei"], ["lel"]),
+        lambda: ts(T.la[:, 0:8], T.lai[:, 0:8], T.g8[:, 0:1], None, ALU.add, None, ["lai0", "g8a"], ["la0"]),
+        lambda: ts(T.la[:, 8:10], T.lai[:, 8:10], T.g8[:, 1:2], None, ALU.add, None, ["lai1", "g8b"], ["la1"]),
+        lambda: ts(T.rs[:], T.rsi[:], pc(P_G), -1.0, ALU.is_equal, ALU.mult, ["rsi", "pf"], ["rs"]),
+        lambda: ts(T.em[:], T.kcol[:], pc(P_M), 8192.0, ALU.not_equal, ALU.mult, ["kcol", "pf"], ["em"]),
+        lambda: ts(T.thf[0:8, 0:1], T.thi[0:8, 0:1], -GS / 17, 240.0 * GS / 17, ALU.mult, ALU.add, ["thi"], ["thf"]),
+        lambda: ts(T.th8[0:8, :], T.m8[0:8, :], T.thf[0:8, 0:1], None, ALU.mult, None, ["m8", "thf"], ["th8"]),
+    ]
+    cuts = (0, 0, 2, 2, 6, 8, 9)
+
+    def ycopy(j):
+        mm(pb[6 + j % 2][:], T.idb[:], T.yw[:, 512 * j:512 * (j + 1)], True, True, ["idb", Y3[part[j]]], ["pb%d" % (6 + j % 2)])
+
+    ycopy(0)
+    ycopy(1)
+    for j in range(6):
+        a, b = 512 * j, 512 * (j + 1)
+        tt(T.mx[:, a:b], T.xw[:, a:b], pb[6 + j % 2][:], ALU.max, [X3[part[j]], "pb%d" % (6 + j % 2)], ["im%d" % j])
+        mm(pb[j][:], T.wab[:, 0:128], T.yw[:, a:b], False, False, ["wab", Y3[part[j]]], ["pb%d" % j])
+        if j in (1, 3, 4):
+            ycopy(j + 1)
+        mm(pb[j][:], T.wab[:, 1:129], T.mx[:, a:b], False, True, ["wab", "im%d" % j], ["pb%d" % j])
+        for k in MX[a // 192:(b - 1) // 192 + 1]:
+            readers.setdefault(k, []).append(lastw["pb%d" % j])
+        if j == 1:
+            ycopy(j + 2)
+        ac(T.sw[:, a:b], pb[j][:], AF.Copy, ["pb%d" % j], [S6[j]])
+        for f in fill[cuts[j]:cuts[j + 1]]:
+            f()
+
+    def late_constants():
+        for c, ap, key in ((C_WE, T.tq[:, 0, 0::2], 0), (C_WO, T.tq[:, 0, 1::2], 0), (C_CE, T.tq[:, 1, 0::2], 1), (C_CO, T.tq[:, 1, 1::2], 1),
+                           (C_MR, T.tq[:, 2, :], 2), (C_VB, T.tq[:, 3, :], 3), (C_ID, T.tq[:, 4, :], 4), (C_LEN, T.tq[:, 5, :], 5)):
+            op("v", ["tq%d" % key], ["col%d" % c], lambda c=c, ap=ap: vec.tensor_reduce(col(c), ap, AX.X, ALU.add))
+        ts(col(C_CR), col(C_MR), -1.0, 1.0, ALU.mult, ALU.add, ["col%d" % C_MR], ["col%d" % C_CR])
+
+    chunks = ((0, 1), (1, 2), (2, 4), (4, 6), (6, 10), (10, 14), (14, 15), (15, 16))
+    achunks = ((0, 5), (5, 10), (10, 13), (13, 15), (15, 16))
+    towns = (0, 2, 4, 6, 1, 3, 5, 7)
+    bank = dict(zip(towns, (4, 3, 5, 6, 7, 0, 2, 1)))
+    on_vector = (2, 6, 3, 7)
+
+    for n in range(NR):
+        last = n == NR - 1
+        cn, an, fn = "c%d" % n, "al%d" % n, "inf%d" % n
+        cc = T.cL[:, n, 0:NT]
+        if n > 0:
+            lists(n)
+            copies(n)
+            if not last:
+                dma("s", [cn], ["yd"], T.yw[:, V:W], cc)
+        mm(pb[0][0:96, 0:256], T.s17[0:8, :], T.th8[0:8, :], True, False, ["s17", "th8"], ["pb0"])
+        mm(pb[0][0:96, 0:256], T.ones[0:1, 0:96], T.kc[0:1, :], False, False, ["ones", "kc"], ["pb0"])
+        for h in range(2):
+            mm(pb[0][0:96, 128 * h:128 * (h + 1)], T.cL[:, n, HALF * h:HALF * (h + 1)], T.wsc[:], False, False, [cn, "wsc"], ["pb0"])
+        for (a, b) in achunks:
+            ac(T.sg[:, NT * a:NT * b], T.sw[:, 0:V].indirect(T.off[:, 12 * a:12 * b]), AF.Copy, S6 + ["off"], ["sg%d" % k for k in range(a, b)])
+        for (a, b) in chunks:
+            ck = [cn] + ([cn + "b"] if b - a > 1 else []) + ([cn + "c"] if b - a > 2 else [])
+            tt(T.mx[:, NT * a:NT * b], T.xw[:, 0:V].indirect(T.off[:, 12 * a:12 * b]), T.cL[:, n, 0:NT * (b - a)], ALU.max,
+               X3 + ["off"] + ck, MX[a:b])
+            for k in range(a, b):
+                for h in range(2):
+                    c0 = NT * k + HALF * h
+                    o = pb[0][0:96, 128 * h + k:128 * (h + 1):16]
+                    mm(o, T.mx[:, c0:c0 + HALF], T.wm[:], False, False, [MX[k], "wm"], ["pb0"])
+                    mm(o, T.sg[:, c0:c0 + HALF], T.ws[:], False, k == 15 and h == 1, ["sg%d" % k, "ws"], ["pb0"])
+        if n == 0:
+            late_constants()
+        elif not last:
+            cp(T.aw[:, V:W], T.alL[:, n, 16:208], [an], ["ad"])
+        ac(T.sw[:, V:W], T.inf[:, n, :], AF.Identity, [fn, "col%d" % C_ID], ["sd"], scale=col(C_ID))
+        if n == 0:
+            ac(T.leno[:], T.inf[:, n, :], AF.Identity, [fn], ["leno"], scale=0.0)
+        else:
+            ac(T.leno[:], T.inf[:, n, :], AF.Identity, [fn, "col%d" % C_LEN], ["leno"], scale=col(C_LEN))
+        op("v", ["pb0", "rm"], ["scn"], lambda: vec.tensor_tensor_scan(T.scn[0:96, :], T.rm[0:96, :], pb[0][0:96, 0:256], 0.0, ALU.add, ALU.max))
+        tt(T.rr[:], T.scn[:, 0:256].indirect(T.la[:, 0:10]), T.scl[:], ALU.mult, ["scn", "scp", "la0", "la1"] + SCL, ["rr"])
+        ts(T.s8[0:96, :], T.rr[0:96, 64:128], -8.0, None, ALU.mult, None, ["rr"], ["s8"])
+        ts(T.dd[0:96, :, 9:11], T.rr[0:96, 128:160], 0.0, None, ALU.max, None, ["rr"], ["dg"])
+        tt(T.dd[0:96, :, 0:4], T.rr[0:96, 0:64], T.s8[0:96, :], ALU.add, ["rr", "s8"], ["da"])
+        ts(T.f1[0:96, :], T.rr[0:96, 67:128:4], 4096.0, None, ALU.mult, None, ["rr"], ["f1"])
+        ac(T.dd[0:96, :, 11:15], T.dd[0:96, :, 0:4], AF.Square, ["da"], ["dq2"])
+        tt(T.dd[0:96, :, 4:8], T.dd[0:96, :, 0:4], T.dd[0:96, :, 0:4], ALU.mult, ["da"], ["dq1"])
+        for b in (2, 1):
+            for h in range(2):
+                mm(pb[b][:, HALF * h:HALF * (h + 1)], T.dd[0:96, 8 * h:8 * (h + 1), :], T.idb[0:96, 0:96], True, True,
+                   ["da", "dg", "dq1", "dq2", "dtie", "idb"], ["pb%d" % b])
+        ts(T.f3[0:96, :], T.dd[0:96, :, 9], 1.0, None, ALU.min, None, ["dg"], ["f3"])
+        tt(T.f4[0:96, :], T.f1[0:96, :], T.rr[0:96, 0:64:4], ALU.subtract, ["f1", "rr"], ["f4"])
+        ac(T.rb[:], pb[2][:, 0:NT], AF.Identity, ["pb2", "col%d" % C_MR, "col%d" % C_CR], ["rb"], scale=col(C_MR), bias=col(C_CR))
+        ts(T.le[:], pb[1][:, 0:NT], col(C_WE), col(C_CE), ALU.mult, ALU.add, ["pb1", "col%d" % C_WE, "col%d" % C_CE], ["le"])
+        ac(T.lo[:], pb[2][:, 0:NT], AF.Identity, ["pb2", "col%d" % C_WO, "col%d" % C_CO], ["lo"], scale=col(C_WO), bias=col(C_CO))
+        tt(T.f2[0:96, :], T.dt0[0:96, :], T.f4[0:96, :], ALU.add, ["dt0", "f4"], ["f2"])
+        tt(T.pos[0:96, :], T.f2[0:96, :], T.f3[0:96, :], ALU.mult, ["f2", "f3"], ["pos"])
+        nj = 0
+        for t in towns:
+            p0, bk = 32 * (t // 2), bank[t]
+            lt, lk = (T.lo, "lo") if t % 2 else (T.le, "le")
+            for h in range(2):
+                mm(pb[bk][0:96, NT * h:NT * (h + 1)], lt[p0:p0 + 32, HALF * h:HALF * (h + 1)], T.rb[p0:p0 + 32, :], True, True,
+                   [lk, "rb"], ["pb%d" % bk])
+            for h in range(2):
+                o, src = T.lose[0:96, 8 * h + t:8 * h + t + 1], pb[bk][0:96, NT * h:NT * (h + 1)]
+                if t in on_vector:
+                    op("v", ["pb%d" % bk], ["ls%d" % (8 * h + t)], lambda o=o, src=src: vec.tensor_reduce(o, src, AX.X, ALU.max))
+                else:
+                    ac(T.junk[0:96, nj, :], src, AF.Relu, ["pb%d" % bk], ["ls%d" % (8 * h + t), "junk%d" % nj], accum_out=o)
+                    nj += 1
+        mm(pb[3][:, 0:12], T.idf[:], T.dc[:], True, False, ["idf", "dc"], ["pb3"])
+        tt(T.zz[0:96, :], T.pos[0:96, :], T.lose[0:96, :], ALU.subtract, ["pos"] + ["ls%d" % q for q in range(16)], ["zz"])
+        tt(T.ee[:], T.zz[:, 0:16].indirect(T.lel[:]), T.em[:], ALU.max, ["zz", "zzp", "lel", "em"], ["ee"])
+        for h in range(2):
+            mm(pb[3][:, 0:12], T.ee[0:96, 128 * h:128 * (h + 1)], T.rs[0:96, 12 * h:12 * (h + 1)], False, h == 1, ["ee", "rs"], ["pb3"])
+        cp(T.lst[:], pb[3][:, 0:12], ["pb3"], ["lst"])
+        lst = T.lst[:]
+        if not last:
+            cp(T.outA[:, n, :], T.aw[:, 0:W].indirect(lst), ["aw", "ad", "lst"], ["oa%d" % n])
+            ac(T.outC[:, n, :], T.yw[:, 0:W].indirect(lst), AF.Copy, Y3 + ["yd", "lst"], ["oc%d" % n])
+            send(["oa%d" % n], lambda h: T.outA[:, n, HALF * h:HALF * (h + 1)],
+                 lambda h: T.alL[:, n + 1, 16 + HALF * h:16 + HALF * (h + 1)], "ra%d" % n, "al%d" % (n + 1))
+            send(["oc%d" % n], lambda h: T.outC[:, n, HALF * h:HALF * (h + 1)],
+                 lambda h: T.cL[:, n + 1, HALF * h:HALF * (h + 1)], "rc%d" % n, "c%d" % (n + 1))
+            tt(T.mst[:], T.xw[:, 0:W].indirect(lst), cc, ALU.max, X3 + ["xd", "lst", cn], ["mst"])
+        tt(T.outI[:, n, :], T.sw[:, 0:W].indirect(lst), T.leno[:], ALU.add, S6 + ["sd", "lst", "leno"], ["oi%d" % n])
+        send(["oi%d" % n], lambda h: T.outI[:, n, HALF * h:HALF * (h + 1)],
+             lambda h: T.inf[:, n + 1, HALF * h:HALF * (h + 1)], "ri%d" % n, "inf%d" % (n + 1))
+        if not last:
+            o = pb[4][:, 0:NT]
+            mm(o, T.wf[:, 1, :], T.inf[:, n, :], True, False, ["wf", fn], ["pb4"])
+            mm(o, T.wab[:, 0:128], cc, False, False, ["wab", cn], ["pb4"])
+            mm(o, T.wab[:, 1:129], T.mst[:], False, False, ["wab", "mst"], ["pb4"])
+            mm(o, T.wf[:, 0, :], T.outI[:, n, :], False, True, ["wf", "oi%d" % n], ["pb4"])
+            ac(T.vv[:], o, AF.Identity, ["pb4", "col%d" % C_VB], ["vv"], bias=col(C_VB))
+            if n < NR - 2:
+                cp(T.yw[:, 0:W].indirect(lst), cc, [cn, "lst"], Y3 + ["yd"])
+            cp(T.sw[:, 0:W].indirect(lst), T.vv[:], ["vv", "lst"], S6 + ["sd"])
+            if n < NR - 2:
+                cp(T.aw[:, 0:W].indirect(lst), T.alL[:, n, 16:208], [an, "lst"], ["aw", "ad"])
+        else:
+            cp(T.sw[:, 0:W].indirect(lst), T.inf[:, n, :], [fn, "lst"], S6 + ["sd"])
+
+    fn = "inf%d" % NR
+    dma("s", S6, ["yh"], T.yh[:], T.sw[R_ID::16, 0:V])
+    dma("a", [fn], ["yt"], T.yt[:], T.inf[R_ID::16, NR, :])
+    dma("s", [fn], ["yl"], T.yl[:], T.inf[R_LEN::16, NR, :])
+    need("g", [(sem, val, "end") for sem, val in count.items()])

@@ -2,20 +2,20 @@ from concourse.bass import DstId, RemoteDMATransfer
 from concourse.mybir import AluOpType as ALU, AxisListType as AX, ActivationFunctionType as AF
 
 V, NT, HALF, NR = 3072, 192, 96, 4
-W = V + NT
+W = V + NR * NT
+NU = NT + 1
 F, B, I, U = "float32", "bfloat16", "int32", "uint16"
 
 SCRATCH = {}
 for _dt, _bufs in (
-    (F, dict(sw=[W], alL=[NR, 224], inf=[NR + 1, NT], outA=[NR - 1, NT], outI=[NR, NT], tt=[416], scn=[256], s8=[64], lose=[16],
-             f1=[16], f2=[16], f3=[16], f4=[16], pos=[16], zz=[16], ee=[256], leno=[NT], vv=[NT], pf=[8], j16=[12], g1=[12], g3=[12],
-             g6=[24], g7=[12], g8=[12], gcol=[128], thf=[4], tq=[6, 8], cols=[12], kcol=[256], em=[256], rm=[256],
-             scl=[160], idf=[128], wf=[2, 128], dt0=[16], lai=[12], rsi=[24], rs=[24], dc=[12])),
-    (B, dict(xw=[W], yw=[W], mx=[V], sg=[V], cL=[NR, 768], outC=[NR - 1, NT], dd=[16, 16], rb=[NT], le=[NT], lo=[NT], junk=[8, NT],
-             mst=[NT], crow=[512], wc=[6, 128], wab=[144], wm=[8], ws=[8], wsc=[128], ones=[256], kc=[256], m8=[256], s17=[96],
-             th8=[256], idb=[128])),
-    (I, dict(aw=[W], vai=[NT], rr=[160], pidx=[4], pi3=[8], g2=[12], g4=[12], g5=[24], thi=[4], lei=[16])),
-    (U, dict(off=[NT], lst=[12], gl=[12], la=[12], lel=[16])),
+    (F, dict(sw=[W], alL=[NR, 224], inf=[NR + 1, NT], outA=[NR - 1, NT], outI=[NR, NT], tt=[416], scn=[NT], rm=[NT], sg2=[8],
+             leno=[NT], vv=[NT], pf=[12], j16=[12], g1=[12], g3=[12], g6=[24], g7=[12], g8=[8], gcol=[128], gnat=[8], thf=[4], tq=[3, 8],
+             cols=[4], wf=[2, 128], conv=[HALF], spc=[2, 8, 12])),
+    (B, dict(xw=[W], yw=[W], mx=[V], sg=[V], cL=[NR, 768], outC=[NR - 1, NT], dd=[416], rb=[NU + 7], ll=[2 * NT], junk=[2, NU + 7],
+             mst=[NT], crow=[512], wc=[6, 128], wab=[144], wm=[8], ws=[8], wsc=[8, 16], ones=[256], kc=[NT], m8=[8, 16],
+             th8=[8, 16], idb=[128], res=[16], tri=[4, NU], pick=[8, 128], cst=[8, 12])),
+    (I, dict(aw=[W], vai=[NT], gi=[12], pidx=[4], pi3=[8], g2=[12], g4=[12], g5=[24], thi=[4])),
+    (U, dict(off=[NT], lst=[NR, 16], gl=[12], gl2=[2])),
 ):
     for _k, _s in _bufs.items():
         SCRATCH[_k] = ("sbuf", [128] + _s, _dt)
@@ -25,12 +25,16 @@ for _b in range(8):
 SEMAPHORES = (["cv", "ca", "cp", "cg", "sent"] + ["d%d" % _i for _i in range(24)]
               + ["ra%d" % _i for _i in range(3)] + ["rc%d" % _i for _i in range(3)] + ["ri%d" % _i for _i in range(4)])
 
-S16 = 65536.0
-GS = 17 * 4096.0
-Z = 4096.0
+GS = 16.0
+FAM = 4096.0
+MID = V // 2
+WIN = 256.0
+WF = 1024.0 * FAM
+ROUND_1, ROUND_64 = 1.5 * 2.0 ** 23, 1.5 * 2.0 ** 17
+D0 = 16
 R_A, R_B, R_HI, R_LO, R_ID, R_LEN = 0, 1, 2, 3, 4, 5
-C_WE, C_WO, C_CE, C_CO, C_MR, C_CR, C_VB, C_ID, C_LEN = range(9)
-P_G, P_H, P_M, P_12, P_14, P_S1, P_S2 = range(7)
+C_VB, C_ID, C_LEN = range(3)
+P_G, P_H, P_M, P_8, P_Q, P_S1, P_S2 = range(7)
 
 
 def rank_program(g, core, T, topo):
@@ -150,13 +154,15 @@ def rank_program(g, core, T, topo):
     part = (0, 0, 1, 1, 2, 3)
     S6 = ["s%d" % j for j in range(6)]
     MX = ["mx%d" % k for k in range(16)]
-    SCL = ["scl%d" % j for j in range(6)]
 
     def pc(j):
         return T.pf[:, j:j + 1]
 
     def col(j):
         return T.cols[:, j:j + 1]
+
+    def spare(n):
+        return slice(V + NT * n, V + NT * (n + 1))
 
     for j, (a, b) in enumerate(((0, 1024), (1024, 2048), (2048, 2560), (2560, V))):
         dma("a", [], [Y3[j]], T.yw[:, a:b], T.hx[:, a:b])
@@ -165,14 +171,14 @@ def rank_program(g, core, T, topo):
             dma("s", [], ["vai"], T.vai[:], T.va[:])
     dma("a", [], ["c0"], T.cL[:, 0, 0:NT], T.vx[:])
     dma("s", [Y3[3], X3[3]], ["aw"], T.aw[:, 0:V], T.ha[:])
-    dma("s", [], ["ad"], T.aw[:, V:W], T.va[:])
-    dma("s", [], ["yd"], T.yw[:, V:W], T.vx[:])
+    dma("s", [], ["ad0"], T.aw[:, spare(0)], T.va[:])
+    dma("s", [], ["yd0"], T.yw[:, spare(0)], T.vx[:])
 
     iota(T.pidx[:, 0:1], [[0, 1]], 0, 1, ["pidx"], flag=False)
     mset(T.ones[:], 1.0, ["ones"])
     mset(T.crow[0:64, :], 0.0, ["crow"])
     mset(T.wc[0:96, :, :], 0.0, ["wc"])
-    iota(T.gcol[:], [[1, 8], [0, 16]], 0, 0, ["gcol"])
+    iota(T.gcol[:], [[1, 2], [2, 4], [0, 16]], 0, 0, ["gcol"])
     CR = ["cr%d" % j for j in range(10)]
     WCK = ["wa%d" % j for j in range(8)]
     for k in CR:
@@ -180,8 +186,9 @@ def rank_program(g, core, T, topo):
     for k in WCK:
         lastw[k] = lastw["wc"]
     iota(T.crow[32:33, 0:64], [[1, 64]], 0, 0, [CR[0]])
+    iota(T.gnat[:], [[1, 8]], 0, 0, ["gnat"])
     iota(T.j16[:], [[16, 12]], 0, 0, ["j16"])
-    iota(T.wc[64:65, :, R_HI::16], [[8, 6], [0, 8]], -24, 0, [WCK[6]])
+    iota(T.wc[64:65, :, R_HI::16], [[8, 6], [0, 8]], -MID // 64, 0, [WCK[6]])
     iota(T.wc[64:65, :, R_ID::16], [[512, 6], [0, 8]], V * rank, 0, [WCK[7]])
     sel(T.idb[:], T.ones[:, 0:128], [[-1, 128]], ALU.is_equal, 0.0, 0, 1, ["ones"], ["idb"])
     dma("g", [], ["thi"], T.thi[0:8, 0:1], T.th[:], allow_slow_non_contiguous=True)
@@ -193,45 +200,42 @@ def rank_program(g, core, T, topo):
     mset(T.crow[64:65, :], 1.0, [CR[8]])
     for j, (p, r, val) in enumerate(((0, R_HI, 1.0), (0, R_ID, 64.0), (32, R_LO, 1.0), (32, R_ID, 1.0), (64, R_A, -120.0), (64, R_LEN, 1.0))):
         mset(T.wc[p:p + 1, :, r::16], val, [WCK[j]])
-    ts(T.pi3[:, 0:1], T.pidx[:, 0:1], 4, None, ALU.arith_shift_right, None, ["pidx"], ["pi0"])
-    ts(T.pi3[:, 1:2], T.pidx[:, 0:1], 4, 1, ALU.arith_shift_right, ALU.bitwise_and, ["pidx"], ["pi1"])
-    for j, m in ((P_M, 15), (P_12, 12), (P_14, 14)):
-        ts(T.pi3[:, j:j + 1], T.pidx[:, 0:1], m, None, ALU.bitwise_and, None, ["pidx"], ["pi%d" % j])
+    ts(T.pi3[:, P_G:P_G + 1], T.pidx[:, 0:1], 4, None, ALU.arith_shift_right, None, ["pidx"], ["pi0"])
+    ts(T.pi3[:, P_H:P_H + 1], T.pidx[:, 0:1], 4, 1, ALU.arith_shift_right, ALU.bitwise_and, ["pidx"], ["pi1"])
+    ts(T.pi3[:, P_M:P_M + 1], T.pidx[:, 0:1], 15, None, ALU.bitwise_and, None, ["pidx"], ["pi2"])
+    ts(T.pi3[:, P_8:P_8 + 1], T.pidx[:, 0:1], 3, 1, ALU.arith_shift_right, ALU.bitwise_and, ["pidx"], ["pi3"])
+    ts(T.pi3[:, P_Q:P_Q + 1], T.pidx[:, 0:1], 5, None, ALU.arith_shift_right, None, ["pidx"], ["pi4"])
     mset(T.wab[:], 0.0, ["wab"])
     cp(T.pf[:, 0:5], T.pi3[:, 0:5], ["pi0", "pi1", "pi2", "pi3", "pi4"], ["pf"])
     aset(T.alL[:, :, 0:16], T.ones[:, 0:64], 0.0, ["pad0"])
     aset(T.alL[:, :, 208:224], T.ones[:, 0:64], 0.0, ["pad1"])
     aset(T.ws[:], T.ones[:, 0:8], 0.0, ["ws"])
-    aset(T.tq[:], T.ones[:, 0:48], 0.0, ["tq"])
-    aset(T.s17[0:8, :], T.ones[0:8, 0:96], 17.0, ["s17"])
-    aset(T.rm[:], T.ones[:], 0.0, ["rm"])
-    for j in range(4):
-        aset(T.scl[:, j:64:4], T.ones[:, 0:16], 8.0 ** -j, ["scl%d" % j])
-    aset(T.rm[:, 0::16], T.ones[:, 0:16], -1.0e9, ["rm"])
-    aset(T.scl[:, 128:160], T.ones[:, 0:32], 1.0 / GS, ["scl5"])
-    ac(T.scl[:, 64:128], T.scl[:, 0:64], AF.Identity, SCL[0:4], ["scl4"], scale=0.125)
-    aset(T.zz[96:128, :], T.ones[96:128, 0:16], 0.0, ["zzp"])
-    aset(T.scn[96:128, :], T.ones[96:128, :], 0.0, ["scp"])
-    aset(T.xw[:, V:W], T.ones[:, 0:NT], 0.0, ["xd"])
-    ts(T.wab[:, 1:129:16], T.gcol[:, 0::16], pc(P_G), None, ALU.is_equal, None, ["gcol", "pf"], ["wab"])
+    aset(T.tq[:], T.ones[:, 0:24], 0.0, ["tq"])
+    aset(T.rm[:], T.ones[:, 0:NT], 1.0, ["rm"])
+    aset(T.cst[0:1, :, :], T.ones[0:1, 0:HALF], WIN * FAM, ["cst"])
+    aset(T.rm[:, 0::16], T.ones[:, 0:12], 0.0, ["rm"])
+    ts(T.wab[:, 1:129:16], T.gnat[:], pc(P_G), None, ALU.is_equal, None, ["gnat", "pf"], ["wab"])
     ts(T.g1[:], T.j16[:], pc(P_M), None, ALU.add, None, ["j16", "pf"], ["g1"])
     ts(pc(P_S1), pc(P_H), -416.0, 224.0, ALU.mult, ALU.add, ["pf"], ["pf1"])
     ts(pc(P_S2), pc(P_H), 208.0, None, ALU.mult, None, ["pf"], ["pf2"])
     ts(T.g2[:], T.g1[:], -5.5, 1.0 / 12.0, ALU.add, ALU.mult, ["g1"], ["g2"])
     ts(T.wm[:], T.gcol[:, 0::16], pc(P_G), -2.0 * GS, ALU.is_equal, ALU.mult, ["gcol", "pf"], ["wm"])
     ts(T.g3[:], T.g2[:], -12.0, None, ALU.mult, None, ["g2"], ["g3"])
-    ts(T.g8[:, 0:1], pc(P_12), 4.0, None, ALU.mult, None, ["pf"], ["g8a"])
     tt(T.g4[:], T.g3[:], T.g1[:], ALU.add, ["g3", "g1"], ["g4"])
     ts(T.wsc[:], T.gcol[:], pc(P_G), GS, ALU.is_equal, ALU.mult, ["gcol", "pf"], ["wsc"])
     ts(T.g5[:, 0:12], T.g4[:], 1, None, ALU.arith_shift_right, None, ["g4"], ["g5a"])
     ts(T.g5[:, 12:24], T.g4[:], 1, None, ALU.bitwise_and, None, ["g4"], ["g5b"])
-    ts(T.g8[:, 1:2], pc(P_14), 8.0, None, ALU.mult, None, ["pf"], ["g8b"])
+    ts(T.rb[:, NT:NU], pc(P_M), 5.0, -2.0, ALU.is_equal, ALU.mult, ["pf"], ["rbx"])
     ts(T.g6[:, 0:12], T.g5[:, 0:12], 32.0, None, ALU.mult, None, ["g5a"], ["g6a"])
     ts(T.g6[:, 12:24], T.g5[:, 12:24], pc(P_S1), pc(P_S2), ALU.mult, ALU.add, ["g5b", "pf1", "pf2"], ["g6b"])
-    ts(T.dc[:], T.j16[:], pc(P_M), V + 15 * 8192.0, ALU.add, ALU.add, ["j16", "pf"], ["dc"])
+    ts(T.g8[:, 1:2], pc(P_H), 4.0, pc(P_Q), ALU.mult, ALU.add, ["pf"], ["g81"])
+    ts(T.g8[:, 2:3], pc(P_H), 44.0, -88.0, ALU.mult, ALU.add, ["pf"], ["g82"])
     tt(T.g7[:], T.g6[:, 0:12], T.g2[:], ALU.add, ["g6a", "g2"], ["g7"])
+    ts(T.g8[:, 0:1], pc(P_M), 12.0, T.g8[:, 1:2], ALU.mult, ALU.add, ["g81", "pf"], ["g80"])
     tt(T.g3[:], T.g7[:], T.g6[:, 12:24], ALU.add, ["g7", "g6b"], ["g3"])
+    ts(T.g8[:, 3:4], T.g8[:, 2:3], pc(P_8), T.g8[:, 0:1], ALU.mult, ALU.add, ["g82", "g80", "pf"], ["g83"])
     cp(T.gl[:], T.g3[:], ["g3"], ["gl"])
+    ts(T.gl2[:, 0:1], T.g8[:, 3:4], HALF - 1.0, None, ALU.min, None, ["g83"], ["gl2"])
 
     def lists(n):
         op("v", ["al%d" % n], ["tt1"], lambda: vec.transpose(T.tt[:, 0:192], T.alL[:, n, 16:208]))
@@ -245,46 +249,54 @@ def rank_program(g, core, T, topo):
     for j in range(6):
         mm(pb[j][:], T.wc[0:65, j, :], T.crow[0:65, :], True, False, CR + WCK, ["pb%d" % j])
 
-    iota(T.kc[0:1, :], [[0, 16], [-4096, 16]], 28672, 0, ["kc"])
-    sel(T.m8[0:8, :], T.ones[0:8, :], [[0, 2], [-1, 8], [0, 16]], ALU.is_equal, 0.0, 0, 1, ["ones"], ["m8"])
-    iota(T.lai[:, 0:8], [[0, 2], [64, 4]], 15, 0, ["lai0"])
-    iota(T.lai[:, 8:10], [[128, 2]], 15, 0, ["lai1"])
-    iota(T.lei[:], [[1, 16]], 0, 0, ["lei"], flag=False)
-    iota(T.rsi[:], [[-6, 2], [1, 12]], 0, 0, ["rsi"])
-    iota(T.kcol[:], [[0, 16], [1, 16]], 0, 0, ["kcol"])
-    for r, val in ((R_A, 2.0 * GS), (R_B, -GS), (R_HI, 64.0), (R_LO, 1.0)):
-        sel(T.ws[:], T.ws[:], [[-16, 8]], ALU.not_equal, val, -r, 1, ["ws"], ["ws"])
+    iota(T.kc[0:1, :], [[0, 12], [-1, 16]], 7, 0, ["kc"])
+    sel(T.m8[0:8, :, :], T.ones[0:8, 0:128], [[-1, 2], [-2, 4], [0, 16]], ALU.is_equal, 0.0, 0, 1, ["ones"], ["m8"])
+    for r, val in ((R_A, 2.0 * GS), (R_B, -GS), (R_HI, 64.0 / FAM), (R_LO, 1.0 / FAM)):
+        sel(T.ws[:], T.ws[:], [[-16, 2], [-32, 4]], ALU.not_equal, val, -r, 1, ["ws"], ["ws"])
+    iota(T.tri[:], [[0, 4 * NU]], 1 - int(WIN), 0, ["tri"])
+    sel(T.tri[:, 0:2, 0:NT], T.tri[:, 0:2, 0:NT], [[0, 2], [-1, NT]], ALU.is_gt, -WIN, 0, 1, ["tri"], ["tri"])
     copies(0)
-    steps = {0: ((0, 2 * S16 * Z), (4, 0.0), (10, -256 * Z), (11, -S16 * Z), (15, -Z), (16, 0.0)),
-             1: ((4, -S16 * Z), (8, Z), (9, 256 * Z), (10, 0.0)), 2: ((0, 1.0), (10, 0.0))}
-    for j in range(6):
-        lastw["tq%d" % j] = lastw["tq"]
-    for i in range(6):
-        for j in steps:
-            if i < len(steps[j]):
-                sel(T.tq[:, j, :], T.tq[:, j, :], [[16, 8]], ALU.is_ge, steps[j][i][1], steps[j][i][0] - 1, -1, ["tq%d" % j], ["tq%d" % j])
-    for j, r, val in ((3, R_A, -120.0), (4, R_ID, 1.0), (5, R_LEN, 1.0), (3, R_LEN, 1.0)):
-        sel(T.tq[:, j, :], T.tq[:, j, :], [[-16, 8]], ALU.not_equal, val, -r, 1, ["tq%d" % j], ["tq%d" % j])
-    iota(T.dd[:, :, 8::7], [[-HALF, 2], [0, 8], [0, 2]], NT - 1, -1, ["dtie"])
-    iota(T.inf[:, 0, :], [[1, NT]], n_ranks * V + NT * rank, 0, ["inf0"])
-    iota(T.dt0[:], [[HALF, 2], [0, 8]], V // 2, 1, ["dt0"])
-    sel(T.idf[:], T.ones[:, 0:128], [[-1, 128]], ALU.is_equal, 0.0, 0, 1, ["ones"], ["idf"])
-    iota(T.wf[:], [[0, 256]], 0, 0, ["wf"])
-    for j, r in ((0, R_HI), (1, R_ID), (0, R_LO)):
-        sel(T.wf[:, j, r::16], T.wf[:, j, r::16], [[-16, 8]], ALU.not_equal, 1.0, -r, 1, ["wf"], ["wf"])
+    for p in (0, 64):
+        sel(T.tri[p:p + 64, 2:4, 128:NT], T.tri[p:p + 64, 2:4, 128:NT], [[0, 2], [-1, 64]], ALU.is_gt, -WIN, 0, 1, ["tri"], ["tri"])
 
+    def late_tables():
+        for j in range(3):
+            lastw["tq%d" % j] = lastw["tq"]
+        for j, r, val in ((0, R_A, -120.0), (1, R_ID, 1.0), (2, R_LEN, 1.0), (0, R_LEN, 1.0)):
+            sel(T.tq[:, j, :], T.tq[:, j, :], [[-16, 8]], ALU.not_equal, val, -r, 1, ["tq%d" % j], ["tq%d" % j])
+        iota(T.inf[:, 0, :], [[1, NT]], n_ranks * V + NT * rank, 0, ["inf0"])
+        iota(T.spc[:, 0, :, 0:8], [[16, 8], [0, 8]], V - MID, 1, ["spa"])
+        iota(T.spc[:, 0, :, 8:12], [[0, 2], [16, 4], [0, 4]], V - MID + 128, 1, ["spb"])
+        sel(T.pick[:], T.pick[:], [[-16, 8], [0, 8], [-1, 16]], ALU.is_equal, 0.0, 0, 1, ["pick"], ["pick"])
+        iota(T.wf[:], [[0, 256]], 0, 0, ["wf"])
+        for j, r in ((0, R_HI), (1, R_ID), (0, R_LO)):
+            sel(T.wf[:, j, r::16], T.wf[:, j, r::16], [[-16, 8]], ALU.not_equal, 1.0, -r, 1, ["wf"], ["wf"])
+
+    on_scalar = (4, 5, 7)
+    for t in on_scalar:
+        aset(T.cst[0:1, :, t], T.ones[0:1, 0:8], 0.0, ["cst"])
+
+    def weights():
+        for j, (r, val) in enumerate(((0, WF), (1, WF), (2, 2.0), (6, -WF), (7, -WF), (8, -2.0))):
+            mset(row(r), val, ["dw%d" % j])
+
+    def row(r):
+        return T.dd[:, D0 + r:D0 + 32 * 12:32]
+
+    DW = ["dw%d" % j for j in range(6)]
     fill = [
+        lambda: mset(T.pick[:], FAM, ["pick"]),
+        lambda: mset(T.dd[:], 0.0, DW + ["dh", "dl", "dg"]),
         lambda: cp(T.alL[:, 0, 16:208], T.vai[:], ["vai"], ["al0"]),
         lambda: lists(0),
-        lambda: cp(T.lel[:], T.lei[:], ["lei"], ["lel"]),
-        lambda: ts(T.la[:, 0:8], T.lai[:, 0:8], T.g8[:, 0:1], None, ALU.add, None, ["lai0", "g8a"], ["la0"]),
-        lambda: ts(T.la[:, 8:10], T.lai[:, 8:10], T.g8[:, 1:2], None, ALU.add, None, ["lai1", "g8b"], ["la1"]),
-        lambda: ts(T.rs[:], T.rsi[:], pc(P_G), -1.0, ALU.is_equal, ALU.mult, ["rsi", "pf"], ["rs"]),
-        lambda: ts(T.em[:], T.kcol[:], pc(P_M), 8192.0, ALU.not_equal, ALU.mult, ["kcol", "pf"], ["em"]),
-        lambda: ts(T.thf[0:8, 0:1], T.thi[0:8, 0:1], -GS / 17, 240.0 * GS / 17, ALU.mult, ALU.add, ["thi"], ["thf"]),
-        lambda: ts(T.th8[0:8, :], T.m8[0:8, :], T.thf[0:8, 0:1], None, ALU.mult, None, ["m8", "thf"], ["th8"]),
+        lambda: mset(T.xw[:, V:W], 0.0, ["xd"]),
+        weights,
+        lambda: ts(T.g8[:, 4:5], pc(P_G), -16.0, None, ALU.mult, None, ["pf"], ["g84"]),
+        lambda: ts(T.thf[0:8, 0:1], T.thi[0:8, 0:1], -GS, 240.0 * GS, ALU.mult, ALU.add, ["thi"], ["thf"]),
+        lambda: ts(T.g8[:, 4:8], T.j16[:, 0:4], NT / 16.0, T.g8[:, 4:5], ALU.mult, ALU.add, ["j16", "g84"], ["g84"]),
+        lambda: ts(T.th8[0:8, :, :], T.m8[0:8, :, :], T.thf[0:8, 0:1], None, ALU.mult, None, ["m8", "thf"], ["th8"]),
     ]
-    cuts = (0, 0, 2, 2, 6, 8, 9)
+    cuts = (0, 2, 4, 6, 8, 10, 10)
 
     def ycopy(j):
         mm(pb[6 + j % 2][:], T.idb[:], T.yw[:, 512 * j:512 * (j + 1)], True, True, ["idb", Y3[part[j]]], ["pb%d" % (6 + j % 2)])
@@ -305,32 +317,49 @@ def rank_program(g, core, T, topo):
         ac(T.sw[:, a:b], pb[j][:], AF.Copy, ["pb%d" % j], [S6[j]])
         for f in fill[cuts[j]:cuts[j + 1]]:
             f()
+    late_tables()
 
     def late_constants():
-        for c, ap, key in ((C_WE, T.tq[:, 0, 0::2], 0), (C_WO, T.tq[:, 0, 1::2], 0), (C_CE, T.tq[:, 1, 0::2], 1), (C_CO, T.tq[:, 1, 1::2], 1),
-                           (C_MR, T.tq[:, 2, :], 2), (C_VB, T.tq[:, 3, :], 3), (C_ID, T.tq[:, 4, :], 4), (C_LEN, T.tq[:, 5, :], 5)):
-            op("v", ["tq%d" % key], ["col%d" % c], lambda c=c, ap=ap: vec.tensor_reduce(col(c), ap, AX.X, ALU.add))
-        ts(col(C_CR), col(C_MR), -1.0, 1.0, ALU.mult, ALU.add, ["col%d" % C_MR], ["col%d" % C_CR])
+        for c in (C_VB, C_ID, C_LEN):
+            op("v", ["tq%d" % c], ["col%d" % c], lambda c=c: vec.tensor_reduce(col(c), T.tq[:, c, :], AX.X, ALU.add))
 
-    chunks = ((0, 1), (1, 2), (2, 4), (4, 6), (6, 10), (10, 14), (14, 15), (15, 16))
-    achunks = ((0, 5), (5, 10), (10, 13), (13, 15), (15, 16))
-    towns = (0, 2, 4, 6, 1, 3, 5, 7)
-    bank = dict(zip(towns, (4, 3, 5, 6, 7, 0, 2, 1)))
-    on_vector = (2, 6, 3, 7)
+    chunks = ((0, 1), (1, 2), (2, 4), (4, 6), (6, 10), (10, 12), (12, 14), (14, 15), (15, 16))
+    achunks = ((0, 5), (5, 10), (10, 12), (12, 14), (14, 15), (15, 16))
+    banks = ((3, (0, 1)), (4, (4, 5)), (5, (2, 3)), (0, (6, 7)), (6, (8, 9)), (7, (10, 11)))
+    place = {t: (bk, s) for bk, two in banks for s, t in enumerate(two)}
+    on_vector = (0, 1, 2, 3, 6, 8, 9, 10, 11)
 
+    def ties(bk, two):
+        j = 0 if two[0] < 8 else 2
+        mm(pb[bk][:, 0:2 * NU], T.idb[:], T.tri[:, j:j + 2, :], True, False, ["idb", "tri"], ["pb%d" % bk])
+
+    def keyed(data, c0, wts, k, last, rd):
+        if k is None:
+            outs = (pb[0][:, 0:128], pb[0][0:64, 128:NT], pb[0][64:128, 128:NT])
+        else:
+            outs = (pb[0][:, k:128:16], pb[0][0:64, 128 + k:NT:16], pb[0][64:128, 128 + k:NT:16])
+        mm(outs[1], data(c0 + 128, c0 + NT), wts(0, 4), False, False, rd, ["pb0"])
+        mm(outs[2], data(c0 + 128, c0 + NT), wts(4, 8), False, False, rd, ["pb0"])
+        mm(outs[0], data(c0, c0 + 128), wts(0, 8), False, last, rd, ["pb0"])
+
+    later = []
     for n in range(NR):
         last = n == NR - 1
         cn, an, fn = "c%d" % n, "al%d" % n, "inf%d" % n
         cc = T.cL[:, n, 0:NT]
+        wn = V + NT * (n + 1)
+        AD, YD, SD = (["%s%d" % (s, j) for j in range(n + 1)] for s in ("ad", "yd", "sd"))
         if n > 0:
             lists(n)
             copies(n)
             if not last:
-                dma("s", [cn], ["yd"], T.yw[:, V:W], cc)
-        mm(pb[0][0:96, 0:256], T.s17[0:8, :], T.th8[0:8, :], True, False, ["s17", "th8"], ["pb0"])
-        mm(pb[0][0:96, 0:256], T.ones[0:1, 0:96], T.kc[0:1, :], False, False, ["ones", "kc"], ["pb0"])
-        for h in range(2):
-            mm(pb[0][0:96, 128 * h:128 * (h + 1)], T.cL[:, n, HALF * h:HALF * (h + 1)], T.wsc[:], False, False, [cn, "wsc"], ["pb0"])
+                dma("s", [cn], ["yd%d" % n], T.yw[:, spare(n)], cc)
+            for bk, two in banks:
+                if bk:
+                    ties(bk, two)
+        mm(pb[0][:, 0:NT], T.ones[0:1, 0:128], T.kc[0:1, :], True, False, ["ones", "kc"], ["pb0"])
+        keyed(lambda a, b: T.ones[0:8, a:b], 0, lambda s, d: T.th8[0:8, s:d, :], None, False, ["ones", "th8"])
+        keyed(lambda a, b: T.cL[:, n, a:b], 0, lambda s, d: T.wsc[:, s:d, :], None, False, [cn, "wsc"])
         for (a, b) in achunks:
             ac(T.sg[:, NT * a:NT * b], T.sw[:, 0:V].indirect(T.off[:, 12 * a:12 * b]), AF.Copy, S6 + ["off"], ["sg%d" % k for k in range(a, b)])
         for (a, b) in chunks:
@@ -338,85 +367,134 @@ def rank_program(g, core, T, topo):
             tt(T.mx[:, NT * a:NT * b], T.xw[:, 0:V].indirect(T.off[:, 12 * a:12 * b]), T.cL[:, n, 0:NT * (b - a)], ALU.max,
                X3 + ["off"] + ck, MX[a:b])
             for k in range(a, b):
-                for h in range(2):
-                    c0 = NT * k + HALF * h
-                    o = pb[0][0:96, 128 * h + k:128 * (h + 1):16]
-                    mm(o, T.mx[:, c0:c0 + HALF], T.wm[:], False, False, [MX[k], "wm"], ["pb0"])
-                    mm(o, T.sg[:, c0:c0 + HALF], T.ws[:], False, k == 15 and h == 1, ["sg%d" % k, "ws"], ["pb0"])
+                keyed(lambda a, b: T.mx[:, a:b], NT * k, lambda s, d: T.wm[:, s:d], k, False, [MX[k], "wm"])
+                keyed(lambda a, b: T.sg[:, a:b], NT * k, lambda s, d: T.ws[:, s:d], k, k == 15, ["sg%d" % k, "ws"])
+            if n == 0 and b == 6:
+                for bk, two in banks:
+                    if bk:
+                        ties(bk, two)
         if n == 0:
             late_constants()
         elif not last:
-            cp(T.aw[:, V:W], T.alL[:, n, 16:208], [an], ["ad"])
-        ac(T.sw[:, V:W], T.inf[:, n, :], AF.Identity, [fn, "col%d" % C_ID], ["sd"], scale=col(C_ID))
+            cp(T.aw[:, spare(n)], T.alL[:, n, 16:208], [an], ["ad%d" % n])
+        ac(T.sw[:, spare(n)], T.inf[:, n, :], AF.Identity, [fn, "col%d" % C_ID], ["sd%d" % n], scale=col(C_ID))
         if n == 0:
             ac(T.leno[:], T.inf[:, n, :], AF.Identity, [fn], ["leno"], scale=0.0)
         else:
             ac(T.leno[:], T.inf[:, n, :], AF.Identity, [fn, "col%d" % C_LEN], ["leno"], scale=col(C_LEN))
-        op("v", ["pb0", "rm"], ["scn"], lambda: vec.tensor_tensor_scan(T.scn[0:96, :], T.rm[0:96, :], pb[0][0:96, 0:256], 0.0, ALU.add, ALU.max))
-        tt(T.rr[:], T.scn[:, 0:256].indirect(T.la[:, 0:10]), T.scl[:], ALU.mult, ["scn", "scp", "la0", "la1"] + SCL, ["rr"])
-        ts(T.s8[0:96, :], T.rr[0:96, 64:128], -8.0, None, ALU.mult, None, ["rr"], ["s8"])
-        ts(T.dd[0:96, :, 9:11], T.rr[0:96, 128:160], 0.0, None, ALU.max, None, ["rr"], ["dg"])
-        tt(T.dd[0:96, :, 0:4], T.rr[0:96, 0:64], T.s8[0:96, :], ALU.add, ["rr", "s8"], ["da"])
-        ts(T.f1[0:96, :], T.rr[0:96, 67:128:4], 4096.0, None, ALU.mult, None, ["rr"], ["f1"])
-        ac(T.dd[0:96, :, 11:15], T.dd[0:96, :, 0:4], AF.Square, ["da"], ["dq2"])
-        tt(T.dd[0:96, :, 4:8], T.dd[0:96, :, 0:4], T.dd[0:96, :, 0:4], ALU.mult, ["da"], ["dq1"])
-        for b in (2, 1):
-            for h in range(2):
-                mm(pb[b][:, HALF * h:HALF * (h + 1)], T.dd[0:96, 8 * h:8 * (h + 1), :], T.idb[0:96, 0:96], True, True,
-                   ["da", "dg", "dq1", "dq2", "dtie", "idb"], ["pb%d" % b])
-        ts(T.f3[0:96, :], T.dd[0:96, :, 9], 1.0, None, ALU.min, None, ["dg"], ["f3"])
-        tt(T.f4[0:96, :], T.f1[0:96, :], T.rr[0:96, 0:64:4], ALU.subtract, ["f1", "rr"], ["f4"])
-        ac(T.rb[:], pb[2][:, 0:NT], AF.Identity, ["pb2", "col%d" % C_MR, "col%d" % C_CR], ["rb"], scale=col(C_MR), bias=col(C_CR))
-        ts(T.le[:], pb[1][:, 0:NT], col(C_WE), col(C_CE), ALU.mult, ALU.add, ["pb1", "col%d" % C_WE, "col%d" % C_CE], ["le"])
-        ac(T.lo[:], pb[2][:, 0:NT], AF.Identity, ["pb2", "col%d" % C_WO, "col%d" % C_CO], ["lo"], scale=col(C_WO), bias=col(C_CO))
-        tt(T.f2[0:96, :], T.dt0[0:96, :], T.f4[0:96, :], ALU.add, ["dt0", "f4"], ["f2"])
-        tt(T.pos[0:96, :], T.f2[0:96, :], T.f3[0:96, :], ALU.mult, ["f2", "f3"], ["pos"])
-        nj = 0
-        for t in towns:
-            p0, bk = 32 * (t // 2), bank[t]
-            lt, lk = (T.lo, "lo") if t % 2 else (T.le, "le")
-            for h in range(2):
-                mm(pb[bk][0:96, NT * h:NT * (h + 1)], lt[p0:p0 + 32, HALF * h:HALF * (h + 1)], T.rb[p0:p0 + 32, :], True, True,
-                   [lk, "rb"], ["pb%d" % bk])
-            for h in range(2):
-                o, src = T.lose[0:96, 8 * h + t:8 * h + t + 1], pb[bk][0:96, NT * h:NT * (h + 1)]
-                if t in on_vector:
-                    op("v", ["pb%d" % bk], ["ls%d" % (8 * h + t)], lambda o=o, src=src: vec.tensor_reduce(o, src, AX.X, ALU.max))
-                else:
-                    ac(T.junk[0:96, nj, :], src, AF.Relu, ["pb%d" % bk], ["ls%d" % (8 * h + t), "junk%d" % nj], accum_out=o)
-                    nj += 1
-        mm(pb[3][:, 0:12], T.idf[:], T.dc[:], True, False, ["idf", "dc"], ["pb3"])
-        tt(T.zz[0:96, :], T.pos[0:96, :], T.lose[0:96, :], ALU.subtract, ["pos"] + ["ls%d" % q for q in range(16)], ["zz"])
-        tt(T.ee[:], T.zz[:, 0:16].indirect(T.lel[:]), T.em[:], ALU.max, ["zz", "zzp", "lel", "em"], ["ee"])
-        for h in range(2):
-            mm(pb[3][:, 0:12], T.ee[0:96, 128 * h:128 * (h + 1)], T.rs[0:96, 12 * h:12 * (h + 1)], False, h == 1, ["ee", "rs"], ["pb3"])
-        cp(T.lst[:], pb[3][:, 0:12], ["pb3"], ["lst"])
-        lst = T.lst[:]
+        ac(T.spc[:, 1, :, :], T.spc[:, 0, :, :], AF.Identity, ["spa", "spb", "g84"], ["spc"], bias=T.g8[:, 4 + n:5 + n])
+        op("v", ["pb0", "rm"], ["scn", "r1", "r64"],
+           lambda: vec.tensor_tensor_scan(T.scn[:], T.rm[:], pb[0][:, 0:NT], 0.0, ALU.mult, ALU.max))
+        key, r64, r1 = T.scn[:, 15::16], T.scn[:, 14::16], T.scn[:, 13::16]
+        ts(r64, key, ROUND_64, ROUND_64, ALU.add, ALU.subtract, ["scn"], ["r64"])
+        ts(r1, key, ROUND_1, ROUND_1, ALU.add, ALU.subtract, ["scn"], ["r1"])
+        ts(T.gi[:], key, 0.5, 1.0 / GS, ALU.add, ALU.mult, ["scn"], ["gi"])
+        tt(row(4), key, r64, ALU.subtract, ["scn", "r64"], ["dl"])
+        tt(row(3), r64, r1, ALU.subtract, ["r1", "r64"], ["dh"])
+        cp(row(5), T.gi[:], ["gi"], ["dg"])
+        DD = DW + ["dh", "dl", "dg", "idb"]
+
+        def turn(o, t0, odd, shift, start, stop, bk):
+            c0 = D0 + 32 * t0 + shift - 16 * odd
+            p = slice(0, 128) if t0 < 8 else slice(64 * odd, 64 * odd + 64)
+            mm(o, T.dd[:, c0:c0 + 128], T.idb[:, p], start, stop, DD, ["pb%d" % bk])
+
+        turn(pb[1][:, 0:128], 0, 0, 3, True, False, 1)
+        turn(pb[1][:, 0:128], 4, 1, 3, False, True, 1)
+        turn(pb[1][:, 128:NT], 8, 0, 3, True, False, 1)
+        turn(pb[1][:, 128:NT], 8, 1, 3, False, True, 1)
+        turn(pb[2][:, 0:128], 0, 0, 0, True, True, 2)
+        turn(pb[2][:, 128:NT], 8, 0, 0, True, True, 2)
+        turn(pb[0][:, 0:64], 8, 1, 0, True, True, 0)
+        turn(pb[0][:, 64:NT], 4, 1, 0, True, True, 0)
+        if later:
+            later.pop(0)()
+        cp(T.ll[:, 0:NT], pb[2][:, 0:NT], ["pb2"], ["le"])
+        ac(T.rb[:, 0:NT], pb[1][:, 0:NT], AF.Copy, ["pb1"], ["rb"])
+        ac(T.ll[:, NT:2 * NT], pb[0][:, 0:NT], AF.Copy, ["pb0"], ["lo"])
+        if later:
+            later.pop(0)()
+        for t in (0, 2, 1, 3, 4, None, 5, 6, 8, 7, 10, 9, 11):
+            if t is None:
+                ties(*banks[3])
+                continue
+            bk, s = place[t]
+            if s:
+                need("p", [lastw["pb%d" % bk][0:2] + ("tile",)])
+            p0, c0 = 32 * (t % 4), (0, 256, 128)[t // 4]
+            mm(pb[bk][:, NU * s:NU * (s + 1)], T.ll[p0:p0 + 32, c0:c0 + 128], T.rb[p0:p0 + 32, 0:NU], False, s == 1,
+               (["le"], ["lo"], ["le", "lo"])[t // 4] + ["rb", "rbx"], ["pb%d" % bk])
+        conv = pb[1][:, 0:HALF]
+        mm(conv, T.ones[0:1, 0:128], T.cst[0:1, :, :], True, False, ["ones", "cst"], ["pb1"])
+        for a in range(8):
+            for r in (3, 4):
+                mm(pb[1][:, 12 * a:12 * (a + 1)], T.pick[:, a, :], row(r), False, False, ["pick", "dh", "dl"], ["pb1"])
+
+        def tile(t):
+            bk, s = place[t]
+            return pb[bk][:, NU * s:NU * (s + 1)], "pb%d" % bk
+
+        def by_scalar(j):
+            t = on_scalar[j]
+            src, bk = tile(t)
+            a, b = T.sg2[:, 2 * j:2 * j + 1], T.sg2[:, 2 * j + 1:2 * j + 2]
+            ac(T.junk[:, 0, 0:NU], src, AF.Sign, [bk], ["junk0", "sa%d" % j], bias=WIN - 0.5, accum_out=a)
+            ac(T.junk[:, 1, 0:NU], src, AF.Sign, [bk], ["junk1", "sb%d" % j], scale=-1.0, bias=WIN, accum_out=b)
+
+        def sum_scalar(j):
+            t = on_scalar[j]
+            ac(T.res[:, t:t + 1], T.sg2[:, 2 * j:2 * j + 1], AF.Identity, ["sa%d" % j, "sb%d" % j], ["res%d" % t],
+               bias=T.sg2[:, 2 * j + 1:2 * j + 2])
+
+        def by_vector(t):
+            src, bk = tile(t)
+            op("v", [bk], ["res%d" % t],
+               lambda: vec.tensor_reduce(T.res[:, t:t + 1], src, AX.X, ALU.min, negate=True, apply_absolute_value=True))
+
+        for t in on_vector[0:5]:
+            by_vector(t)
+        for j in range(3):
+            by_scalar(j)
+            if j:
+                sum_scalar(j - 1)
+        sum_scalar(2)
+        for t in on_vector[5:]:
+            by_vector(t)
+        for a in range(8):
+            mm(pb[1][:, 12 * a:12 * (a + 1)], T.pick[:, a, :], T.res[:, 0:12], False, a == 7,
+               ["pick"] + ["res%d" % t for t in range(12)], ["pb1"])
+        tt(T.conv[:], conv, T.spc[:, 1, :, :], ALU.min, ["pb1", "spc"], ["conv"])
+        ln = "lst%d" % n
+        ts(T.lst[:, n, :], T.conv[:].indirect(T.gl2[:, 0:1]), float(MID), None, ALU.add, None, ["conv", "gl2"], [ln])
+        lst = T.lst[:, n, 0:12]
         if not last:
-            cp(T.outA[:, n, :], T.aw[:, 0:W].indirect(lst), ["aw", "ad", "lst"], ["oa%d" % n])
-            ac(T.outC[:, n, :], T.yw[:, 0:W].indirect(lst), AF.Copy, Y3 + ["yd", "lst"], ["oc%d" % n])
+            cp(T.outA[:, n, :], T.aw[:, 0:wn].indirect(lst), ["aw", ln] + AD, ["oa%d" % n])
+            ac(T.outC[:, n, :], T.yw[:, 0:wn].indirect(lst), AF.Copy, Y3 + YD + [ln], ["oc%d" % n])
             send(["oa%d" % n], lambda h: T.outA[:, n, HALF * h:HALF * (h + 1)],
                  lambda h: T.alL[:, n + 1, 16 + HALF * h:16 + HALF * (h + 1)], "ra%d" % n, "al%d" % (n + 1))
             send(["oc%d" % n], lambda h: T.outC[:, n, HALF * h:HALF * (h + 1)],
                  lambda h: T.cL[:, n + 1, HALF * h:HALF * (h + 1)], "rc%d" % n, "c%d" % (n + 1))
-            tt(T.mst[:], T.xw[:, 0:W].indirect(lst), cc, ALU.max, X3 + ["xd", "lst", cn], ["mst"])
-        tt(T.outI[:, n, :], T.sw[:, 0:W].indirect(lst), T.leno[:], ALU.add, S6 + ["sd", "lst", "leno"], ["oi%d" % n])
+            tt(T.mst[:], T.xw[:, 0:wn].indirect(lst), cc, ALU.max, X3 + ["xd", ln, cn], ["mst"])
+        tt(T.outI[:, n, :], T.sw[:, 0:wn].indirect(lst), T.leno[:], ALU.add, S6 + SD + [ln, "leno"], ["oi%d" % n])
         send(["oi%d" % n], lambda h: T.outI[:, n, HALF * h:HALF * (h + 1)],
              lambda h: T.inf[:, n + 1, HALF * h:HALF * (h + 1)], "ri%d" % n, "inf%d" % (n + 1))
         if not last:
-            o = pb[4][:, 0:NT]
-            mm(o, T.wf[:, 1, :], T.inf[:, n, :], True, False, ["wf", fn], ["pb4"])
-            mm(o, T.wab[:, 0:128], cc, False, False, ["wab", cn], ["pb4"])
-            mm(o, T.wab[:, 1:129], T.mst[:], False, False, ["wab", "mst"], ["pb4"])
-            mm(o, T.wf[:, 0, :], T.outI[:, n, :], False, True, ["wf", "oi%d" % n], ["pb4"])
-            ac(T.vv[:], o, AF.Identity, ["pb4", "col%d" % C_VB], ["vv"], bias=col(C_VB))
+            o = pb[2][:, 0:NT]
+            mm(o, T.wf[:, 1, :], T.inf[:, n, :], True, False, ["wf", fn], ["pb2"])
+            mm(o, T.wab[:, 0:128], cc, False, False, ["wab", cn], ["pb2"])
+            mm(o, T.wab[:, 1:129], T.mst[:], False, False, ["wab", "mst"], ["pb2"])
+            mm(o, T.wf[:, 0, :], T.outI[:, n, :], False, True, ["wf", "oi%d" % n], ["pb2"])
+            ac(T.vv[:], o, AF.Identity, ["pb2", "col%d" % C_VB], ["vv"], bias=col(C_VB))
             if n < NR - 2:
-                cp(T.yw[:, 0:W].indirect(lst), cc, [cn, "lst"], Y3 + ["yd"])
-            cp(T.sw[:, 0:W].indirect(lst), T.vv[:], ["vv", "lst"], S6 + ["sd"])
+                cp(T.yw[:, 0:wn].indirect(lst), cc, [cn, ln], Y3 + YD)
+            cp(T.sw[:, 0:wn].indirect(lst), T.vv[:], ["vv", ln], S6 + SD)
             if n < NR - 2:
-                cp(T.aw[:, 0:W].indirect(lst), T.alL[:, n, 16:208], [an, "lst"], ["aw", "ad"])
+                for h in range(2):
+                    later.append(lambda n=n, h=h, wn=wn, AD=AD: cp(
+                        T.aw[:, 0:wn].indirect(T.lst[:, n, 6 * h:6 * (h + 1)]), T.alL[:, n, 16 + HALF * h:16 + HALF * (h + 1)],
+                        ["al%d" % n, "lst%d" % n], ["aw"] + AD))
         else:
-            cp(T.sw[:, 0:W].indirect(lst), T.inf[:, n, :], [fn, "lst"], S6 + ["sd"])
+            cp(T.sw[:, 0:wn].indirect(lst), T.inf[:, n, :], [fn, ln], S6 + SD)
 
     fn = "inf%d" % NR
     dma("s", S6, ["yh"], T.yh[:], T.sw[R_ID::16, 0:V])

@@ -8,22 +8,21 @@ F, B, I, U = "float32", "bfloat16", "int32", "uint16"
 
 SCRATCH = {}
 for _dt, _bufs in (
-    (F, dict(sw=[W], alL=[NR, 224], inf=[NR + 1, NT], outA=[NR - 1, NT], outI=[NR, NT], tt=[416], scn=[NT], rm=[NT], sg2=[8],
-             leno=[NT], vv=[NT], pf=[12], j16=[12], g1=[12], g3=[12], g6=[24], g7=[12], g8=[8], gcol=[128], gnat=[8], thf=[4], tq=[3, 8],
-             cols=[4], wf=[2, 128], conv=[HALF], spc=[2, 8, 12])),
-    (B, dict(xw=[W], yw=[W], mx=[V], sg=[V], cL=[NR, 768], outC=[NR - 1, NT], dd=[416], rb=[NU + 7], ll=[2 * NT], junk=[2, NU + 7],
-             mst=[NT], crow=[512], wc=[6, 128], wab=[144], wm=[8], ws=[8], wsc=[8, 16], ones=[256], kc=[NT], m8=[8, 16],
-             th8=[8, 16], idb=[128], res=[16], tri=[4, NU], pick=[8, 128], cst=[8, 12])),
-    (I, dict(aw=[W], vai=[NT], gi=[12], pidx=[4], pi3=[8], g2=[12], g4=[12], g5=[24], thi=[4])),
-    (U, dict(off=[NT], lst=[NR, 16], gl=[12], gl2=[2])),
+    (F, dict(sw=[W], inf=[NR + 1, NT], outI=[NR, NT], raw=[NT], scn=[NT], rm=[NT], sg2=[8],
+             leno=[NT], vv=[NT], pf=[12], j16=[NR], g1=[6], g3=[6], g6=[6], g7=[6], g8=[8], gcol=[128], gnat=[8], thf=[4], tq=[3, 8],
+             cols=[4], wf=[4, 128], conv=[HALF], spc=[2, 8, 12])),
+    (B, dict(xw=[V], yw=[W], mx=[V], sg=[V], cL=[2 * NR, 4 * HALF], outC=[NR - 1, NT], dd=[416], rb=[NU + 7], ll=[2 * NT],
+             junk=[2, NU + 7], crow=[512], wc=[6, 128], wab=[144], wg=[128], wm=[8], ws=[8], wsc=[8, 16], ones=[256], kc=[NT],
+             m8=[8, 16], th8=[8, 16], idb=[128], res=[16], tri=[3, NU], pick=[8, 128], cst=[8, 12])),
+    (I, dict(aw=[W], alL=[NR, NT], oa=[2 * NR, 128], tt=[2, 224], gi=[12], pidx=[4], pi3=[8], g2=[6], thi=[4], thc=[4])),
+    (U, dict(off=[2 * NR, HALF], outO=[2 * NR, HALF], lst=[NR, 16], gl=[6], gl2=[2])),
 ):
     for _k, _s in _bufs.items():
         SCRATCH[_k] = ("sbuf", [128] + _s, _dt)
 for _b in range(8):
     SCRATCH["pb%d" % _b] = ("psum", [128, 512], F)
 
-SEMAPHORES = (["cv", "ca", "cp", "cg", "sent"] + ["d%d" % _i for _i in range(24)]
-              + ["ra%d" % _i for _i in range(3)] + ["rc%d" % _i for _i in range(3)] + ["ri%d" % _i for _i in range(4)])
+SEMAPHORES = (["cv", "ca", "cp", "cg", "sent"] + ["d%d" % _i for _i in range(24)] + ["r%d" % _i for _i in range(20)])
 
 GS = 16.0
 FAM = 4096.0
@@ -33,8 +32,8 @@ WF = 1024.0 * FAM
 ROUND_1, ROUND_64 = 1.5 * 2.0 ** 23, 1.5 * 2.0 ** 17
 D0 = 16
 R_A, R_B, R_HI, R_LO, R_ID, R_LEN = 0, 1, 2, 3, 4, 5
-C_VB, C_ID, C_LEN = range(3)
-P_G, P_H, P_M, P_8, P_Q, P_S1, P_S2 = range(7)
+C_VB, C_ID, C_LEN, C_TH = range(4)
+P_G, P_H, P_M, P_8, P_Q, P_1, P_S1, P_S2, P_16 = range(9)
 
 
 def rank_program(g, core, T, topo):
@@ -48,7 +47,7 @@ def rank_program(g, core, T, topo):
     count = {}
     waited = {q: {} for q in queues}
     lastw, readers = {}, {}
-    ndma = [0]
+    ndma, nsend = [0], [0]
 
     def need(q, toks):
         top = {}
@@ -83,8 +82,6 @@ def rank_program(g, core, T, topo):
             readers[k] = []
 
     def op(q, rd, wr, call):
-        if q == "g":
-            wr = wr + ["pool"]
         order(q, rd, wr)
         sem = csem[q]
         count[sem] = count.get(sem, 0) + 1
@@ -99,20 +96,24 @@ def rank_program(g, core, T, topo):
         queues[q].dma_start(out, in_, **kw).then_inc(T.sem[sem], 16)
         done((sem, 16, "dma"), rd, wr)
 
-    def send(rd, src, dst, sem, key):
+    def send(rd, moves, keys):
         order("g", rd, [])
-        trs, sent = [], 0
-        for h, to in enumerate((nxt, prv)):
+        sem = "r%d" % nsend[0]
+        nsend[0] += 1
+        trs = []
+        count[sem] = 0
+        for j, (h, src, dst) in enumerate(moves):
+            to, frm = (nxt, prv)[h], (prv, nxt)[h]
             eng = topo.engines(core, to)
-            eng = eng[h * (len(eng) // 2):(h + 1) * (len(eng) // 2)]
+            eng = eng[j * len(eng) // len(moves):(j + 1) * len(eng) // len(moves)]
             rid, pid = topo.addr(to)[0:2]
             trs.append(RemoteDMATransfer(dst_ids=[DstId(rid=rid, pnc=pid)], dma_engine_mask=sum(1 << e for e in eng),
-                                         remote_sem=T.sem[sem], src=src(h), dst=dst(h)))
-            sent += len(eng)
+                                         remote_sem=T.sem[sem], src=src, dst=dst))
+            count["sent"] = count.get("sent", 0) + len(eng)
+            count[sem] += len(topo.engines(frm, core)) // len(moves)
         g.remote_dma_fused(trs, local_sem=T.sem.sent)
-        count["sent"] = count.get("sent", 0) + sent
-        count[sem] = len(topo.engines(prv, core)) // 2 + len(topo.engines(nxt, core)) // 2
-        lastw[key] = (sem, count[sem], "remote")
+        for k in keys:
+            lastw[k] = (sem, count[sem], "remote")
 
     vec, act, pe = g.vector, g.scalar, g.tensor
 
@@ -141,19 +142,21 @@ def rank_program(g, core, T, topo):
         op("p", rd, wr, lambda: pe.matmul(out, lhsT, rhs, start, stop))
 
     def iota(out, pat, base, ch, wr, flag=True):
+        rd = [] if "pool" in wr else ["pool"]
         if flag:
-            op("g", [], wr, lambda: g.iota(out, pat, base, ch, allow_small_or_imprecise_dtypes=True))
+            op("g", rd, wr, lambda: g.iota(out, pat, base, ch, allow_small_or_imprecise_dtypes=True))
         else:
-            op("g", [], wr, lambda: g.iota(out, pat, base, ch))
+            op("g", rd, wr, lambda: g.iota(out, pat, base, ch))
 
     def sel(out, in_, pat, cmp, fill, base, ch, rd, wr):
-        op("g", rd, wr, lambda: g.affine_select(out, in_, pat, cmp, fill, base, ch))
+        op("g", rd + ([] if "pool" in wr else ["pool"]), wr, lambda: g.affine_select(out, in_, pat, cmp, fill, base, ch))
 
     pb = [T["pb%d" % b] for b in range(8)]
     X3, Y3 = ["x0", "x1", "x2", "x3"], ["y0", "y1", "y2", "y3"]
-    part = (0, 0, 1, 1, 2, 3)
-    S6 = ["s%d" % j for j in range(6)]
-    MX = ["mx%d" % k for k in range(16)]
+    pieces = [(512 * j, 512 * (j + 1)) for j in range(5)] + [(2560, 2816), (2816, V)]
+    part = (0, 0, 1, 1, 2, 2, 3)
+    S6 = ["s%d" % j for j in range(len(pieces))]
+    MX = ["mx%d" % k for k in range(32)]
 
     def pc(j):
         return T.pf[:, j:j + 1]
@@ -164,34 +167,38 @@ def rank_program(g, core, T, topo):
     def spare(n):
         return slice(V + NT * n, V + NT * (n + 1))
 
-    for j, (a, b) in enumerate(((0, 1024), (1024, 2048), (2048, 2560), (2560, V))):
+    mset(T.thc[:], 0, ["thc"])
+    dma("s", [], ["oa0", "oa1"], T.oa[:, 0:2, 16:16 + HALF], T.va[:])
+    for j, (a, b) in enumerate(((0, 1024), (1024, 2048), (2048, 2816), (2816, V))):
         dma("a", [], [Y3[j]], T.yw[:, a:b], T.hx[:, a:b])
         dma("s", [], [X3[j]], T.xw[:, a:b], T.fx[:, a:b])
         if j == 0:
-            dma("s", [], ["vai"], T.vai[:], T.va[:])
-    dma("a", [], ["c0"], T.cL[:, 0, 0:NT], T.vx[:])
+            dma("a", [], ["c0", "c1"], T.cL[:, 0:2, 0:HALF], T.vx[:])
+            dma("s", [], ["thi"], T.thi[0:8, 0:1], T.th[:, 0])
     dma("s", [Y3[3], X3[3]], ["aw"], T.aw[:, 0:V], T.ha[:])
     dma("s", [], ["ad0"], T.aw[:, spare(0)], T.va[:])
     dma("s", [], ["yd0"], T.yw[:, spare(0)], T.vx[:])
+    dma("s", [], ["al0"], T.alL[:, 0, :], T.va[:])
+    dma("s", [], ["thc"], T.thc[R_B::16, 0:1], T.th[:, 0])
 
     iota(T.pidx[:, 0:1], [[0, 1]], 0, 1, ["pidx"], flag=False)
     mset(T.ones[:], 1.0, ["ones"])
     mset(T.crow[0:64, :], 0.0, ["crow"])
     mset(T.wc[0:96, :, :], 0.0, ["wc"])
-    iota(T.gcol[:], [[1, 2], [2, 4], [0, 16]], 0, 0, ["gcol"])
     CR = ["cr%d" % j for j in range(10)]
     WCK = ["wa%d" % j for j in range(8)]
     for k in CR:
         lastw[k] = lastw["crow"]
     for k in WCK:
         lastw[k] = lastw["wc"]
-    iota(T.crow[32:33, 0:64], [[1, 64]], 0, 0, [CR[0]])
     iota(T.gnat[:], [[1, 8]], 0, 0, ["gnat"])
-    iota(T.j16[:], [[16, 12]], 0, 0, ["j16"])
-    iota(T.wc[64:65, :, R_HI::16], [[8, 6], [0, 8]], -MID // 64, 0, [WCK[6]])
-    iota(T.wc[64:65, :, R_ID::16], [[512, 6], [0, 8]], V * rank, 0, [WCK[7]])
     sel(T.idb[:], T.ones[:, 0:128], [[-1, 128]], ALU.is_equal, 0.0, 0, 1, ["ones"], ["idb"])
-    dma("g", [], ["thi"], T.thi[0:8, 0:1], T.th[:], allow_slow_non_contiguous=True)
+    iota(T.crow[32:33, 0:64], [[1, 64]], 0, 0, [CR[0], "pool"])
+    iota(T.wc[64:65, :, R_HI::16], [[8, 6], [0, 8]], -MID // 64, 0, [WCK[6], "pool"])
+    iota(T.wc[64:65, :, R_ID::16], [[512, 6], [0, 8]], V * rank, 0, [WCK[7], "pool"])
+    iota(T.g1[:], [[256, 6]], 0, 16, ["g1"])
+    iota(T.gcol[:], [[1, 2], [2, 4], [0, 16]], 0, 0, ["gcol"])
+    iota(T.j16[:], [[NT, NR]], 0, 0, ["j16"])
     for j in range(1, 8):
         aset(T.crow[0:1, 64 * j:64 * (j + 1)], T.ones[0:1, 0:64], float(j), [CR[j]])
         if j in (3, 5, 7):
@@ -205,184 +212,237 @@ def rank_program(g, core, T, topo):
     ts(T.pi3[:, P_M:P_M + 1], T.pidx[:, 0:1], 15, None, ALU.bitwise_and, None, ["pidx"], ["pi2"])
     ts(T.pi3[:, P_8:P_8 + 1], T.pidx[:, 0:1], 3, 1, ALU.arith_shift_right, ALU.bitwise_and, ["pidx"], ["pi3"])
     ts(T.pi3[:, P_Q:P_Q + 1], T.pidx[:, 0:1], 5, None, ALU.arith_shift_right, None, ["pidx"], ["pi4"])
+    ts(T.pi3[:, P_1:P_1 + 1], T.pidx[:, 0:1], 1, None, ALU.bitwise_and, None, ["pidx"], ["pi5"])
     mset(T.wab[:], 0.0, ["wab"])
-    cp(T.pf[:, 0:5], T.pi3[:, 0:5], ["pi0", "pi1", "pi2", "pi3", "pi4"], ["pf"])
-    aset(T.alL[:, :, 0:16], T.ones[:, 0:64], 0.0, ["pad0"])
-    aset(T.alL[:, :, 208:224], T.ones[:, 0:64], 0.0, ["pad1"])
+    cp(T.pf[:, 0:6], T.pi3[:, 0:6], ["pi%d" % j for j in range(6)], ["pf"])
+    mset(T.oa[:, :, 0:16], 0, ["pad0"])
+    mset(T.oa[:, :, 16 + HALF:128], 0, ["pad1"])
     aset(T.ws[:], T.ones[:, 0:8], 0.0, ["ws"])
     aset(T.tq[:], T.ones[:, 0:24], 0.0, ["tq"])
-    aset(T.rm[:], T.ones[:, 0:NT], 1.0, ["rm"])
-    aset(T.cst[0:1, :, :], T.ones[0:1, 0:HALF], WIN * FAM, ["cst"])
-    aset(T.rm[:, 0::16], T.ones[:, 0:12], 0.0, ["rm"])
     ts(T.wab[:, 1:129:16], T.gnat[:], pc(P_G), None, ALU.is_equal, None, ["gnat", "pf"], ["wab"])
-    ts(T.g1[:], T.j16[:], pc(P_M), None, ALU.add, None, ["j16", "pf"], ["g1"])
-    ts(pc(P_S1), pc(P_H), -416.0, 224.0, ALU.mult, ALU.add, ["pf"], ["pf1"])
-    ts(pc(P_S2), pc(P_H), 208.0, None, ALU.mult, None, ["pf"], ["pf2"])
-    ts(T.g2[:], T.g1[:], -5.5, 1.0 / 12.0, ALU.add, ALU.mult, ["g1"], ["g2"])
+    ts(pc(P_S1), pc(P_G), -256.0, -40.0, ALU.mult, ALU.add, ["pf"], ["pf1"])
+    ts(pc(P_S2), pc(P_1), pc(P_H), 112.0, ALU.not_equal, ALU.mult, ["pf"], ["pf2"])
     ts(T.wm[:], T.gcol[:, 0::16], pc(P_G), -2.0 * GS, ALU.is_equal, ALU.mult, ["gcol", "pf"], ["wm"])
-    ts(T.g3[:], T.g2[:], -12.0, None, ALU.mult, None, ["g2"], ["g3"])
-    tt(T.g4[:], T.g3[:], T.g1[:], ALU.add, ["g3", "g1"], ["g4"])
+    ts(T.g2[:], T.g1[:], pc(P_S1), 1.0 / HALF, ALU.add, ALU.mult, ["g1", "pf1"], ["g2"])
+    ts(T.g7[:], T.g1[:], pc(P_S1), pc(P_S2), ALU.add, ALU.add, ["g1", "pf1", "pf2"], ["g7"])
     ts(T.wsc[:], T.gcol[:], pc(P_G), GS, ALU.is_equal, ALU.mult, ["gcol", "pf"], ["wsc"])
-    ts(T.g5[:, 0:12], T.g4[:], 1, None, ALU.arith_shift_right, None, ["g4"], ["g5a"])
-    ts(T.g5[:, 12:24], T.g4[:], 1, None, ALU.bitwise_and, None, ["g4"], ["g5b"])
-    ts(T.rb[:, NT:NU], pc(P_M), 5.0, -2.0, ALU.is_equal, ALU.mult, ["pf"], ["rbx"])
-    ts(T.g6[:, 0:12], T.g5[:, 0:12], 32.0, None, ALU.mult, None, ["g5a"], ["g6a"])
-    ts(T.g6[:, 12:24], T.g5[:, 12:24], pc(P_S1), pc(P_S2), ALU.mult, ALU.add, ["g5b", "pf1", "pf2"], ["g6b"])
-    ts(T.g8[:, 1:2], pc(P_H), 4.0, pc(P_Q), ALU.mult, ALU.add, ["pf"], ["g81"])
-    ts(T.g8[:, 2:3], pc(P_H), 44.0, -88.0, ALU.mult, ALU.add, ["pf"], ["g82"])
-    tt(T.g7[:], T.g6[:, 0:12], T.g2[:], ALU.add, ["g6a", "g2"], ["g7"])
-    ts(T.g8[:, 0:1], pc(P_M), 12.0, T.g8[:, 1:2], ALU.mult, ALU.add, ["g81", "pf"], ["g80"])
-    tt(T.g3[:], T.g7[:], T.g6[:, 12:24], ALU.add, ["g7", "g6b"], ["g3"])
-    ts(T.g8[:, 3:4], T.g8[:, 2:3], pc(P_8), T.g8[:, 0:1], ALU.mult, ALU.add, ["g82", "g80", "pf"], ["g83"])
-    cp(T.gl[:], T.g3[:], ["g3"], ["gl"])
-    ts(T.gl2[:, 0:1], T.g8[:, 3:4], HALF - 1.0, None, ALU.min, None, ["g83"], ["gl2"])
+    ts(T.g3[:], T.g2[:], 1.0 - HALF, 40.0, ALU.mult, ALU.add, ["g2"], ["g3"])
+    ts(pc(P_16), pc(P_G), -16.0, None, ALU.mult, None, ["pf"], ["pf16"])
+    tt(T.g6[:], T.g7[:], T.g3[:], ALU.add, ["g7", "g3"], ["g6"])
+    cp(T.gl[:], T.g6[:], ["g6"], ["gl"])
 
-    def lists(n):
-        op("v", ["al%d" % n], ["tt1"], lambda: vec.transpose(T.tt[:, 0:192], T.alL[:, n, 16:208]))
-        op("v", ["al%d" % n, "pad0", "pad1"], ["tt2"], lambda: vec.transpose(T.tt[:, 192:416], T.alL[:, n, 0:224]))
-        cp(T.off[:], T.tt[:, 0:416].indirect(T.gl[:]), ["tt1", "tt2", "gl"], ["off"])
+    def turns(s):
+        h = s % 2
+        op("v", ["oa%d" % s], ["tt%da" % h], lambda: vec.transpose(T.tt[:, h, 0:HALF], T.oa[:, s, 16:16 + HALF]))
+        op("v", ["oa%d" % s, "pad0", "pad1"], ["tt%db" % h], lambda: vec.transpose(T.tt[:, h, HALF:224], T.oa[:, s, :]))
 
-    def copies(n):
-        sel(T.cL[:, n, 192:384], T.cL[:, n, 0:192], [[0, 192]], ALU.is_ge, 0.0, 0, 0, ["c%d" % n], ["c%db" % n])
-        sel(T.cL[:, n, 384:768], T.cL[:, n, 0:384], [[0, 384]], ALU.is_ge, 0.0, 0, 0, ["c%d" % n, "c%db" % n], ["c%dc" % n])
+    def offsets(s, out, key):
+        cp(out[:, s, :], T.tt[:, s % 2, :].indirect(T.gl[:]), ["tt%da" % (s % 2), "tt%db" % (s % 2), "gl"], [key + str(s)])
+
+    def copies(s, q):
+        for w, rd, wr in ((HALF, ["c%d" % s], "c%db" % s), (NT, ["c%d" % s, "c%db" % s], "c%dc" % s)):
+            if q == "g":
+                sel(T.cL[:, s, w:2 * w], T.cL[:, s, 0:w], [[0, w]], ALU.is_ge, 0.0, 0, 0, rd, [wr])
+            else:
+                ac(T.cL[:, s, w:2 * w], T.cL[:, s, 0:w], AF.Copy, rd, [wr])
+
+    def numbers(j):
+        a, b = pieces[j]
+        mm(pb[j % 6][:, 0:b - a], T.wc[0:65, a // 512, :], T.crow[0:65, a % 512:a % 512 + b - a], True, False, CR + WCK, ["pb%d" % (j % 6)])
 
     for j in range(6):
-        mm(pb[j][:], T.wc[0:65, j, :], T.crow[0:65, :], True, False, CR + WCK, ["pb%d" % j])
+        numbers(j)
 
     iota(T.kc[0:1, :], [[0, 12], [-1, 16]], 7, 0, ["kc"])
     sel(T.m8[0:8, :, :], T.ones[0:8, 0:128], [[-1, 2], [-2, 4], [0, 16]], ALU.is_equal, 0.0, 0, 1, ["ones"], ["m8"])
-    for r, val in ((R_A, 2.0 * GS), (R_B, -GS), (R_HI, 64.0 / FAM), (R_LO, 1.0 / FAM)):
+    for j in range(3):
+        lastw["tq%d" % j] = lastw["tq"]
+    for (r, val), (j, r2, val2) in zip(((R_A, 2.0 * GS), (R_B, -GS), (R_HI, 64.0 / FAM), (R_LO, 1.0 / FAM)),
+                                       ((0, R_LEN, 1.0), (1, R_ID, 1.0), (2, R_LEN, 1.0), (None, None, None))):
         sel(T.ws[:], T.ws[:], [[-16, 2], [-32, 4]], ALU.not_equal, val, -r, 1, ["ws"], ["ws"])
-    iota(T.tri[:], [[0, 4 * NU]], 1 - int(WIN), 0, ["tri"])
+        if j is not None:
+            sel(T.tq[:, j, :], T.tq[:, j, :], [[-16, 8]], ALU.not_equal, val2, -r2, 1, ["tq%d" % j], ["tq%d" % j])
+    copies(1, "g")
+    copies(0, "g")
+    iota(T.tri[:], [[0, 3 * NU]], 1 - int(WIN), 0, ["tri", "tr0", "tr64"])
+    iota(T.inf[:, 0, :], [[1, NT]], n_ranks * V + NT * rank, 0, ["inf0"])
     sel(T.tri[:, 0:2, 0:NT], T.tri[:, 0:2, 0:NT], [[0, 2], [-1, NT]], ALU.is_gt, -WIN, 0, 1, ["tri"], ["tri"])
-    copies(0)
     for p in (0, 64):
-        sel(T.tri[p:p + 64, 2:4, 128:NT], T.tri[p:p + 64, 2:4, 128:NT], [[0, 2], [-1, 64]], ALU.is_gt, -WIN, 0, 1, ["tri"], ["tri"])
-
-    def late_tables():
-        for j in range(3):
-            lastw["tq%d" % j] = lastw["tq"]
-        for j, r, val in ((0, R_A, -120.0), (1, R_ID, 1.0), (2, R_LEN, 1.0), (0, R_LEN, 1.0)):
-            sel(T.tq[:, j, :], T.tq[:, j, :], [[-16, 8]], ALU.not_equal, val, -r, 1, ["tq%d" % j], ["tq%d" % j])
-        iota(T.inf[:, 0, :], [[1, NT]], n_ranks * V + NT * rank, 0, ["inf0"])
-        iota(T.spc[:, 0, :, 0:8], [[16, 8], [0, 8]], V - MID, 1, ["spa"])
-        iota(T.spc[:, 0, :, 8:12], [[0, 2], [16, 4], [0, 4]], V - MID + 128, 1, ["spb"])
-        sel(T.pick[:], T.pick[:], [[-16, 8], [0, 8], [-1, 16]], ALU.is_equal, 0.0, 0, 1, ["pick"], ["pick"])
-        iota(T.wf[:], [[0, 256]], 0, 0, ["wf"])
-        for j, r in ((0, R_HI), (1, R_ID), (0, R_LO)):
-            sel(T.wf[:, j, r::16], T.wf[:, j, r::16], [[-16, 8]], ALU.not_equal, 1.0, -r, 1, ["wf"], ["wf"])
-
-    on_scalar = (4, 5, 7)
-    for t in on_scalar:
-        aset(T.cst[0:1, :, t], T.ones[0:1, 0:8], 0.0, ["cst"])
-
-    def weights():
-        for j, (r, val) in enumerate(((0, WF), (1, WF), (2, 2.0), (6, -WF), (7, -WF), (8, -2.0))):
-            mset(row(r), val, ["dw%d" % j])
+        sel(T.tri[p:p + 64, 2, 128:NT], T.tri[p:p + 64, 2, 128:NT], [[-1, 64]], ALU.is_gt, -WIN, 0, 1, ["tr%d" % p], ["tr%d" % p] + ["pool"] * (p > 0))
+    iota(T.spc[:, 0, :, 0:8], [[16, 8], [0, 8]], V - MID, 1, ["spa"])
+    iota(T.spc[:, 0, :, 8:12], [[0, 2], [16, 4], [0, 4]], V - MID + 128, 1, ["spb"])
+    PK = ["pick%d" % a for a in range(4)]
+    for a in range(4):
+        sel(T.pick[:, 2 * a:2 * a + 2, :], T.ones[:], [[-16, 2], [0, 8], [-1, 16]], ALU.is_equal, 0.0, -32 * a, 1, ["ones"], [PK[a]])
+    WF8 = ["wf%d" % j for j in range(8)]
+    iota(T.wf[:], [[0, 512]], 0, 0, WF8)
+    iota(T.wg[:], [[0, 128]], 0, 0, ["wg"])
+    for i, (j, r, r2, val) in enumerate(((0, R_HI, R_HI, 1.0), (0, R_LO, R_LO, 1.0), (0, R_A, R_B, -2.0), (1, R_ID, R_ID, 1.0),
+                                         (2, R_LEN, R_LEN, 1.0), (3, R_ID, R_ID, 1.0), (3, R_LEN, R_LEN, 1.0), (0, R_B, R_B, 1.0))):
+        k = WF8[2 if i == 7 else i]
+        sel(T.wf[:, j, r2::16], T.wf[:, j, r2::16], [[-16, 8]], ALU.not_equal, val, -r, 1, [k], [k])
+    sel(T.wg[:, R_B::16], T.wg[:, R_B::16], [[-16, 8]], ALU.not_equal, 1.0, -2, 1, ["wg"], ["wg"])
 
     def row(r):
         return T.dd[:, D0 + r:D0 + 32 * 12:32]
 
+    on_scalar = (4, 5, 7)
     DW = ["dw%d" % j for j in range(6)]
+    aset(T.dd[:, 0:208], T.ones[:, 0:208], 0.0, ["dd0"])
+    aset(T.dd[:, 208:416], T.ones[:, 0:208], 0.0, ["dd1"])
+    aset(T.rm[:], T.ones[:, 0:NT], 1.0, ["rm"])
+    aset(T.cst[0:1, :, :], T.ones[0:1, 0:HALF], WIN, ["cst"])
+    for k in DW + ["dh", "dl", "dg"]:
+        lastw[k] = lastw["dd1"]
+    for j, (r, val) in enumerate(((0, WF), (1, WF), (2, 2.0), (6, -WF), (7, -WF), (8, -2.0))):
+        aset(row(r), T.ones[:, 0:12], val, [DW[j]])
+    aset(T.rm[:, 0::16], T.ones[:, 0:12], 0.0, ["rm"])
+    for j, t in enumerate(on_scalar):
+        lastw["cst%d" % j] = lastw["cst"]
+        aset(T.cst[0:1, :, t], T.ones[0:1, 0:8], 0.0, ["cst%d" % j])
+
+    turns(1)
+    turns(0)
+    offsets(1, T.off, "off")
+    offsets(0, T.off, "off")
     fill = [
-        lambda: mset(T.pick[:], FAM, ["pick"]),
-        lambda: mset(T.dd[:], 0.0, DW + ["dh", "dl", "dg"]),
-        lambda: cp(T.alL[:, 0, 16:208], T.vai[:], ["vai"], ["al0"]),
-        lambda: lists(0),
-        lambda: mset(T.xw[:, V:W], 0.0, ["xd"]),
-        weights,
-        lambda: ts(T.g8[:, 4:5], pc(P_G), -16.0, None, ALU.mult, None, ["pf"], ["g84"]),
         lambda: ts(T.thf[0:8, 0:1], T.thi[0:8, 0:1], -GS, 240.0 * GS, ALU.mult, ALU.add, ["thi"], ["thf"]),
-        lambda: ts(T.g8[:, 4:8], T.j16[:, 0:4], NT / 16.0, T.g8[:, 4:5], ALU.mult, ALU.add, ["j16", "g84"], ["g84"]),
+        lambda: ts(T.g8[:, 4:8], T.j16[:], pc(P_16), 1.0 / FAM, ALU.add, ALU.mult, ["j16", "pf16"], ["g84"]),
         lambda: ts(T.th8[0:8, :, :], T.m8[0:8, :, :], T.thf[0:8, 0:1], None, ALU.mult, None, ["m8", "thf"], ["th8"]),
     ]
-    cuts = (0, 2, 4, 6, 8, 10, 10)
 
     def ycopy(j):
-        mm(pb[6 + j % 2][:], T.idb[:], T.yw[:, 512 * j:512 * (j + 1)], True, True, ["idb", Y3[part[j]]], ["pb%d" % (6 + j % 2)])
+        a, b = pieces[j]
+        mm(pb[6 + j % 2][:, 0:b - a], T.idb[:], T.yw[:, a:b], True, True, ["idb", Y3[part[j]]], ["pb%d" % (6 + j % 2)])
 
     ycopy(0)
     ycopy(1)
-    for j in range(6):
-        a, b = 512 * j, 512 * (j + 1)
-        tt(T.mx[:, a:b], T.xw[:, a:b], pb[6 + j % 2][:], ALU.max, [X3[part[j]], "pb%d" % (6 + j % 2)], ["im%d" % j])
-        mm(pb[j][:], T.wab[:, 0:128], T.yw[:, a:b], False, False, ["wab", Y3[part[j]]], ["pb%d" % j])
-        if j in (1, 3, 4):
+    for j, (a, b) in enumerate(pieces):
+        o, bk = pb[j % 6][:, 0:b - a], "pb%d" % (j % 6)
+        tt(T.mx[:, a:b], T.xw[:, a:b], pb[6 + j % 2][:, 0:b - a], ALU.max, [X3[part[j]], "pb%d" % (6 + j % 2)], ["im%d" % j])
+        mm(o, T.wab[:, 0:128], T.yw[:, a:b], False, False, ["wab", Y3[part[j]]], [bk])
+        if j in (1, 3, 4, 5):
             ycopy(j + 1)
-        mm(pb[j][:], T.wab[:, 1:129], T.mx[:, a:b], False, True, ["wab", "im%d" % j], ["pb%d" % j])
-        for k in MX[a // 192:(b - 1) // 192 + 1]:
-            readers.setdefault(k, []).append(lastw["pb%d" % j])
+        mm(o, T.wab[:, 1:129], T.mx[:, a:b], False, True, ["wab", "im%d" % j], [bk])
+        for k in MX[a // HALF:(b - 1) // HALF + 1]:
+            readers.setdefault(k, []).append(lastw[bk])
         if j == 1:
             ycopy(j + 2)
-        ac(T.sw[:, a:b], pb[j][:], AF.Copy, ["pb%d" % j], [S6[j]])
-        for f in fill[cuts[j]:cuts[j + 1]]:
-            f()
-    late_tables()
+        ac(T.sw[:, a:b], o, AF.Copy, [bk], [S6[j]])
+        if j == 1:
+            numbers(6)
+        if j < len(fill):
+            fill[j]()
 
     def late_constants():
         for c in (C_VB, C_ID, C_LEN):
             op("v", ["tq%d" % c], ["col%d" % c], lambda c=c: vec.tensor_reduce(col(c), T.tq[:, c, :], AX.X, ALU.add))
+        ts(T.rb[:, NT:NU], pc(P_M), 5.0, -2.0, ALU.is_equal, ALU.mult, ["pf"], ["rbx"])
+        ts(col(C_TH), T.thc[:, 0:1], col(C_VB), None, ALU.add, None, ["thc", "col%d" % C_VB], ["col%d" % C_TH])
 
-    chunks = ((0, 1), (1, 2), (2, 4), (4, 6), (6, 10), (10, 12), (12, 14), (14, 15), (15, 16))
-    achunks = ((0, 5), (5, 10), (10, 12), (12, 14), (14, 15), (15, 16))
-    banks = ((3, (0, 1)), (4, (4, 5)), (5, (2, 3)), (0, (6, 7)), (6, (8, 9)), (7, (10, 11)))
+    def conv_list():
+        ts(T.g8[:, 1:2], pc(P_H), 4.0, pc(P_Q), ALU.mult, ALU.add, ["pf"], ["g81"])
+        ts(T.g8[:, 2:3], pc(P_H), 44.0, -88.0, ALU.mult, ALU.add, ["pf"], ["g82"])
+        ts(T.g8[:, 0:1], pc(P_M), 12.0, T.g8[:, 1:2], ALU.mult, ALU.add, ["g81", "pf"], ["g80"])
+        ts(T.g8[:, 3:4], T.g8[:, 2:3], pc(P_8), T.g8[:, 0:1], ALU.mult, ALU.add, ["g82", "g80", "pf"], ["g83"])
+        ts(T.gl2[:, 0:1], T.g8[:, 3:4], HALF - 1.0, None, ALU.min, None, ["g83"], ["gl2"])
+
+    chunks = ((0, 2), (2, 6), (6, 10), (10, 14), (14, 16), (16, 20), (20, 24), (24, 28), (28, 30), (30, 31), (31, 32))
+    achunks = ((0, 8), (8, 16), (16, 24), (24, 28), (28, 30), (30, 31), (31, 32))
+    banks = ((3, (0, 8)), (4, (4, 5)), (5, (1, 9)), (0, (6, 7)), (6, (2, 10)), (7, (3, 11)))
     place = {t: (bk, s) for bk, two in banks for s, t in enumerate(two)}
-    on_vector = (0, 1, 2, 3, 6, 8, 9, 10, 11)
+    on_vector = (0, 8, 1, 9, 6, 2, 10, 3, 11)
 
     def ties(bk, two):
-        j = 0 if two[0] < 8 else 2
-        mm(pb[bk][:, 0:2 * NU], T.idb[:], T.tri[:, j:j + 2, :], True, False, ["idb", "tri"], ["pb%d" % bk])
+        j = 0 if two[1] < 8 else 1
+        mm(pb[bk][:, 0:2 * NU], T.idb[:], T.tri[:, j:j + 2, :], True, False, ["idb", "tri", "tr0", "tr64"], ["pb%d" % bk])
 
-    def keyed(data, c0, wts, k, last, rd):
-        if k is None:
-            outs = (pb[0][:, 0:128], pb[0][0:64, 128:NT], pb[0][64:128, 128:NT])
+    def keyed(h, data, wts, k, last, rd):
+        def cols(a, b):
+            return slice(a, b) if k is None else slice(a + k, b, 16)
+        if h:
+            mm(pb[0][0:64, cols(128, NT)], data(32, HALF), wts(0, 4), False, False, rd, ["pb0"])
+            mm(pb[0][64:128, cols(128, NT)], data(32, HALF), wts(4, 8), False, False, rd, ["pb0"])
+            mm(pb[0][HALF:128, cols(0, 128)], data(0, 32), wts(0, 8), False, last, rd, ["pb0"])
         else:
-            outs = (pb[0][:, k:128:16], pb[0][0:64, 128 + k:NT:16], pb[0][64:128, 128 + k:NT:16])
-        mm(outs[1], data(c0 + 128, c0 + NT), wts(0, 4), False, False, rd, ["pb0"])
-        mm(outs[2], data(c0 + 128, c0 + NT), wts(4, 8), False, False, rd, ["pb0"])
-        mm(outs[0], data(c0, c0 + 128), wts(0, 8), False, last, rd, ["pb0"])
+            mm(pb[0][0:HALF, cols(0, 128)], data(0, HALF), wts(0, 8), False, last, rd, ["pb0"])
 
-    later = []
+    later = [late_constants, conv_list]
+
+    def half(t, n, h):
+        return t[:, n, HALF * h:HALF * (h + 1)]
+
+    def send_ids(n):
+        send(["oi%d" % n], [(h, half(T.outI, n, h), half(T.inf, n + 1, h)) for h in range(2)], ["inf%d" % (n + 1)])
+
+    def meanwhile():
+        if later:
+            later.pop(0)()
+
     for n in range(NR):
         last = n == NR - 1
-        cn, an, fn = "c%d" % n, "al%d" % n, "inf%d" % n
-        cc = T.cL[:, n, 0:NT]
+        an, fn = "al%d" % n, "inf%d" % n
         wn = V + NT * (n + 1)
         AD, YD, SD = (["%s%d" % (s, j) for j in range(n + 1)] for s in ("ad", "yd", "sd"))
         if n > 0:
-            lists(n)
-            copies(n)
+            copies(2 * n + 1, "a")
+            copies(2 * n, "g")
+            send_ids(n - 1)
             if not last:
-                dma("s", [cn], ["yd%d" % n], T.yw[:, spare(n)], cc)
+                dma("s", ["c%d" % (2 * n), "c%d" % (2 * n + 1)], ["yd%d" % n], T.yw[:, spare(n)], T.cL[:, 2 * n:2 * n + 2, 0:HALF])
+                dma("s", [an], ["ad%d" % n], T.aw[:, spare(n)], T.alL[:, n, :])
             for bk, two in banks:
                 if bk:
                     ties(bk, two)
         mm(pb[0][:, 0:NT], T.ones[0:1, 0:128], T.kc[0:1, :], True, False, ["ones", "kc"], ["pb0"])
-        keyed(lambda a, b: T.ones[0:8, a:b], 0, lambda s, d: T.th8[0:8, s:d, :], None, False, ["ones", "th8"])
-        keyed(lambda a, b: T.cL[:, n, a:b], 0, lambda s, d: T.wsc[:, s:d, :], None, False, [cn, "wsc"])
+        for h in range(2):
+            keyed(h, lambda a, b: T.ones[0:8, a:b], lambda a, b: T.th8[0:8, a:b, :], None, False, ["ones", "th8"])
+        lag = 2 if n == 0 else 0
+
+        def slot(a):
+            return 2 * n + 1 - a // 16
+
+        def offs(a, b):
+            return T.off[:, slot(a), 6 * (a % 16):6 * (a % 16 + b - a)]
+
+        def rows_of(a, b):
+            return T.sg[:, HALF * a:HALF * b], T.sw[:, 0:V].indirect(offs(a, b))
+
+        def own(j):
+            keyed(slot(j) % 2, lambda a, b: T.sg[:, HALF * j + a:HALF * j + b], lambda a, b: T.ws[:, a:b], j % 16, j % 16 == 15,
+                  ["sg%d" % j, "ws"])
+
         for (a, b) in achunks:
-            ac(T.sg[:, NT * a:NT * b], T.sw[:, 0:V].indirect(T.off[:, 12 * a:12 * b]), AF.Copy, S6 + ["off"], ["sg%d" % k for k in range(a, b)])
+            if b <= 32 - lag:
+                ac(*rows_of(a, b), AF.Copy, S6 + ["off%d" % slot(a)], ["sg%d" % j for j in range(a, b)])
+        jdone = 0
         for (a, b) in chunks:
+            s = slot(a)
+            cn = "c%d" % s
+            if a % 16 == 0:
+                keyed(s % 2, lambda a, b: T.cL[:, s, a:b], lambda a, b: T.wsc[:, a:b, :], None, False, [cn, "wsc"])
             ck = [cn] + ([cn + "b"] if b - a > 1 else []) + ([cn + "c"] if b - a > 2 else [])
-            tt(T.mx[:, NT * a:NT * b], T.xw[:, 0:V].indirect(T.off[:, 12 * a:12 * b]), T.cL[:, n, 0:NT * (b - a)], ALU.max,
-               X3 + ["off"] + ck, MX[a:b])
-            for k in range(a, b):
-                keyed(lambda a, b: T.mx[:, a:b], NT * k, lambda s, d: T.wm[:, s:d], k, False, [MX[k], "wm"])
-                keyed(lambda a, b: T.sg[:, a:b], NT * k, lambda s, d: T.ws[:, s:d], k, k == 15, ["sg%d" % k, "ws"])
+            tt(T.mx[:, HALF * a:HALF * b], T.xw[:].indirect(offs(a, b)), T.cL[:, s, 0:HALF * (b - a)], ALU.max,
+               X3 + ["off%d" % s] + ck, MX[a:b])
+            for j in range(a, b):
+                keyed(s % 2, lambda a, b: T.mx[:, HALF * j + a:HALF * j + b], lambda a, b: T.wm[:, a:b], j % 16, False, [MX[j], "wm"])
+            upto = max([0] + [e for (_, e) in achunks if e + lag <= b])
+            for j in range(jdone, upto):
+                own(j)
+            jdone = upto
             if n == 0 and b == 6:
                 for bk, two in banks:
                     if bk:
                         ties(bk, two)
-        if n == 0:
-            late_constants()
-        elif not last:
-            cp(T.aw[:, spare(n)], T.alL[:, n, 16:208], [an], ["ad%d" % n])
+        if lag:
+            cp(*rows_of(jdone, 32), S6 + ["off%d" % slot(jdone)], ["sg%d" % j for j in range(jdone, 32)])
+            for j in range(jdone, 32):
+                own(j)
+        meanwhile()
         ac(T.sw[:, spare(n)], T.inf[:, n, :], AF.Identity, [fn, "col%d" % C_ID], ["sd%d" % n], scale=col(C_ID))
-        if n == 0:
-            ac(T.leno[:], T.inf[:, n, :], AF.Identity, [fn], ["leno"], scale=0.0)
-        else:
+        if last:
             ac(T.leno[:], T.inf[:, n, :], AF.Identity, [fn, "col%d" % C_LEN], ["leno"], scale=col(C_LEN))
-        ac(T.spc[:, 1, :, :], T.spc[:, 0, :, :], AF.Identity, ["spa", "spb", "g84"], ["spc"], bias=T.g8[:, 4 + n:5 + n])
+        ac(T.spc[:, 1, :, :], T.spc[:, 0, :, :], AF.Identity, ["spa", "spb", "g84"], ["spc"], scale=1.0 / FAM, bias=T.g8[:, 4 + n:5 + n])
         op("v", ["pb0", "rm"], ["scn", "r1", "r64"],
            lambda: vec.tensor_tensor_scan(T.scn[:], T.rm[:], pb[0][:, 0:NT], 0.0, ALU.mult, ALU.max))
         key, r64, r1 = T.scn[:, 15::16], T.scn[:, 14::16], T.scn[:, 13::16]
@@ -405,30 +465,28 @@ def rank_program(g, core, T, topo):
         turn(pb[1][:, 128:NT], 8, 1, 3, False, True, 1)
         turn(pb[2][:, 0:128], 0, 0, 0, True, True, 2)
         turn(pb[2][:, 128:NT], 8, 0, 0, True, True, 2)
-        turn(pb[0][:, 0:64], 8, 1, 0, True, True, 0)
-        turn(pb[0][:, 64:NT], 4, 1, 0, True, True, 0)
-        if later:
-            later.pop(0)()
-        cp(T.ll[:, 0:NT], pb[2][:, 0:NT], ["pb2"], ["le"])
+        turn(pb[2][:, NT:256], 8, 1, 0, True, True, 2)
+        turn(pb[0][:, 0:128], 4, 1, 0, True, True, 0)
+        meanwhile()
+        cp(T.ll[:, 0:256], pb[2][:, 0:256], ["pb2"], ["le"])
         ac(T.rb[:, 0:NT], pb[1][:, 0:NT], AF.Copy, ["pb1"], ["rb"])
-        ac(T.ll[:, NT:2 * NT], pb[0][:, 0:NT], AF.Copy, ["pb0"], ["lo"])
-        if later:
-            later.pop(0)()
-        for t in (0, 2, 1, 3, 4, None, 5, 6, 8, 7, 10, 9, 11):
+        ac(T.ll[:, 256:2 * NT], pb[0][:, 0:128], AF.Copy, ["pb0"], ["lo"])
+        meanwhile()
+        for t in (0, 8, 4, 1, 5, 9, None, 6, 2, 7, 10, 3, 11):
             if t is None:
                 ties(*banks[3])
                 continue
             bk, s = place[t]
-            if s:
+            if s and t < 8:
                 need("p", [lastw["pb%d" % bk][0:2] + ("tile",)])
             p0, c0 = 32 * (t % 4), (0, 256, 128)[t // 4]
             mm(pb[bk][:, NU * s:NU * (s + 1)], T.ll[p0:p0 + 32, c0:c0 + 128], T.rb[p0:p0 + 32, 0:NU], False, s == 1,
-               (["le"], ["lo"], ["le", "lo"])[t // 4] + ["rb", "rbx"], ["pb%d" % bk])
+               [("le", "lo", "le")[t // 4], "rb", "rbx"], ["pb%d" % bk])
         conv = pb[1][:, 0:HALF]
-        mm(conv, T.ones[0:1, 0:128], T.cst[0:1, :, :], True, False, ["ones", "cst"], ["pb1"])
+        mm(conv, T.ones[0:1, 0:128], T.cst[0:1, :, :], True, False, ["ones", "cst0", "cst1", "cst2"], ["pb1"])
         for a in range(8):
             for r in (3, 4):
-                mm(pb[1][:, 12 * a:12 * (a + 1)], T.pick[:, a, :], row(r), False, False, ["pick", "dh", "dl"], ["pb1"])
+                mm(pb[1][:, 12 * a:12 * (a + 1)], T.pick[:, a, :], row(r), False, False, PK + ["dh", "dl"], ["pb1"])
 
         def tile(t):
             bk, s = place[t]
@@ -460,40 +518,61 @@ def rank_program(g, core, T, topo):
         sum_scalar(2)
         for t in on_vector[5:]:
             by_vector(t)
+        meanwhile()
         for a in range(8):
             mm(pb[1][:, 12 * a:12 * (a + 1)], T.pick[:, a, :], T.res[:, 0:12], False, a == 7,
-               ["pick"] + ["res%d" % t for t in range(12)], ["pb1"])
+               PK + ["res%d" % t for t in range(12)], ["pb1"])
         tt(T.conv[:], conv, T.spc[:, 1, :, :], ALU.min, ["pb1", "spc"], ["conv"])
         ln = "lst%d" % n
-        ts(T.lst[:, n, :], T.conv[:].indirect(T.gl2[:, 0:1]), float(MID), None, ALU.add, None, ["conv", "gl2"], [ln])
+        ts(T.lst[:, n, :], T.conv[:].indirect(T.gl2[:, 0:1]), FAM, float(MID), ALU.mult, ALU.add, ["conv", "gl2"], [ln])
         lst = T.lst[:, n, 0:12]
         if not last:
-            cp(T.outA[:, n, :], T.aw[:, 0:wn].indirect(lst), ["aw", ln] + AD, ["oa%d" % n])
-            ac(T.outC[:, n, :], T.yw[:, 0:wn].indirect(lst), AF.Copy, Y3 + YD + [ln], ["oc%d" % n])
-            send(["oa%d" % n], lambda h: T.outA[:, n, HALF * h:HALF * (h + 1)],
-                 lambda h: T.alL[:, n + 1, 16 + HALF * h:16 + HALF * (h + 1)], "ra%d" % n, "al%d" % (n + 1))
-            send(["oc%d" % n], lambda h: T.outC[:, n, HALF * h:HALF * (h + 1)],
-                 lambda h: T.cL[:, n + 1, HALF * h:HALF * (h + 1)], "rc%d" % n, "c%d" % (n + 1))
-            tt(T.mst[:], T.xw[:, 0:wn].indirect(lst), cc, ALU.max, X3 + ["xd", ln, cn], ["mst"])
-        tt(T.outI[:, n, :], T.sw[:, 0:wn].indirect(lst), T.leno[:], ALU.add, S6 + SD + [ln, "leno"], ["oi%d" % n])
-        send(["oi%d" % n], lambda h: T.outI[:, n, HALF * h:HALF * (h + 1)],
-             lambda h: T.inf[:, n + 1, HALF * h:HALF * (h + 1)], "ri%d" % n, "inf%d" % (n + 1))
-        if not last:
-            o = pb[2][:, 0:NT]
-            mm(o, T.wf[:, 1, :], T.inf[:, n, :], True, False, ["wf", fn], ["pb2"])
-            mm(o, T.wab[:, 0:128], cc, False, False, ["wab", cn], ["pb2"])
-            mm(o, T.wab[:, 1:129], T.mst[:], False, False, ["wab", "mst"], ["pb2"])
-            mm(o, T.wf[:, 0, :], T.outI[:, n, :], False, True, ["wf", "oi%d" % n], ["pb2"])
-            ac(T.vv[:], o, AF.Identity, ["pb2", "col%d" % C_VB], ["vv"], bias=col(C_VB))
+            s0, s1 = 2 * n + 2, 2 * n + 3
+
+            def take(h):
+                s, lh = s0 + h, T.lst[:, n, 6 * h:6 * (h + 1)]
+                cp(T.oa[:, s, 16:16 + HALF], T.aw[:, 0:wn].indirect(lh), ["aw", ln] + AD, ["oa%d" % s])
+                ac(half(T.outC, n, h), T.yw[:, 0:wn].indirect(lh), AF.Copy, Y3 + YD + [ln], ["oc%d" % s])
+
+            take(1)
+            send(["oc%d" % s1], [(1, half(T.outC, n, 1), T.cL[:, s1, 0:HALF])], ["c%d" % s1])
+            ac(T.raw[:], T.sw[:, 0:wn].indirect(lst), AF.Copy, S6 + SD + [ln], ["raw"])
+            turns(s1)
+            take(0)
+            offsets(s1, T.outO, "oo")
+            send(["oo%d" % s1], [(1, T.outO[:, s1, :], T.off[:, s1, :])], ["off%d" % s1])
+            turns(s0)
+            offsets(s0, T.outO, "oo")
+            send(["oc%d" % s0, "oo%d" % s0], [(0, half(T.outC, n, 0), T.cL[:, s0, 0:HALF]), (0, T.outO[:, s0, :], T.off[:, s0, :])],
+                 ["c%d" % s0, "off%d" % s0])
             if n < NR - 2:
-                cp(T.yw[:, 0:wn].indirect(lst), cc, [cn, ln], Y3 + YD)
+                send(["oa%d" % s0, "oa%d" % s1], [(h, T.oa[:, s0 + h, 16:16 + HALF], half(T.alL, n + 1, h)) for h in range(2)],
+                     ["al%d" % (n + 1)])
+            o = pb[2][:, 0:NT]
+            mm(o, T.wf[:, 1, :], T.inf[:, n, :], True, False, WF8 + [fn], ["pb2"])
+            mm(o, T.wg[:], T.rb[:, 0:NT], False, False, ["wg", "rb"], ["pb2"])
+            mm(o, T.wf[:, 0, :], T.raw[:], False, True, WF8 + ["raw"], ["pb2"])
+            ac(T.vv[:], o, AF.Identity, ["pb2", "col%d" % C_TH], ["vv"], bias=col(C_TH))
+            o = pb[1][:, 0:NT]
+            if n:
+                mm(o, T.wf[:, 2, :], T.inf[:, n, :], True, False, WF8 + [fn], ["pb1"])
+            mm(o, T.wf[:, 3, :], T.raw[:], n == 0, True, WF8 + ["raw"], ["pb1"])
+            ac(T.outI[:, n, :], o, AF.Copy, ["pb1"], ["oi%d" % n])
+
+            def features(h, n=n, wn=wn, YD=YD):
+                cp(T.yw[:, 0:wn].indirect(T.lst[:, n, 6 * h:6 * (h + 1)]), T.cL[:, 2 * n + h, 0:HALF], ["c%d" % (2 * n + h), "lst%d" % n],
+                   Y3 + YD)
+
+            def applicants(h, n=n, wn=wn, AD=AD):
+                cp(T.aw[:, 0:wn].indirect(T.lst[:, n, 6 * h:6 * (h + 1)]), half(T.alL, n, h), ["al%d" % n, "lst%d" % n], ["aw"] + AD)
+
             cp(T.sw[:, 0:wn].indirect(lst), T.vv[:], ["vv", ln], S6 + SD)
             if n < NR - 2:
-                for h in range(2):
-                    later.append(lambda n=n, h=h, wn=wn, AD=AD: cp(
-                        T.aw[:, 0:wn].indirect(T.lst[:, n, 6 * h:6 * (h + 1)]), T.alL[:, n, 16 + HALF * h:16 + HALF * (h + 1)],
-                        ["al%d" % n, "lst%d" % n], ["aw"] + AD))
+                features(0)
+                later += [lambda: None, lambda f=applicants: f(0), lambda f=features: f(1), lambda f=applicants: f(1)]
         else:
+            tt(T.outI[:, n, :], T.sw[:, 0:wn].indirect(lst), T.leno[:], ALU.add, S6 + SD + [ln, "leno"], ["oi%d" % n])
+            send_ids(n)
             cp(T.sw[:, 0:wn].indirect(lst), T.inf[:, n, :], [fn, ln], S6 + SD)
 
     fn = "inf%d" % NR

@@ -9,20 +9,20 @@ F, B, I, U = "float32", "bfloat16", "int32", "uint16"
 SCRATCH = {}
 for _dt, _bufs in (
     (F, dict(sw=[W], inf=[NR + 1, NT], outI=[NR, NT], raw=[NT], scn=[NT], rm=[NT], sg2=[8],
-             leno=[NT], vv=[NT], pf=[12], j16=[NR], g1=[6], g3=[6], g6=[6], g7=[6], g8=[8], gcol=[128], gnat=[8], thf=[4], tq=[3, 8],
-             cols=[4], wf=[4, 128], conv=[HALF], spc=[2, 8, 12])),
+             leno=[NT], vv=[NT], pf=[12], j16=[NR], g1=[6], g3=[6], g6=[6], g7=[6], g8=[24], gcol=[128], gnat=[8], thf=[4], rown=[8], tcol=[2],
+             cols=[4], wf0=[128], wf1=[128], wf2=[128], wf3=[128], conv=[HALF], spc=[2, HALF])),
     (B, dict(xw=[V], yw=[W], mx=[V], sg=[V], cL=[2 * NR, 4 * HALF], outC=[NR - 1, NT], dd=[416], rb=[NU + 7], ll=[2 * NT],
              junk=[2, NU + 7], crow=[512], wc=[6, 128], wab=[144], wg=[128], wm=[8], ws=[8], wsc=[8, 16], ones=[256], kc=[NT],
-             m8=[8, 16], th8=[8, 16], idb=[128], res=[16], tri=[3, NU], pick=[8, 128], cst=[8, 12])),
-    (I, dict(aw=[W], alL=[NR, NT], oa=[2 * NR, 128], tt=[2, 224], gi=[12], pidx=[4], pi3=[8], g2=[6], thi=[4], thc=[4])),
-    (U, dict(off=[2 * NR, HALF], outO=[2 * NR, HALF], lst=[NR, 16], gl=[6], gl2=[2])),
+             m8=[8, 16], th8=[8, 16], idb=[128], res=[16], tri=[4, NU], trow=[NU + 7], pick=[8, 128], cst=[128])),
+    (I, dict(aw=[W], alL=[NR, NT], ia=[224], oa=[2 * NR, 128], tt=[2, 224], gi=[12], pidx=[4], pi3=[8], g2=[6], thi=[4], thc=[4])),
+    (U, dict(off=[2 * NR, HALF], outO=[2 * NR, HALF], lst=[NR, 24], gl=[6], gl2=[4])),
 ):
     for _k, _s in _bufs.items():
         SCRATCH[_k] = ("sbuf", [128] + _s, _dt)
 for _b in range(8):
     SCRATCH["pb%d" % _b] = ("psum", [128, 512], F)
 
-SEMAPHORES = (["cv", "ca", "cp", "cg", "sent"] + ["d%d" % _i for _i in range(24)] + ["r%d" % _i for _i in range(20)])
+SEMAPHORES = (["cv", "ca", "cp", "cg", "sent"] + ["d%d" % _i for _i in range(28)] + ["r%d" % _i for _i in range(24)])
 
 GS = 16.0
 FAM = 4096.0
@@ -32,8 +32,8 @@ WF = 1024.0 * FAM
 ROUND_1, ROUND_64 = 1.5 * 2.0 ** 23, 1.5 * 2.0 ** 17
 D0 = 16
 R_A, R_B, R_HI, R_LO, R_ID, R_LEN = 0, 1, 2, 3, 4, 5
-C_VB, C_ID, C_LEN, C_TH = range(4)
-P_G, P_H, P_M, P_8, P_Q, P_1, P_S1, P_S2, P_16 = range(9)
+C_ID, C_LEN, C_TH = range(3)
+P_G, P_H, P_1, P_M, P_Q, P_2, P_S1, P_S2, P_16 = range(9)
 
 
 def rank_program(g, core, T, topo):
@@ -42,6 +42,13 @@ def rank_program(g, core, T, topo):
         return
     n_ranks = len(T.cores)
     nxt, prv = T.cores[(rank + 1) % n_ranks], T.cores[(rank - 1) % n_ranks]
+
+    def swapped(r):
+        return int(topo.mates(topo.chip(T.cores[r % n_ranks]), topo.chip(T.cores[(r - 1) % n_ranks])))
+
+    flip = swapped(rank)
+    there = [h ^ flip ^ swapped(rank + (1, -1)[h ^ flip]) for h in range(2)]
+    assert there == [1, 0]
     queues = {"v": g.vector, "a": g.scalar, "p": g.tensor, "g": g, "s": g.sync}
     csem = {"v": "cv", "a": "ca", "p": "cp", "g": "cg"}
     count = {}
@@ -103,7 +110,7 @@ def rank_program(g, core, T, topo):
         trs = []
         count[sem] = 0
         for j, (h, src, dst) in enumerate(moves):
-            to, frm = (nxt, prv)[h], (prv, nxt)[h]
+            to, frm = (nxt, prv)[h ^ flip], (prv, nxt)[there[h] ^ flip]
             eng = topo.engines(core, to)
             eng = eng[j * len(eng) // len(moves):(j + 1) * len(eng) // len(moves)]
             rid, pid = topo.addr(to)[0:2]
@@ -167,74 +174,80 @@ def rank_program(g, core, T, topo):
     def spare(n):
         return slice(V + NT * n, V + NT * (n + 1))
 
-    mset(T.thc[:], 0, ["thc"])
-    dma("s", [], ["oa0", "oa1"], T.oa[:, 0:2, 16:16 + HALF], T.va[:])
     for j, (a, b) in enumerate(((0, 1024), (1024, 2048), (2048, 2816), (2816, V))):
         dma("a", [], [Y3[j]], T.yw[:, a:b], T.hx[:, a:b])
         dma("s", [], [X3[j]], T.xw[:, a:b], T.fx[:, a:b])
         if j == 0:
-            dma("a", [], ["c0", "c1"], T.cL[:, 0:2, 0:HALF], T.vx[:])
+            dma("s", [], ["ia"], T.ia[:, 16:16 + NT], T.va[:])
             dma("s", [], ["thi"], T.thi[0:8, 0:1], T.th[:, 0])
-    dma("s", [Y3[3], X3[3]], ["aw"], T.aw[:, 0:V], T.ha[:])
-    dma("s", [], ["ad0"], T.aw[:, spare(0)], T.va[:])
-    dma("s", [], ["yd0"], T.yw[:, spare(0)], T.vx[:])
-    dma("s", [], ["al0"], T.alL[:, 0, :], T.va[:])
-    dma("s", [], ["thc"], T.thc[R_B::16, 0:1], T.th[:, 0])
+        if j in (1, 3):
+            h = int(j == 1)
+            dma("a", [], ["c%d" % h], T.cL[:, h, 0:HALF], T.vx[:, HALF * (h ^ flip):HALF * ((h ^ flip) + 1)])
 
-    iota(T.pidx[:, 0:1], [[0, 1]], 0, 1, ["pidx"], flag=False)
-    mset(T.ones[:], 1.0, ["ones"])
-    mset(T.crow[0:64, :], 0.0, ["crow"])
-    mset(T.wc[0:96, :, :], 0.0, ["wc"])
-    CR = ["cr%d" % j for j in range(10)]
+    CR = ["cr%d" % j for j in range(9)]
     WCK = ["wa%d" % j for j in range(8)]
-    for k in CR:
-        lastw[k] = lastw["crow"]
-    for k in WCK:
-        lastw[k] = lastw["wc"]
+    mset(T.crow[0:65, :], 1.0, CR)
+    iota(T.pidx[:, 0:1], [[0, 1]], 0, 1, ["pidx"], flag=False)
     iota(T.gnat[:], [[1, 8]], 0, 0, ["gnat"])
+    iota(T.crow[32:33, 0:64], [[1, 64]], 0, 0, [CR[8], "pool"])
+    for j in range(8):
+        ac(T.crow[0:1, 64 * j:64 * (j + 1)], T.crow[0:1, 64 * j:64 * (j + 1)], AF.Identity, [CR[j]], [CR[j]], scale=float(j))
+    mset(T.ones[:], 1.0, ["ones"])
+    mset(T.wc[0:65, :, :], 0.0, WCK)
     sel(T.idb[:], T.ones[:, 0:128], [[-1, 128]], ALU.is_equal, 0.0, 0, 1, ["ones"], ["idb"])
-    iota(T.crow[32:33, 0:64], [[1, 64]], 0, 0, [CR[0], "pool"])
     iota(T.wc[64:65, :, R_HI::16], [[8, 6], [0, 8]], -MID // 64, 0, [WCK[6], "pool"])
     iota(T.wc[64:65, :, R_ID::16], [[512, 6], [0, 8]], V * rank, 0, [WCK[7], "pool"])
     iota(T.g1[:], [[256, 6]], 0, 16, ["g1"])
     iota(T.gcol[:], [[1, 2], [2, 4], [0, 16]], 0, 0, ["gcol"])
     iota(T.j16[:], [[NT, NR]], 0, 0, ["j16"])
-    for j in range(1, 8):
-        aset(T.crow[0:1, 64 * j:64 * (j + 1)], T.ones[0:1, 0:64], float(j), [CR[j]])
-        if j in (3, 5, 7):
-            w = 64 << (j // 2 - 1)
-            ac(T.crow[32:33, w:2 * w], T.crow[32:33, 0:w], AF.Copy, [CR[0]], [CR[0]])
-    mset(T.crow[64:65, :], 1.0, [CR[8]])
     for j, (p, r, val) in enumerate(((0, R_HI, 1.0), (0, R_ID, 64.0), (32, R_LO, 1.0), (32, R_ID, 1.0), (64, R_A, -120.0), (64, R_LEN, 1.0))):
+        if j % 2 == 0:
+            w = 64 << (j // 2)
+            cp(T.crow[32:33, w:2 * w], T.crow[32:33, 0:w], [CR[8]], [CR[8]])
         mset(T.wc[p:p + 1, :, r::16], val, [WCK[j]])
-    ts(T.pi3[:, P_G:P_G + 1], T.pidx[:, 0:1], 4, None, ALU.arith_shift_right, None, ["pidx"], ["pi0"])
-    ts(T.pi3[:, P_H:P_H + 1], T.pidx[:, 0:1], 4, 1, ALU.arith_shift_right, ALU.bitwise_and, ["pidx"], ["pi1"])
-    ts(T.pi3[:, P_M:P_M + 1], T.pidx[:, 0:1], 15, None, ALU.bitwise_and, None, ["pidx"], ["pi2"])
-    ts(T.pi3[:, P_8:P_8 + 1], T.pidx[:, 0:1], 3, 1, ALU.arith_shift_right, ALU.bitwise_and, ["pidx"], ["pi3"])
-    ts(T.pi3[:, P_Q:P_Q + 1], T.pidx[:, 0:1], 5, None, ALU.arith_shift_right, None, ["pidx"], ["pi4"])
-    ts(T.pi3[:, P_1:P_1 + 1], T.pidx[:, 0:1], 1, None, ALU.bitwise_and, None, ["pidx"], ["pi5"])
-    mset(T.wab[:], 0.0, ["wab"])
-    cp(T.pf[:, 0:6], T.pi3[:, 0:6], ["pi%d" % j for j in range(6)], ["pf"])
-    mset(T.oa[:, :, 0:16], 0, ["pad0"])
-    mset(T.oa[:, :, 16 + HALF:128], 0, ["pad1"])
-    aset(T.ws[:], T.ones[:, 0:8], 0.0, ["ws"])
-    aset(T.tq[:], T.ones[:, 0:24], 0.0, ["tq"])
-    ts(T.wab[:, 1:129:16], T.gnat[:], pc(P_G), None, ALU.is_equal, None, ["gnat", "pf"], ["wab"])
-    ts(pc(P_S1), pc(P_G), -256.0, -40.0, ALU.mult, ALU.add, ["pf"], ["pf1"])
-    ts(pc(P_S2), pc(P_1), pc(P_H), 112.0, ALU.not_equal, ALU.mult, ["pf"], ["pf2"])
-    ts(T.wm[:], T.gcol[:, 0::16], pc(P_G), -2.0 * GS, ALU.is_equal, ALU.mult, ["gcol", "pf"], ["wm"])
-    ts(T.g2[:], T.g1[:], pc(P_S1), 1.0 / HALF, ALU.add, ALU.mult, ["g1", "pf1"], ["g2"])
-    ts(T.g7[:], T.g1[:], pc(P_S1), pc(P_S2), ALU.add, ALU.add, ["g1", "pf1", "pf2"], ["g7"])
-    ts(T.wsc[:], T.gcol[:], pc(P_G), GS, ALU.is_equal, ALU.mult, ["gcol", "pf"], ["wsc"])
-    ts(T.g3[:], T.g2[:], 1.0 - HALF, 40.0, ALU.mult, ALU.add, ["g2"], ["g3"])
-    ts(pc(P_16), pc(P_G), -16.0, None, ALU.mult, None, ["pf"], ["pf16"])
-    tt(T.g6[:], T.g7[:], T.g3[:], ALU.add, ["g7", "g3"], ["g6"])
-    cp(T.gl[:], T.g6[:], ["g6"], ["gl"])
 
-    def turns(s):
+    def bits(j, shift, mask):
+        ts(T.pi3[:, j:j + 1], T.pidx[:, 0:1], shift, mask, ALU.arith_shift_right, ALU.bitwise_and, ["pidx"], ["pi%d" % j])
+
+    bits(P_G, 4, 7)
+    bits(P_H, 4, 1)
+    bits(P_1, 0, 1)
+    mset(T.wab[:], 0.0, ["wab"])
+    cp(T.pf[:, 0:3], T.pi3[:, 0:3], ["pi0", "pi1", "pi2"], ["pf"])
+    mset(T.thc[:], 0, ["thc"])
+    ts(T.wab[:, 1:129:16], T.gnat[:], pc(P_G), None, ALU.is_equal, None, ["gnat", "pf"], ["wab"])
+    aset(T.ws[:], T.ones[:, 0:8], 0.0, ["ws"])
+    dma("s", [Y3[3], X3[3]], ["aw"], T.aw[:, 0:V], T.ha[:])
+    for a, b in ((0, HALF), (HALF, NT)) if flip else ((0, NT),):
+        a2 = (a + HALF * flip) % NT
+        dma("s", [], ["ad0" + "b" * (a > 0)], T.aw[:, V + a:V + b], T.va[:, a2:a2 + b - a])
+        dma("s", [], ["yd0" + "b" * (a > 0)], T.yw[:, V + a:V + b], T.vx[:, a2:a2 + b - a])
+    dma("s", [], ["thc"], T.thc[R_B::16, 0:1], T.th[:, 0])
+    dma("s", ["ad0", "ad0b"], ["al0"], T.alL[:, 0, :], T.aw[:, spare(0)])
+
+    def turn_list():
+        ts(pc(P_S1), pc(P_G), -256.0, -40.0, ALU.mult, ALU.add, ["pf"], ["pf1"])
+        ts(pc(P_S2), pc(P_1), pc(P_H), 112.0, ALU.not_equal, ALU.mult, ["pf"], ["pf2"])
+        mset(T.ia[:, 0:16], 0, ["ipad0"])
+        ts(T.g2[:], T.g1[:], pc(P_S1), 1.0 / HALF, ALU.add, ALU.mult, ["g1", "pf1"], ["g2"])
+        ts(T.g7[:], T.g1[:], pc(P_S1), pc(P_S2), ALU.add, ALU.add, ["g1", "pf1", "pf2"], ["g7"])
+        mset(T.ia[:, 16 + NT:224], 0, ["ipad1"])
+        ts(T.g3[:], T.g2[:], 1.0 - HALF, 40.0, ALU.mult, ALU.add, ["g2"], ["g3"])
+        ts(T.wm[:], T.gcol[:, 0::16], pc(P_G), -2.0 * GS, ALU.is_equal, ALU.mult, ["gcol", "pf"], ["wm"])
+        tt(T.g6[:], T.g7[:], T.g3[:], ALU.add, ["g7", "g3"], ["g6"])
+        cp(T.gl[:], T.g6[:], ["g6"], ["gl"])
+
+    def turns(s, which=(0, 1)):
         h = s % 2
-        op("v", ["oa%d" % s], ["tt%da" % h], lambda: vec.transpose(T.tt[:, h, 0:HALF], T.oa[:, s, 16:16 + HALF]))
-        op("v", ["oa%d" % s, "pad0", "pad1"], ["tt%db" % h], lambda: vec.transpose(T.tt[:, h, HALF:224], T.oa[:, s, :]))
+        if s < 2:
+            c0 = HALF * (h ^ flip)
+            one, two, rd = T.ia[:, c0 + 16:c0 + 16 + HALF], T.ia[:, c0:c0 + 128], ["ia", "ipad0", "ipad1"]
+        else:
+            one, two, rd = T.oa[:, s, 16:16 + HALF], T.oa[:, s, :], ["oa%d" % s, "pad0", "pad1"]
+        if 0 in which:
+            op("v", rd, ["tt%db" % h], lambda: vec.transpose(T.tt[:, h, HALF:224], two))
+        if 1 in which:
+            op("v", rd[0:1], ["tt%da" % h], lambda: vec.transpose(T.tt[:, h, 0:HALF], one))
 
     def offsets(s, out, key):
         cp(out[:, s, :], T.tt[:, s % 2, :].indirect(T.gl[:]), ["tt%da" % (s % 2), "tt%db" % (s % 2), "gl"], [key + str(s)])
@@ -250,48 +263,56 @@ def rank_program(g, core, T, topo):
         a, b = pieces[j]
         mm(pb[j % 6][:, 0:b - a], T.wc[0:65, a // 512, :], T.crow[0:65, a % 512:a % 512 + b - a], True, False, CR + WCK, ["pb%d" % (j % 6)])
 
-    for j in range(6):
+    for j in range(3):
         numbers(j)
 
     iota(T.kc[0:1, :], [[0, 12], [-1, 16]], 7, 0, ["kc"])
     sel(T.m8[0:8, :, :], T.ones[0:8, 0:128], [[-1, 2], [-2, 4], [0, 16]], ALU.is_equal, 0.0, 0, 1, ["ones"], ["m8"])
-    for j in range(3):
-        lastw["tq%d" % j] = lastw["tq"]
-    for (r, val), (j, r2, val2) in zip(((R_A, 2.0 * GS), (R_B, -GS), (R_HI, 64.0 / FAM), (R_LO, 1.0 / FAM)),
-                                       ((0, R_LEN, 1.0), (1, R_ID, 1.0), (2, R_LEN, 1.0), (None, None, None))):
+    between = [
+        lambda: iota(T.trow[:, 0:NT], [[HALF - NT * flip, 2], [1, HALF]], HALF * flip, 0, ["trow"]),
+        lambda: iota(T.tcol[:, 0:2], [[128 - NT * flip, 2]], HALF * flip, 1, ["tcol"]),
+        lambda: iota(T.trow[:, NT:NU], [[0, 1]], -1, 0, ["trox"]),
+        lambda: iota(T.rown[:], [[-16, 8]], 0, 1, ["rown"]),
+    ]
+    for j, (r, val) in enumerate(((R_A, 2.0 * GS), (R_B, -GS), (R_HI, 64.0 / FAM), (R_LO, 1.0 / FAM))):
         sel(T.ws[:], T.ws[:], [[-16, 2], [-32, 4]], ALU.not_equal, val, -r, 1, ["ws"], ["ws"])
-        if j is not None:
-            sel(T.tq[:, j, :], T.tq[:, j, :], [[-16, 8]], ALU.not_equal, val2, -r2, 1, ["tq%d" % j], ["tq%d" % j])
+        between[j]()
+    iota(T.tcol[64:128, 1:2], [[0, 1]], 128 - HALF * flip, 1, ["tcol", "pool"])
+    iota(T.tcol[HALF:128, 0:1], [[0, 1]], HALF - HALF * flip, 1, ["tcol", "pool"])
     copies(1, "g")
+    iota(T.inf[:, 0, :], [[HALF - NT * flip, 2], [1, HALF]], n_ranks * V + NT * rank + HALF * flip, 0, ["inf0"])
     copies(0, "g")
-    iota(T.tri[:], [[0, 3 * NU]], 1 - int(WIN), 0, ["tri", "tr0", "tr64"])
-    iota(T.inf[:, 0, :], [[1, NT]], n_ranks * V + NT * rank, 0, ["inf0"])
-    sel(T.tri[:, 0:2, 0:NT], T.tri[:, 0:2, 0:NT], [[0, 2], [-1, NT]], ALU.is_gt, -WIN, 0, 1, ["tri"], ["tri"])
-    for p in (0, 64):
-        sel(T.tri[p:p + 64, 2, 128:NT], T.tri[p:p + 64, 2, 128:NT], [[-1, 64]], ALU.is_gt, -WIN, 0, 1, ["tr%d" % p], ["tr%d" % p] + ["pool"] * (p > 0))
-    iota(T.spc[:, 0, :, 0:8], [[16, 8], [0, 8]], V - MID, 1, ["spa"])
-    iota(T.spc[:, 0, :, 8:12], [[0, 2], [16, 4], [0, 4]], V - MID + 128, 1, ["spb"])
-    PK = ["pick%d" % a for a in range(4)]
-    for a in range(4):
-        sel(T.pick[:, 2 * a:2 * a + 2, :], T.ones[:], [[-16, 2], [0, 8], [-1, 16]], ALU.is_equal, 0.0, -32 * a, 1, ["ones"], [PK[a]])
-    WF8 = ["wf%d" % j for j in range(8)]
-    iota(T.wf[:], [[0, 512]], 0, 0, WF8)
-    iota(T.wg[:], [[0, 128]], 0, 0, ["wg"])
-    for i, (j, r, r2, val) in enumerate(((0, R_HI, R_HI, 1.0), (0, R_LO, R_LO, 1.0), (0, R_A, R_B, -2.0), (1, R_ID, R_ID, 1.0),
-                                         (2, R_LEN, R_LEN, 1.0), (3, R_ID, R_ID, 1.0), (3, R_LEN, R_LEN, 1.0), (0, R_B, R_B, 1.0))):
-        k = WF8[2 if i == 7 else i]
-        sel(T.wf[:, j, r2::16], T.wf[:, j, r2::16], [[-16, 8]], ALU.not_equal, val, -r, 1, [k], [k])
-    sel(T.wg[:, R_B::16], T.wg[:, R_B::16], [[-16, 8]], ALU.not_equal, 1.0, -2, 1, ["wg"], ["wg"])
+    iota(T.spc[:, 0, 0:64], [[16, 8], [0, 8]], V - MID, 1, ["spa"])
+    iota(T.spc[:, 0, 64:HALF], [[0, 2], [16, 4], [0, 4]], V - MID + 128, 1, ["spb"])
+    WF8 = ["wf%d" % j for j in range(7)]
+    TRI = ["tri%d" % j for j in range(4)]
+    PK = ["pick"]
 
-    def row(r):
-        return T.dd[:, D0 + r:D0 + 32 * 12:32]
+    def tie_tables():
+        for j in range(4):
+            ts(T.tri[:, j, :], T.trow[:, 0:NU], T.tcol[:, j // 2:j // 2 + 1], -WIN, ALU.is_lt, ALU.add, ["trow", "trox", "tcol"], [TRI[j]])
 
-    on_scalar = (4, 5, 7)
+    def pick_tables(j):
+        if j == 0:
+            ac(T.pick[:, :, 0:16], T.idb[:], AF.Copy, ["idb"], PK)
+        else:
+            w = 8 << j
+            ac(T.pick[:, :, w:2 * w], T.pick[:, :, 0:w], AF.Copy, PK, PK)
+
+    def row(r, t0=0, t1=12):
+        return T.dd[:, D0 + r + 32 * t0:D0 + 32 * t1:32]
+
+    on_scalar = (3, 7, 10)
+    CST = ["cst%d" % j for j in range(3)]
     DW = ["dw%d" % j for j in range(6)]
+    pick_tables(0)
     aset(T.dd[:, 0:208], T.ones[:, 0:208], 0.0, ["dd0"])
+    pick_tables(1)
     aset(T.dd[:, 208:416], T.ones[:, 0:208], 0.0, ["dd1"])
+    pick_tables(2)
     aset(T.rm[:], T.ones[:, 0:NT], 1.0, ["rm"])
-    aset(T.cst[0:1, :, :], T.ones[0:1, 0:HALF], WIN, ["cst"])
+    aset(T.cst[0:1, :], T.ones[0:1, 0:128], WIN, ["cst"])
+    pick_tables(3)
     for k in DW + ["dh", "dl", "dg"]:
         lastw[k] = lastw["dd1"]
     for j, (r, val) in enumerate(((0, WF), (1, WF), (2, 2.0), (6, -WF), (7, -WF), (8, -2.0))):
@@ -299,17 +320,28 @@ def rank_program(g, core, T, topo):
     aset(T.rm[:, 0::16], T.ones[:, 0:12], 0.0, ["rm"])
     for j, t in enumerate(on_scalar):
         lastw["cst%d" % j] = lastw["cst"]
-        aset(T.cst[0:1, :, t], T.ones[0:1, 0:8], 0.0, ["cst%d" % j])
+        aset(T.cst[0:1, t:64:8] if t < 8 else T.cst[0:1, 56 + t:HALF:4], T.ones[0:1, 0:8], 0.0, [CST[j]])
 
-    turns(1)
-    turns(0)
-    offsets(1, T.off, "off")
-    offsets(0, T.off, "off")
-    fill = [
-        lambda: ts(T.thf[0:8, 0:1], T.thi[0:8, 0:1], -GS, 240.0 * GS, ALU.mult, ALU.add, ["thi"], ["thf"]),
-        lambda: ts(T.g8[:, 4:8], T.j16[:], pc(P_16), 1.0 / FAM, ALU.add, ALU.mult, ["j16", "pf16"], ["g84"]),
-        lambda: ts(T.th8[0:8, :, :], T.m8[0:8, :, :], T.thf[0:8, 0:1], None, ALU.mult, None, ["m8", "thf"], ["th8"]),
-    ]
+    def key_weights():
+        ts(T.thf[0:8, 0:1], T.thi[0:8, 0:1], -GS, 240.0 * GS, ALU.mult, ALU.add, ["thi"], ["thf"])
+        ts(T.wsc[:], T.gcol[:], pc(P_G), GS, ALU.is_equal, ALU.mult, ["gcol", "pf"], ["wsc"])
+        ts(T.th8[0:8, :, :], T.m8[0:8, :, :], T.thf[0:8, 0:1], None, ALU.mult, None, ["m8", "thf"], ["th8"])
+
+    def first_lists():
+        turns(1)
+        turns(0)
+        offsets(1, T.off, "off")
+        offsets(0, T.off, "off")
+
+    def late_0():
+        bits(P_M, 0, 15)
+        bits(P_Q, 5, 3)
+        ts(pc(P_16), pc(P_G), -16.0, None, ALU.mult, None, ["pf"], ["pf16"])
+        ts(T.g8[:, 2:3], pc(P_H), 12.0, 8.0, ALU.mult, ALU.add, ["pf"], ["g82"])
+        cp(T.pf[:, 3:5], T.pi3[:, 3:5], ["pi3", "pi4"], ["pfb"])
+
+    turn_list()
+    fill = [late_0, first_lists, key_weights, tie_tables]
 
     def ycopy(j):
         a, b = pieces[j]
@@ -321,59 +353,86 @@ def rank_program(g, core, T, topo):
         o, bk = pb[j % 6][:, 0:b - a], "pb%d" % (j % 6)
         tt(T.mx[:, a:b], T.xw[:, a:b], pb[6 + j % 2][:, 0:b - a], ALU.max, [X3[part[j]], "pb%d" % (6 + j % 2)], ["im%d" % j])
         mm(o, T.wab[:, 0:128], T.yw[:, a:b], False, False, ["wab", Y3[part[j]]], [bk])
-        if j in (1, 3, 4, 5):
-            ycopy(j + 1)
+        if j < 3:
+            numbers(j + 3)
         mm(o, T.wab[:, 1:129], T.mx[:, a:b], False, True, ["wab", "im%d" % j], [bk])
         for k in MX[a // HALF:(b - 1) // HALF + 1]:
             readers.setdefault(k, []).append(lastw[bk])
-        if j == 1:
+        if j + 2 < len(pieces):
             ycopy(j + 2)
         ac(T.sw[:, a:b], o, AF.Copy, [bk], [S6[j]])
-        if j == 1:
+        if j == 3:
             numbers(6)
         if j < len(fill):
             fill[j]()
 
-    def late_constants():
-        for c in (C_VB, C_ID, C_LEN):
-            op("v", ["tq%d" % c], ["col%d" % c], lambda c=c: vec.tensor_reduce(col(c), T.tq[:, c, :], AX.X, ALU.add))
-        ts(T.rb[:, NT:NU], pc(P_M), 5.0, -2.0, ALU.is_equal, ALU.mult, ["pf"], ["rbx"])
-        ts(col(C_TH), T.thc[:, 0:1], col(C_VB), None, ALU.add, None, ["thc", "col%d" % C_VB], ["col%d" % C_TH])
+    def column(c, r):
+        ts(col(c), pc(P_M), float(r), None, ALU.is_equal, None, ["pfb"], ["col%d" % c])
 
-    def conv_list():
-        ts(T.g8[:, 1:2], pc(P_H), 4.0, pc(P_Q), ALU.mult, ALU.add, ["pf"], ["g81"])
-        ts(T.g8[:, 2:3], pc(P_H), 44.0, -88.0, ALU.mult, ALU.add, ["pf"], ["g82"])
-        ts(T.g8[:, 0:1], pc(P_M), 12.0, T.g8[:, 1:2], ALU.mult, ALU.add, ["g81", "pf"], ["g80"])
-        ts(T.g8[:, 3:4], T.g8[:, 2:3], pc(P_8), T.g8[:, 0:1], ALU.mult, ALU.add, ["g82", "g80", "pf"], ["g83"])
-        ts(T.gl2[:, 0:1], T.g8[:, 3:4], HALF - 1.0, None, ALU.min, None, ["g83"], ["gl2"])
+    def passes(key, out, r, r2, val):
+        ts(out[:, r2::16], T.rown[:], float(r), val, ALU.is_equal, ALU.mult, ["rown", "wf"], [key])
 
-    chunks = ((0, 2), (2, 6), (6, 10), (10, 14), (14, 16), (16, 20), (20, 24), (24, 28), (28, 30), (30, 31), (31, 32))
-    achunks = ((0, 8), (8, 16), (16, 24), (24, 28), (28, 30), (30, 31), (31, 32))
-    banks = ((3, (0, 8)), (4, (4, 5)), (5, (1, 9)), (0, (6, 7)), (6, (2, 10)), (7, (3, 11)))
+    def late_1():
+        column(C_ID, R_ID)
+        column(C_LEN, R_LEN)
+        ts(T.g8[:, 4:8], T.j16[:], pc(P_16), 1.0 / FAM, ALU.add, ALU.mult, ["j16", "pf16"], ["g84"])
+        ts(T.rb[:, NT:NU], pc(P_M), 5.0, -2.0, ALU.is_equal, ALU.mult, ["pfb"], ["rbx"])
+
+    def late_2():
+        ts(T.g8[:, 1:2], pc(P_H), 4.0, pc(P_Q), ALU.mult, ALU.add, ["pf", "pfb"], ["g81"])
+        ts(T.g8[:, 8:16], T.rown[:], float(R_A), -2.0, ALU.is_equal, ALU.mult, ["rown"], ["g88"])
+
+    def late_3():
+        ts(T.g8[:, 0:1], pc(P_M), 8.0, T.g8[:, 1:2], ALU.mult, ALU.add, ["g81", "pfb"], ["g80"])
+        ts(T.g8[:, 3:4], pc(P_M), -4.0, T.g8[:, 2:3], ALU.mult, ALU.add, ["g82", "pfb"], ["g83"])
+        ts(pc(P_2), pc(P_M), 2.0, None, ALU.is_ge, None, ["pfb"], ["pf2up"])
+        ts(T.g8[:, 16:24], T.rown[:], float(R_B), None, ALU.is_equal, None, ["rown"], ["g89"])
+        mset(T.oa[:, 2:, 0:16], 0, ["pad0"])
+        ts(T.gl2[:, 0:1], T.g8[:, 0:1], 63.0, None, ALU.min, None, ["g80"], ["gl2"])
+        ts(T.g8[:, 2:3], T.g8[:, 3:4], pc(P_2), T.g8[:, 0:1], ALU.mult, ALU.add, ["g83", "g80", "pf2up"], ["g82"])
+        mset(T.oa[:, 2:, 16 + HALF:128], 0, ["pad1"])
+
+    def late_4():
+        for j, (w, r) in enumerate(((0, R_HI), (0, R_LO), (1, R_ID), (2, R_LEN))):
+            passes(WF8[j], WFV[w], r, r, 1.0)
+        ts(T.gl2[:, 2:3], T.g8[:, 2:3], 48.0, HALF - 1.0, ALU.add, ALU.min, ["g82"], ["gl2b"])
+        passes("wg", T.wg, 2, R_B, 1.0)
+        tt(WFV[0][:, R_B::16], T.g8[:, 8:16], T.g8[:, 16:24], ALU.add, ["g88", "g89", "wf"], [WF8[6]])
+
+    def late_5():
+        passes(WF8[4], WFV[3], R_ID, R_ID, 1.0)
+        passes(WF8[5], WFV[3], R_LEN, R_LEN, 1.0)
+
+    def late_6():
+        ts(col(C_TH), T.thc[:, 0:1], col(C_LEN), None, ALU.add, None, ["thc", "col%d" % C_LEN], ["col%d" % C_TH])
+
+    WFV = [T["wf%d" % j] for j in range(4)]
+
+    chunks = ((0, 2), (2, 6), (6, 10), (10, 14), (14, 16), (16, 20), (20, 24), (24, 28), (28, 30), (30, 32))
+    banks = ((4, (3, 7)), (6, (2, 6)), (7, (8, 9)), (3, (0, 4)), (5, (1, 5)), (0, (10, 11)))
     place = {t: (bk, s) for bk, two in banks for s, t in enumerate(two)}
-    on_vector = (0, 8, 1, 9, 6, 2, 10, 3, 11)
 
     def ties(bk, two):
-        j = 0 if two[1] < 8 else 1
-        mm(pb[bk][:, 0:2 * NU], T.idb[:], T.tri[:, j:j + 2, :], True, False, ["idb", "tri", "tr0", "tr64"], ["pb%d" % bk])
+        j = 0 if two[1] < 8 else 2
+        mm(pb[bk][:, 0:2 * NU], T.idb[:], T.tri[:, j:j + 2, :], True, False, ["idb"] + TRI, ["pb%d" % bk])
 
     def keyed(h, data, wts, k, last, rd):
         def cols(a, b):
             return slice(a, b) if k is None else slice(a + k, b, 16)
         if h:
-            mm(pb[0][0:64, cols(128, NT)], data(32, HALF), wts(0, 4), False, False, rd, ["pb0"])
-            mm(pb[0][64:128, cols(128, NT)], data(32, HALF), wts(4, 8), False, False, rd, ["pb0"])
+            mm(pb[1][0:64, cols(0, 64)], data(32, HALF), wts(0, 4), False, last, rd, ["pb1"])
+            mm(pb[1][64:128, cols(0, 64)], data(32, HALF), wts(4, 8), False, last, rd, ["pb1"])
             mm(pb[0][HALF:128, cols(0, 128)], data(0, 32), wts(0, 8), False, last, rd, ["pb0"])
         else:
             mm(pb[0][0:HALF, cols(0, 128)], data(0, HALF), wts(0, 8), False, last, rd, ["pb0"])
 
-    later = [late_constants, conv_list]
+    later = [late_1, late_2, late_3, late_4, late_5, late_6]
 
     def half(t, n, h):
         return t[:, n, HALF * h:HALF * (h + 1)]
 
     def send_ids(n):
-        send(["oi%d" % n], [(h, half(T.outI, n, h), half(T.inf, n + 1, h)) for h in range(2)], ["inf%d" % (n + 1)])
+        send(["ids"], [(h, half(T.outI, n, h), half(T.inf, n + 1, there[h])) for h in range(2)], ["inf%d" % (n + 1)])
 
     def meanwhile():
         if later:
@@ -383,21 +442,22 @@ def rank_program(g, core, T, topo):
         last = n == NR - 1
         an, fn = "al%d" % n, "inf%d" % n
         wn = V + NT * (n + 1)
-        AD, YD, SD = (["%s%d" % (s, j) for j in range(n + 1)] for s in ("ad", "yd", "sd"))
+        AD, YD, SD = (["%s%d" % (s, j) for j in range(n + 1)] + [s + "0b"] for s in ("ad", "yd", "sd"))
         if n > 0:
             copies(2 * n + 1, "a")
             copies(2 * n, "g")
-            send_ids(n - 1)
             if not last:
                 dma("s", ["c%d" % (2 * n), "c%d" % (2 * n + 1)], ["yd%d" % n], T.yw[:, spare(n)], T.cL[:, 2 * n:2 * n + 2, 0:HALF])
                 dma("s", [an], ["ad%d" % n], T.aw[:, spare(n)], T.alL[:, n, :])
             for bk, two in banks:
                 if bk:
                     ties(bk, two)
-        mm(pb[0][:, 0:NT], T.ones[0:1, 0:128], T.kc[0:1, :], True, False, ["ones", "kc"], ["pb0"])
+        mm(pb[0][:, 0:128], T.ones[0:1, 0:128], T.kc[0:1, 0:128], True, False, ["ones", "kc"], ["pb0"])
+        mm(pb[1][:, 0:64], T.ones[0:1, 0:128], T.kc[0:1, 0:64], True, False, ["ones", "kc"], ["pb1"])
         for h in range(2):
             keyed(h, lambda a, b: T.ones[0:8, a:b], lambda a, b: T.th8[0:8, a:b, :], None, False, ["ones", "th8"])
-        lag = 2 if n == 0 else 0
+        lag = 3 if n == 0 else 0
+        achunks = ((0, 8), (8, 16), (16, 24)) + (((24, 27), (27, 29)) if lag else ((24, 28), (28, 30), (30, 32)))
 
         def slot(a):
             return 2 * n + 1 - a // 16
@@ -430,7 +490,7 @@ def rank_program(g, core, T, topo):
             for j in range(jdone, upto):
                 own(j)
             jdone = upto
-            if n == 0 and b == 6:
+            if n == 0 and b == 20:
                 for bk, two in banks:
                     if bk:
                         ties(bk, two)
@@ -439,17 +499,23 @@ def rank_program(g, core, T, topo):
             for j in range(jdone, 32):
                 own(j)
         meanwhile()
-        ac(T.sw[:, spare(n)], T.inf[:, n, :], AF.Identity, [fn, "col%d" % C_ID], ["sd%d" % n], scale=col(C_ID))
-        if last:
-            ac(T.leno[:], T.inf[:, n, :], AF.Identity, [fn, "col%d" % C_LEN], ["leno"], scale=col(C_LEN))
-        ac(T.spc[:, 1, :, :], T.spc[:, 0, :, :], AF.Identity, ["spa", "spb", "g84"], ["spc"], scale=1.0 / FAM, bias=T.g8[:, 4 + n:5 + n])
-        op("v", ["pb0", "rm"], ["scn", "r1", "r64"],
-           lambda: vec.tensor_tensor_scan(T.scn[:], T.rm[:], pb[0][:, 0:NT], 0.0, ALU.mult, ALU.max))
+        if n == 0:
+            for w in WFV + [T.wg]:
+                aset(w[:], T.ones[:, 0:128], 0.0, ["wf"] * (w is T.wg))
+        else:
+            ac(T.outI[:, n - 1, :], pb[2][:, 0:NT], AF.Copy, ["pb2"], ["ids"])
+            send_ids(n - 1)
+        ac(T.spc[:, 1, :], T.spc[:, 0, :], AF.Identity, ["spa", "spb", "g84"], ["spc"], scale=1.0 / FAM, bias=T.g8[:, 4 + n:5 + n])
+        for bk, a, b in ((1, 128, NT), (0, 0, 128)):
+            op("v", ["pb%d" % bk, "rm"], ["scn%d" % bk] + ["r1", "r64"] * bk,
+               lambda: vec.tensor_tensor_scan(T.scn[:, a:b], T.rm[:, a:b], pb[bk][:, 0:b - a], 0.0, ALU.mult, ALU.max))
+        meanwhile()
         key, r64, r1 = T.scn[:, 15::16], T.scn[:, 14::16], T.scn[:, 13::16]
-        ts(r64, key, ROUND_64, ROUND_64, ALU.add, ALU.subtract, ["scn"], ["r64"])
-        ts(r1, key, ROUND_1, ROUND_1, ALU.add, ALU.subtract, ["scn"], ["r1"])
-        ts(T.gi[:], key, 0.5, 1.0 / GS, ALU.add, ALU.mult, ["scn"], ["gi"])
-        tt(row(4), key, r64, ALU.subtract, ["scn", "r64"], ["dl"])
+        SCN = ["scn0", "scn1"]
+        ts(r64, key, ROUND_64, ROUND_64, ALU.add, ALU.subtract, SCN, ["r64"])
+        ts(r1, key, ROUND_1, ROUND_1, ALU.add, ALU.subtract, SCN, ["r1"])
+        ts(T.gi[:], key, 0.5, 1.0 / GS, ALU.add, ALU.mult, SCN, ["gi"])
+        tt(row(4), key, r64, ALU.subtract, SCN + ["r64"], ["dl"])
         tt(row(3), r64, r1, ALU.subtract, ["r1", "r64"], ["dh"])
         cp(row(5), T.gi[:], ["gi"], ["dg"])
         DD = DW + ["dh", "dl", "dg", "idb"]
@@ -459,34 +525,62 @@ def rank_program(g, core, T, topo):
             p = slice(0, 128) if t0 < 8 else slice(64 * odd, 64 * odd + 64)
             mm(o, T.dd[:, c0:c0 + 128], T.idb[:, p], start, stop, DD, ["pb%d" % bk])
 
+        turn(pb[2][:, 0:128], 0, 0, 0, True, True, 2)
+        turn(pb[2][:, 128:256], 4, 1, 0, True, True, 2)
         turn(pb[1][:, 0:128], 0, 0, 3, True, False, 1)
         turn(pb[1][:, 0:128], 4, 1, 3, False, True, 1)
         turn(pb[1][:, 128:NT], 8, 0, 3, True, False, 1)
         turn(pb[1][:, 128:NT], 8, 1, 3, False, True, 1)
-        turn(pb[2][:, 0:128], 0, 0, 0, True, True, 2)
-        turn(pb[2][:, 128:NT], 8, 0, 0, True, True, 2)
-        turn(pb[2][:, NT:256], 8, 1, 0, True, True, 2)
-        turn(pb[0][:, 0:128], 4, 1, 0, True, True, 0)
+        turn(pb[0][:, 0:64], 8, 0, 0, True, True, 0)
+        turn(pb[0][:, 64:128], 8, 1, 0, True, True, 0)
         meanwhile()
-        cp(T.ll[:, 0:256], pb[2][:, 0:256], ["pb2"], ["le"])
-        ac(T.rb[:, 0:NT], pb[1][:, 0:NT], AF.Copy, ["pb1"], ["rb"])
+        ac(T.ll[:, 0:256], pb[2][:, 0:256], AF.Copy, ["pb2"], ["le"])
+        cp(T.rb[:, 0:NT], pb[1][:, 0:NT], ["pb1"], ["rb"])
         ac(T.ll[:, 256:2 * NT], pb[0][:, 0:128], AF.Copy, ["pb0"], ["lo"])
         meanwhile()
-        for t in (0, 8, 4, 1, 5, 9, None, 6, 2, 7, 10, 3, 11):
-            if t is None:
-                ties(*banks[3])
-                continue
+
+        def pairs(t):
             bk, s = place[t]
-            if s and t < 8:
+            if s and t >= 8:
                 need("p", [lastw["pb%d" % bk][0:2] + ("tile",)])
-            p0, c0 = 32 * (t % 4), (0, 256, 128)[t // 4]
+            p0, c0 = 32 * (t % 4), 128 * (t // 4)
             mm(pb[bk][:, NU * s:NU * (s + 1)], T.ll[p0:p0 + 32, c0:c0 + 128], T.rb[p0:p0 + 32, 0:NU], False, s == 1,
-               [("le", "lo", "le")[t // 4], "rb", "rbx"], ["pb%d" % bk])
-        conv = pb[1][:, 0:HALF]
-        mm(conv, T.ones[0:1, 0:128], T.cst[0:1, :, :], True, False, ["ones", "cst0", "cst1", "cst2"], ["pb1"])
-        for a in range(8):
-            for r in (3, 4):
-                mm(pb[1][:, 12 * a:12 * (a + 1)], T.pick[:, a, :], row(r), False, False, PK + ["dh", "dl"], ["pb1"])
+               [("le", "le", "lo")[t // 4], "rb", "rbx"], ["pb%d" % bk])
+
+        parts = ((1, 0, 8, 0), (2, 8, 4, 64))
+
+        def families(j):
+            bk, t0, nt, c0 = parts[j]
+            c0 += 32 * j * last
+            mm(pb[bk][:, 0:8 * nt], T.ones[0:1, 0:128], T.cst[0:1, c0:c0 + 8 * nt], True, False, ["ones"] + CST, ["pb%d" % bk])
+            for a in range(8):
+                for r in (3, 4):
+                    mm(pb[bk][:, nt * a:nt * (a + 1)], T.pick[:, a, :], row(r, t0, t0 + nt), False, False, PK + ["dh", "dl"], ["pb%d" % bk])
+
+        def losses(j):
+            bk, t0, nt, c0 = parts[j]
+            for a in range(8):
+                mm(pb[bk][:, nt * a:nt * (a + 1)], T.pick[:, a, :], T.res[:, t0:t0 + nt], False, a == 7,
+                   PK + ["res%d" % t for t in range(t0, t0 + nt)], ["pb%d" % bk])
+
+        def least(j):
+            bk, t0, nt, c0 = parts[j]
+            tt(T.conv[:, c0:c0 + 8 * nt], pb[bk][:, 0:8 * nt], T.spc[:, 1, c0:c0 + 8 * nt], ALU.min, ["pb%d" % bk, "spc"], ["conv%d" % j])
+
+        LN = ["lst%d_%d" % (n, h) for h in range(2)]
+
+        def columns(h):
+            ts(T.lst[:, n, 6 * h:6 * h + 16], T.conv[:, 0:64 + 32 * h].indirect(T.gl2[:, 2 * h:2 * h + 1]), FAM, float(MID), ALU.mult, ALU.add,
+               ["conv0", "gl2", "gl2b"] + ["conv1", LN[0]] * h, [LN[h]])
+
+        for t in (0, 4, 3, 7, 1, 5, 2, 6):
+            pairs(t)
+        pairs(8)
+        ties(*banks[5])
+        pairs(9)
+        pairs(10)
+        families(0)
+        pairs(11)
 
         def tile(t):
             bk, s = place[t]
@@ -509,74 +603,116 @@ def rank_program(g, core, T, topo):
             op("v", [bk], ["res%d" % t],
                lambda: vec.tensor_reduce(T.res[:, t:t + 1], src, AX.X, ALU.min, negate=True, apply_absolute_value=True))
 
-        for t in on_vector[0:5]:
+        for t in (0, 4, 1, 5, 2, 6):
             by_vector(t)
-        for j in range(3):
-            by_scalar(j)
-            if j:
-                sum_scalar(j - 1)
-        sum_scalar(2)
-        for t in on_vector[5:]:
-            by_vector(t)
+        by_scalar(0)
+        by_scalar(1)
+        sum_scalar(0)
+        sum_scalar(1)
+        ac(T.sw[:, spare(n)], T.inf[:, n, :], AF.Identity, [fn, "col%d" % C_ID], ["sd%d" % n], scale=col(C_ID))
+        losses(0)
+        families(1)
+        by_vector(8)
+        by_vector(9)
+        if last:
+            ac(T.leno[:], T.inf[:, n, :], AF.Identity, [fn, "col%d" % C_LEN], ["leno"], scale=col(C_LEN))
+            by_vector(10)
+            by_vector(11)
+        else:
+            by_scalar(2)
+            sum_scalar(2)
+        least(0)
         meanwhile()
-        for a in range(8):
-            mm(pb[1][:, 12 * a:12 * (a + 1)], T.pick[:, a, :], T.res[:, 0:12], False, a == 7,
-               PK + ["res%d" % t for t in range(12)], ["pb1"])
-        tt(T.conv[:], conv, T.spc[:, 1, :, :], ALU.min, ["pb1", "spc"], ["conv"])
-        ln = "lst%d" % n
-        ts(T.lst[:, n, :], T.conv[:].indirect(T.gl2[:, 0:1]), FAM, float(MID), ALU.mult, ALU.add, ["conv", "gl2"], [ln])
-        lst = T.lst[:, n, 0:12]
+        columns(0)
         if not last:
-            s0, s1 = 2 * n + 2, 2 * n + 3
+            by_vector(11)
+        meanwhile()
+        s0, s1 = 2 * n + 2, 2 * n + 3
 
-            def take(h):
-                s, lh = s0 + h, T.lst[:, n, 6 * h:6 * (h + 1)]
-                cp(T.oa[:, s, 16:16 + HALF], T.aw[:, 0:wn].indirect(lh), ["aw", ln] + AD, ["oa%d" % s])
-                ac(half(T.outC, n, h), T.yw[:, 0:wn].indirect(lh), AF.Copy, Y3 + YD + [ln], ["oc%d" % s])
+        def lh(h):
+            return T.lst[:, n, 6 * h:6 * (h + 1)]
 
-            take(1)
-            send(["oc%d" % s1], [(1, half(T.outC, n, 1), T.cL[:, s1, 0:HALF])], ["c%d" % s1])
-            ac(T.raw[:], T.sw[:, 0:wn].indirect(lst), AF.Copy, S6 + SD + [ln], ["raw"])
-            turns(s1)
-            take(0)
-            offsets(s1, T.outO, "oo")
-            send(["oo%d" % s1], [(1, T.outO[:, s1, :], T.off[:, s1, :])], ["off%d" % s1])
-            turns(s0)
+        def cut(h):
+            return slice(HALF * h, HALF * (h + 1))
+
+        def take_lists(h):
+            cp(T.oa[:, s0 + h, 16:16 + HALF], T.aw[:, 0:wn].indirect(lh(h)), ["aw", LN[h]] + AD, ["oa%d" % (s0 + h)])
+
+        def take_features(h):
+            ac(half(T.outC, n, h), T.yw[:, 0:wn].indirect(lh(h)), AF.Copy, Y3 + YD + [LN[h]], ["oc%d" % (s0 + h)])
+
+        def take_rows(h):
+            ac(T.raw[:, cut(h)], T.sw[:, 0:wn].indirect(lh(h)), AF.Copy, S6 + SD + [LN[h]], ["raw%d" % h])
+
+        def new_rows(h, which):
+            o, bk = pb[3 + 2 * h][:, 0:HALF], "pb%d" % (3 + 2 * h)
+            if which == 0:
+                mm(o, T.wf1[:], half(T.inf, n, h), True, False, WF8 + [fn], [bk])
+                mm(o, T.wg[:], T.rb[:, cut(h)], False, False, ["wg", "rb"], [bk])
+            elif which == 1:
+                mm(o, T.wf0[:], T.raw[:, cut(h)], False, True, WF8 + ["raw%d" % h], [bk])
+            else:
+                ac(T.vv[:, cut(h)], o, AF.Identity, [bk, "col%d" % C_TH], ["vv%d" % h], bias=col(C_TH))
+
+        def take_ids(h):
+            tt(half(T.outI, n, h), T.sw[:, 0:wn].indirect(lh(h)), T.leno[:, cut(h)], ALU.add, S6 + SD + [LN[h], "leno"], ["oi%d" % h])
+
+        if not last:
+            take_lists(0)
+            take_features(0)
+            send(["oc%d" % s0], [(0, half(T.outC, n, 0), T.cL[:, s1, 0:HALF])], ["c%d" % s1])
+            new_rows(0, 0)
+            losses(1)
+            new_rows(1, 0)
+            take_rows(0)
+            new_rows(0, 1)
+            new_rows(0, 2)
+            turns(s0, (0,))
+            least(1)
+            turns(s0, (1,))
+            columns(1)
             offsets(s0, T.outO, "oo")
-            send(["oc%d" % s0, "oo%d" % s0], [(0, half(T.outC, n, 0), T.cL[:, s0, 0:HALF]), (0, T.outO[:, s0, :], T.off[:, s0, :])],
-                 ["c%d" % s0, "off%d" % s0])
+            send(["oo%d" % s0], [(0, T.outO[:, s0, :], T.off[:, s1, :])], ["off%d" % s1])
+            take_rows(1)
+            new_rows(1, 1)
+            take_features(1)
+            send(["oc%d" % s1], [(1, half(T.outC, n, 1), T.cL[:, s0, 0:HALF])], ["c%d" % s0])
+            new_rows(1, 2)
+            take_lists(1)
+            cp(T.sw[:, 0:wn].indirect(lh(0)), T.vv[:, cut(0)], ["vv0", LN[0]], S6 + SD)
+            turns(s1)
+            cp(T.sw[:, 0:wn].indirect(lh(1)), T.vv[:, cut(1)], ["vv1", LN[1]], S6 + SD)
+            offsets(s1, T.outO, "oo")
+            send(["oo%d" % s1], [(1, T.outO[:, s1, :], T.off[:, s0, :])], ["off%d" % s0])
             if n < NR - 2:
-                send(["oa%d" % s0, "oa%d" % s1], [(h, T.oa[:, s0 + h, 16:16 + HALF], half(T.alL, n + 1, h)) for h in range(2)],
+                send(["oa%d" % s0, "oa%d" % s1], [(h, T.oa[:, s0 + h, 16:16 + HALF], half(T.alL, n + 1, there[h])) for h in range(2)],
                      ["al%d" % (n + 1)])
             o = pb[2][:, 0:NT]
-            mm(o, T.wf[:, 1, :], T.inf[:, n, :], True, False, WF8 + [fn], ["pb2"])
-            mm(o, T.wg[:], T.rb[:, 0:NT], False, False, ["wg", "rb"], ["pb2"])
-            mm(o, T.wf[:, 0, :], T.raw[:], False, True, WF8 + ["raw"], ["pb2"])
-            ac(T.vv[:], o, AF.Identity, ["pb2", "col%d" % C_TH], ["vv"], bias=col(C_TH))
-            o = pb[1][:, 0:NT]
             if n:
-                mm(o, T.wf[:, 2, :], T.inf[:, n, :], True, False, WF8 + [fn], ["pb1"])
-            mm(o, T.wf[:, 3, :], T.raw[:], n == 0, True, WF8 + ["raw"], ["pb1"])
-            ac(T.outI[:, n, :], o, AF.Copy, ["pb1"], ["oi%d" % n])
+                mm(o, T.wf2[:], T.inf[:, n, :], True, False, WF8 + [fn], ["pb2"])
+            mm(o, T.wf3[:], T.raw[:], n == 0, True, WF8 + ["raw0", "raw1"], ["pb2"])
 
-            def features(h, n=n, wn=wn, YD=YD):
-                cp(T.yw[:, 0:wn].indirect(T.lst[:, n, 6 * h:6 * (h + 1)]), T.cL[:, 2 * n + h, 0:HALF], ["c%d" % (2 * n + h), "lst%d" % n],
-                   Y3 + YD)
+            def features(a, b, n=n, wn=wn, YD=YD, LN=LN):
+                s, c0 = 2 * n + a // 6, 16 * (a % 6)
+                cp(T.yw[:, 0:wn].indirect(T.lst[:, n, a:b]), T.cL[:, s, c0:c0 + 16 * (b - a)], ["c%d" % s] + LN, Y3 + YD)
 
-            def applicants(h, n=n, wn=wn, AD=AD):
-                cp(T.aw[:, 0:wn].indirect(T.lst[:, n, 6 * h:6 * (h + 1)]), half(T.alL, n, h), ["al%d" % n, "lst%d" % n], ["aw"] + AD)
+            def applicants(a, b, n=n, wn=wn, AD=AD, LN=LN):
+                cp(T.aw[:, 0:wn].indirect(T.lst[:, n, a:b]), T.alL[:, n, 16 * a:16 * b], ["al%d" % n] + LN, ["aw"] + AD)
 
-            cp(T.sw[:, 0:wn].indirect(lst), T.vv[:], ["vv", ln], S6 + SD)
             if n < NR - 2:
-                features(0)
-                later += [lambda: None, lambda f=applicants: f(0), lambda f=features: f(1), lambda f=applicants: f(1)]
+                later += [lambda f=applicants: f(0, 4), lambda f=features: f(4, 6), lambda f=applicants, f2=features: (f(4, 12), f2(0, 2)),
+                          lambda f=features: f(6, 12), lambda f=features: f(2, 4), lambda: None]
         else:
-            tt(T.outI[:, n, :], T.sw[:, 0:wn].indirect(lst), T.leno[:], ALU.add, S6 + SD + [ln, "leno"], ["oi%d" % n])
-            send_ids(n)
-            cp(T.sw[:, 0:wn].indirect(lst), T.inf[:, n, :], [fn, ln], S6 + SD)
+            losses(1)
+            least(1)
+            take_ids(0)
+            send(["oi0"], [(0, half(T.outI, n, 0), half(T.inf, NR, flip))], ["end0"])
+            columns(1)
+            take_ids(1)
+            send(["oi1"], [(1, half(T.outI, n, 1), half(T.inf, NR, 1 - flip))], ["end1"])
+            cp(T.sw[:, 0:wn].indirect(T.lst[:, n, 0:12]), T.inf[:, n, :], [fn] + LN, S6 + SD)
 
-    fn = "inf%d" % NR
     dma("s", S6, ["yh"], T.yh[:], T.sw[R_ID::16, 0:V])
-    dma("a", [fn], ["yt"], T.yt[:], T.inf[R_ID::16, NR, :])
-    dma("s", [fn], ["yl"], T.yl[:], T.inf[R_LEN::16, NR, :])
+    dma("a", ["end0", "end1"], ["yt"], T.yt[:], T.inf[R_ID::16, NR, :])
+    dma("s", ["end0", "end1"], ["yl"], T.yl[:], T.inf[R_LEN::16, NR, :])
     need("g", [(sem, val, "end") for sem, val in count.items()])

from concourse.bass import DstId, RemoteDMATransfer
from concourse.mybir import AluOpType as ALU, AxisListType as AX, ActivationFunctionType as AF

V, NT, HALF, NR = 3072, 192, 96, 4
W = V + NR * NT
NU = NT + 1
F, B, I, U = "float32", "bfloat16", "int32", "uint16"

SCRATCH = {}
for _dt, _bufs in (
    (F, dict(sw=[W], inf=[NR + 1, NT], outI=[NR, NT], raw=[NT], scn=[NT], rm=[NT], sg2=[8],
             leno=[NT], vv=[NT], pf=[12], j16=[NR], g1=[6], g3=[6], g6=[6], g7=[6], g8=[24], gcol=[128], gnat=[8], thf=[4], rown=[8], tcol=[2],
             cols=[4], wf0=[128], wf1=[128], wf2=[128], wf3=[128], conv=[HALF], spc=[2, HALF])),
    (B, dict(xw=[V], yw=[W], mx=[V], sg=[V], cL=[2 * NR, 4 * HALF], outC=[NR - 1, NT], dd=[416], rb=[NU + 7], ll=[2 * NT],
             junk=[2, NU + 7], crow=[512], wc=[6, 128], wab=[144], wg=[128], wm=[8], ws=[8], wsc=[8, 16], ones=[256], kc=[NT],
             m8=[8, 16], th8=[8, 16], idb=[128], res=[16], tri=[4, NU], trow=[NU + 7], pick=[8, 128], cst=[128])),
    (I, dict(aw=[W], alL=[NR, NT], ia=[224], oa=[2 * NR, 128], tt=[2, 224], gi=[12], pidx=[4], pi3=[8], g2=[6], thi=[4], thc=[4])),
    (U, dict(off=[2 * NR, HALF], outO=[2 * NR, HALF], lst=[NR, 24], gl=[6], gl2=[4])),
):
    for _k, _s in _bufs.items():
        SCRATCH[_k] = ("sbuf", [128] + _s, _dt)
for _b in range(8):
    SCRATCH["pb%d" % _b] = ("psum", [128, 512], F)

SEMAPHORES = (["cv", "ca", "cp", "cg", "sent"] + ["d%d" % _i for _i in range(28)] + ["r%d" % _i for _i in range(24)])

GS = 16.0
FAM = 4096.0
MID = V // 2
WIN = 256.0
WF = 1024.0 * FAM
ROUND_1, ROUND_64 = 1.5 * 2.0 ** 23, 1.5 * 2.0 ** 17
D0 = 16
R_A, R_B, R_HI, R_LO, R_ID, R_LEN = 0, 1, 2, 3, 4, 5
C_ID, C_LEN, C_TH = range(3)
P_G, P_H, P_1, P_M, P_Q, P_2, P_S1, P_S2, P_16 = range(9)


def rank_program(g, core, T, topo):
    rank = T.rank_of(core)
    if rank is None:
        return
    n_ranks = len(T.cores)
    nxt, prv = T.cores[(rank + 1) % n_ranks], T.cores[(rank - 1) % n_ranks]

    def swapped(r):
        return int(topo.mates(topo.chip(T.cores[r % n_ranks]), topo.chip(T.cores[(r - 1) % n_ranks])))

    flip = swapped(rank)
    there = [h ^ flip ^ swapped(rank + (1, -1)[h ^ flip]) for h in range(2)]
    assert there == [1, 0]
    queues = {"v": g.vector, "a": g.scalar, "p": g.tensor, "g": g, "s": g.sync}
    csem = {"v": "cv", "a": "ca", "p": "cp", "g": "cg"}
    count = {}
    waited = {q: {} for q in queues}
    lastw, readers = {}, {}
    ndma, nsend = [0], [0]

    def need(q, toks):
        top = {}
        for (sem, val, owner) in toks:
            if q == "p" and owner == "p":
                continue
            if val > top.get(sem, 0):
                top[sem] = val
        for sem, val in top.items():
            if waited[q].get(sem, 0) < val:
                queues[q].wait_ge(T.sem[sem], val)
                waited[q][sem] = val

    def order(q, rd, wr):
        toks = []
        for k in rd:
            if k in lastw:
                toks.append(lastw[k])
            if k.startswith("pb"):
                toks += [t for t in readers.get(k, []) if t[2] != q]
        for k in wr:
            if k in lastw:
                toks.append(lastw[k])
            toks += readers.get(k, [])
        need(q, toks)

    def done(tok, rd, wr):
        for k in rd:
            readers.setdefault(k, []).append(tok)
        for k in wr:
            lastw[k] = tok
            readers[k] = []

    def op(q, rd, wr, call):
        order(q, rd, wr)
        sem = csem[q]
        count[sem] = count.get(sem, 0) + 1
        call().then_inc(T.sem[sem], 1)
        done((sem, count[sem], q), rd, wr)

    def dma(q, rd, wr, out, in_, **kw):
        order(q, rd, wr)
        sem = "d%d" % ndma[0]
        ndma[0] += 1
        count[sem] = 16
        queues[q].dma_start(out, in_, **kw).then_inc(T.sem[sem], 16)
        done((sem, 16, "dma"), rd, wr)

    def send(rd, moves, keys):
        order("g", rd, [])
        sem = "r%d" % nsend[0]
        nsend[0] += 1
        trs = []
        count[sem] = 0
        for j, (h, src, dst) in enumerate(moves):
            to, frm = (nxt, prv)[h ^ flip], (prv, nxt)[there[h] ^ flip]
            eng = topo.engines(core, to)
            eng = eng[j * len(eng) // len(moves):(j + 1) * len(eng) // len(moves)]
            rid, pid = topo.addr(to)[0:2]
            trs.append(RemoteDMATransfer(dst_ids=[DstId(rid=rid, pnc=pid)], dma_engine_mask=sum(1 << e for e in eng),
                                         remote_sem=T.sem[sem], src=src, dst=dst))
            count["sent"] = count.get("sent", 0) + len(eng)
            count[sem] += len(topo.engines(frm, core)) // len(moves)
        g.remote_dma_fused(trs, local_sem=T.sem.sent)
        for k in keys:
            lastw[k] = (sem, count[sem], "remote")

    vec, act, pe = g.vector, g.scalar, g.tensor

    def mset(ap, val, wr):
        op("v", [], wr, lambda: vec.memset(ap, val))

    def ts(out, in0, s1, s2, o0, o1, rd, wr):
        if o1 is None:
            op("v", rd, wr, lambda: vec.tensor_scalar(out, in0, s1, None, o0))
        else:
            op("v", rd, wr, lambda: vec.tensor_scalar(out, in0, s1, s2, o0, o1))

    def tt(out, in0, in1, o, rd, wr):
        op("v", rd, wr, lambda: vec.tensor_tensor(out, in0, in1, o))

    def cp(out, in_, rd, wr):
        op("v", rd, wr, lambda: vec.tensor_copy(out, in_))

    def ac(out, in_, func, rd, wr, **kw):
        op("a", rd, wr, lambda: act.activation(out, in_, func, **kw))

    def aset(ap, src, val, wr):
        ac(ap, src, AF.Identity, ["ones"], wr, scale=0.0, bias=val)

    def mm(out, lhsT, rhs, start, stop, rd, wr):
        op("p", rd, wr, lambda: pe.matmul(out, lhsT, rhs, start, stop))

    def iota(out, pat, base, ch, wr, flag=True):
        rd = [] if "pool" in wr else ["pool"]
        if flag:
            op("g", rd, wr, lambda: g.iota(out, pat, base, ch, allow_small_or_imprecise_dtypes=True))
        else:
            op("g", rd, wr, lambda: g.iota(out, pat, base, ch))

    def sel(out, in_, pat, cmp, fill, base, ch, rd, wr):
        op("g", rd + ([] if "pool" in wr else ["pool"]), wr, lambda: g.affine_select(out, in_, pat, cmp, fill, base, ch))

    pb = [T["pb%d" % b] for b in range(8)]
    X3, Y3 = ["x0", "x1", "x2", "x3"], ["y0", "y1", "y2", "y3"]
    pieces = [(512 * j, 512 * (j + 1)) for j in range(5)] + [(2560, 2816), (2816, V)]
    part = (0, 0, 1, 1, 2, 2, 3)
    S6 = ["s%d" % j for j in range(len(pieces))]
    MX = ["mx%d" % k for k in range(32)]

    def pc(j):
        return T.pf[:, j:j + 1]

    def col(j):
        return T.cols[:, j:j + 1]

    def spare(n):
        return slice(V + NT * n, V + NT * (n + 1))

    for j, (a, b) in enumerate(((0, 1024), (1024, 2048), (2048, 2816), (2816, V))):
        dma("a", [], [Y3[j]], T.yw[:, a:b], T.hx[:, a:b])
        dma("s", [], [X3[j]], T.xw[:, a:b], T.fx[:, a:b])
        if j == 0:
            dma("s", [], ["ia"], T.ia[:, 16:16 + NT], T.va[:])
            dma("s", [], ["thi"], T.thi[0:8, 0:1], T.th[:, 0])
        if j in (1, 3):
            h = int(j == 1)
            dma("a", [], ["c%d" % h], T.cL[:, h, 0:HALF], T.vx[:, HALF * (h ^ flip):HALF * ((h ^ flip) + 1)])

    CR = ["cr%d" % j for j in range(9)]
    WCK = ["wa%d" % j for j in range(8)]
    mset(T.crow[0:65, :], 1.0, CR)
    iota(T.pidx[:, 0:1], [[0, 1]], 0, 1, ["pidx"], flag=False)
    iota(T.gnat[:], [[1, 8]], 0, 0, ["gnat"])
    iota(T.crow[32:33, 0:64], [[1, 64]], 0, 0, [CR[8], "pool"])
    for j in range(8):
        ac(T.crow[0:1, 64 * j:64 * (j + 1)], T.crow[0:1, 64 * j:64 * (j + 1)], AF.Identity, [CR[j]], [CR[j]], scale=float(j))
    mset(T.ones[:], 1.0, ["ones"])
    mset(T.wc[0:65, :, :], 0.0, WCK)
    sel(T.idb[:], T.ones[:, 0:128], [[-1, 128]], ALU.is_equal, 0.0, 0, 1, ["ones"], ["idb"])
    iota(T.wc[64:65, :, R_HI::16], [[8, 6], [0, 8]], -MID // 64, 0, [WCK[6], "pool"])
    iota(T.wc[64:65, :, R_ID::16], [[512, 6], [0, 8]], V * rank, 0, [WCK[7], "pool"])
    iota(T.g1[:], [[256, 6]], 0, 16, ["g1"])
    iota(T.gcol[:], [[1, 2], [2, 4], [0, 16]], 0, 0, ["gcol"])
    iota(T.j16[:], [[NT, NR]], 0, 0, ["j16"])
    for j, (p, r, val) in enumerate(((0, R_HI, 1.0), (0, R_ID, 64.0), (32, R_LO, 1.0), (32, R_ID, 1.0), (64, R_A, -120.0), (64, R_LEN, 1.0))):
        if j % 2 == 0:
            w = 64 << (j // 2)
            cp(T.crow[32:33, w:2 * w], T.crow[32:33, 0:w], [CR[8]], [CR[8]])
        mset(T.wc[p:p + 1, :, r::16], val, [WCK[j]])

    def bits(j, shift, mask):
        ts(T.pi3[:, j:j + 1], T.pidx[:, 0:1], shift, mask, ALU.arith_shift_right, ALU.bitwise_and, ["pidx"], ["pi%d" % j])

    bits(P_G, 4, 7)
    bits(P_H, 4, 1)
    bits(P_1, 0, 1)
    mset(T.wab[:], 0.0, ["wab"])
    cp(T.pf[:, 0:3], T.pi3[:, 0:3], ["pi0", "pi1", "pi2"], ["pf"])
    mset(T.thc[:], 0, ["thc"])
    ts(T.wab[:, 1:129:16], T.gnat[:], pc(P_G), None, ALU.is_equal, None, ["gnat", "pf"], ["wab"])
    aset(T.ws[:], T.ones[:, 0:8], 0.0, ["ws"])
    dma("s", [Y3[3], X3[3]], ["aw"], T.aw[:, 0:V], T.ha[:])
    for a, b in ((0, HALF), (HALF, NT)) if flip else ((0, NT),):
        a2 = (a + HALF * flip) % NT
        dma("s", [], ["ad0" + "b" * (a > 0)], T.aw[:, V + a:V + b], T.va[:, a2:a2 + b - a])
        dma("s", [], ["yd0" + "b" * (a > 0)], T.yw[:, V + a:V + b], T.vx[:, a2:a2 + b - a])
    dma("s", [], ["thc"], T.thc[R_B::16, 0:1], T.th[:, 0])
    dma("s", ["ad0", "ad0b"], ["al0"], T.alL[:, 0, :], T.aw[:, spare(0)])

    def turn_list():
        ts(pc(P_S1), pc(P_G), -256.0, -40.0, ALU.mult, ALU.add, ["pf"], ["pf1"])
        ts(pc(P_S2), pc(P_1), pc(P_H), 112.0, ALU.not_equal, ALU.mult, ["pf"], ["pf2"])
        mset(T.ia[:, 0:16], 0, ["ipad0"])
        ts(T.g2[:], T.g1[:], pc(P_S1), 1.0 / HALF, ALU.add, ALU.mult, ["g1", "pf1"], ["g2"])
        ts(T.g7[:], T.g1[:], pc(P_S1), pc(P_S2), ALU.add, ALU.add, ["g1", "pf1", "pf2"], ["g7"])
        mset(T.ia[:, 16 + NT:224], 0, ["ipad1"])
        ts(T.g3[:], T.g2[:], 1.0 - HALF, 40.0, ALU.mult, ALU.add, ["g2"], ["g3"])
        ts(T.wm[:], T.gcol[:, 0::16], pc(P_G), -2.0 * GS, ALU.is_equal, ALU.mult, ["gcol", "pf"], ["wm"])
        tt(T.g6[:], T.g7[:], T.g3[:], ALU.add, ["g7", "g3"], ["g6"])
        cp(T.gl[:], T.g6[:], ["g6"], ["gl"])

    def turns(s, which=(0, 1)):
        h = s % 2
        if s < 2:
            c0 = HALF * (h ^ flip)
            one, two, rd = T.ia[:, c0 + 16:c0 + 16 + HALF], T.ia[:, c0:c0 + 128], ["ia", "ipad0", "ipad1"]
        else:
            one, two, rd = T.oa[:, s, 16:16 + HALF], T.oa[:, s, :], ["oa%d" % s, "pad0", "pad1"]
        if 0 in which:
            op("v", rd, ["tt%db" % h], lambda: vec.transpose(T.tt[:, h, HALF:224], two))
        if 1 in which:
            op("v", rd[0:1], ["tt%da" % h], lambda: vec.transpose(T.tt[:, h, 0:HALF], one))

    def offsets(s, out, key):
        cp(out[:, s, :], T.tt[:, s % 2, :].indirect(T.gl[:]), ["tt%da" % (s % 2), "tt%db" % (s % 2), "gl"], [key + str(s)])

    def copies(s, q):
        for w, rd, wr in ((HALF, ["c%d" % s], "c%db" % s), (NT, ["c%d" % s, "c%db" % s], "c%dc" % s)):
            if q == "g":
                sel(T.cL[:, s, w:2 * w], T.cL[:, s, 0:w], [[0, w]], ALU.is_ge, 0.0, 0, 0, rd, [wr])
            else:
                ac(T.cL[:, s, w:2 * w], T.cL[:, s, 0:w], AF.Copy, rd, [wr])

    def numbers(j):
        a, b = pieces[j]
        mm(pb[j % 6][:, 0:b - a], T.wc[0:65, a // 512, :], T.crow[0:65, a % 512:a % 512 + b - a], True, False, CR + WCK, ["pb%d" % (j % 6)])

    for j in range(3):
        numbers(j)

    iota(T.kc[0:1, :], [[0, 12], [-1, 16]], 7, 0, ["kc"])
    sel(T.m8[0:8, :, :], T.ones[0:8, 0:128], [[-1, 2], [-2, 4], [0, 16]], ALU.is_equal, 0.0, 0, 1, ["ones"], ["m8"])
    between = [
        lambda: iota(T.trow[:, 0:NT], [[HALF - NT * flip, 2], [1, HALF]], HALF * flip, 0, ["trow"]),
        lambda: iota(T.tcol[:, 0:2], [[128 - NT * flip, 2]], HALF * flip, 1, ["tcol"]),
        lambda: iota(T.trow[:, NT:NU], [[0, 1]], -1, 0, ["trox"]),
        lambda: iota(T.rown[:], [[-16, 8]], 0, 1, ["rown"]),
    ]
    for j, (r, val) in enumerate(((R_A, 2.0 * GS), (R_B, -GS), (R_HI, 64.0 / FAM), (R_LO, 1.0 / FAM))):
        sel(T.ws[:], T.ws[:], [[-16, 2], [-32, 4]], ALU.not_equal, val, -r, 1, ["ws"], ["ws"])
        between[j]()
    iota(T.tcol[64:128, 1:2], [[0, 1]], 128 - HALF * flip, 1, ["tcol", "pool"])
    iota(T.tcol[HALF:128, 0:1], [[0, 1]], HALF - HALF * flip, 1, ["tcol", "pool"])
    copies(1, "g")
    iota(T.inf[:, 0, :], [[HALF - NT * flip, 2], [1, HALF]], n_ranks * V + NT * rank + HALF * flip, 0, ["inf0"])
    copies(0, "g")
    iota(T.spc[:, 0, 0:64], [[16, 8], [0, 8]], V - MID, 1, ["spa"])
    iota(T.spc[:, 0, 64:HALF], [[0, 2], [16, 4], [0, 4]], V - MID + 128, 1, ["spb"])
    WF8 = ["wf%d" % j for j in range(7)]
    TRI = ["tri%d" % j for j in range(4)]
    PK = ["pick"]

    def tie_tables():
        for j in range(4):
            ts(T.tri[:, j, :], T.trow[:, 0:NU], T.tcol[:, j // 2:j // 2 + 1], -WIN, ALU.is_lt, ALU.add, ["trow", "trox", "tcol"], [TRI[j]])

    def pick_tables(j):
        if j == 0:
            ac(T.pick[:, :, 0:16], T.idb[:], AF.Copy, ["idb"], PK)
        else:
            w = 8 << j
            ac(T.pick[:, :, w:2 * w], T.pick[:, :, 0:w], AF.Copy, PK, PK)

    def row(r, t0=0, t1=12):
        return T.dd[:, D0 + r + 32 * t0:D0 + 32 * t1:32]

    on_scalar = (3, 7, 10)
    CST = ["cst%d" % j for j in range(3)]
    DW = ["dw%d" % j for j in range(6)]
    pick_tables(0)
    aset(T.dd[:, 0:208], T.ones[:, 0:208], 0.0, ["dd0"])
    pick_tables(1)
    aset(T.dd[:, 208:416], T.ones[:, 0:208], 0.0, ["dd1"])
    pick_tables(2)
    aset(T.rm[:], T.ones[:, 0:NT], 1.0, ["rm"])
    aset(T.cst[0:1, :], T.ones[0:1, 0:128], WIN, ["cst"])
    pick_tables(3)
    for k in DW + ["dh", "dl", "dg"]:
        lastw[k] = lastw["dd1"]
    for j, (r, val) in enumerate(((0, WF), (1, WF), (2, 2.0), (6, -WF), (7, -WF), (8, -2.0))):
        aset(row(r), T.ones[:, 0:12], val, [DW[j]])
    aset(T.rm[:, 0::16], T.ones[:, 0:12], 0.0, ["rm"])
    for j, t in enumerate(on_scalar):
        lastw["cst%d" % j] = lastw["cst"]
        aset(T.cst[0:1, t:64:8] if t < 8 else T.cst[0:1, 56 + t:HALF:4], T.ones[0:1, 0:8], 0.0, [CST[j]])

    def key_weights():
        ts(T.thf[0:8, 0:1], T.thi[0:8, 0:1], -GS, 240.0 * GS, ALU.mult, ALU.add, ["thi"], ["thf"])
        ts(T.wsc[:], T.gcol[:], pc(P_G), GS, ALU.is_equal, ALU.mult, ["gcol", "pf"], ["wsc"])
        ts(T.th8[0:8, :, :], T.m8[0:8, :, :], T.thf[0:8, 0:1], None, ALU.mult, None, ["m8", "thf"], ["th8"])

    def first_lists():
        turns(1)
        turns(0)
        offsets(1, T.off, "off")
        offsets(0, T.off, "off")

    def late_0():
        bits(P_M, 0, 15)
        bits(P_Q, 5, 3)
        ts(pc(P_16), pc(P_G), -16.0, None, ALU.mult, None, ["pf"], ["pf16"])
        ts(T.g8[:, 2:3], pc(P_H), 12.0, 8.0, ALU.mult, ALU.add, ["pf"], ["g82"])
        cp(T.pf[:, 3:5], T.pi3[:, 3:5], ["pi3", "pi4"], ["pfb"])

    turn_list()
    fill = [late_0, first_lists, key_weights, tie_tables]

    def ycopy(j):
        a, b = pieces[j]
        mm(pb[6 + j % 2][:, 0:b - a], T.idb[:], T.yw[:, a:b], True, True, ["idb", Y3[part[j]]], ["pb%d" % (6 + j % 2)])

    ycopy(0)
    ycopy(1)
    for j, (a, b) in enumerate(pieces):
        o, bk = pb[j % 6][:, 0:b - a], "pb%d" % (j % 6)
        tt(T.mx[:, a:b], T.xw[:, a:b], pb[6 + j % 2][:, 0:b - a], ALU.max, [X3[part[j]], "pb%d" % (6 + j % 2)], ["im%d" % j])
        mm(o, T.wab[:, 0:128], T.yw[:, a:b], False, False, ["wab", Y3[part[j]]], [bk])
        if j < 3:
            numbers(j + 3)
        mm(o, T.wab[:, 1:129], T.mx[:, a:b], False, True, ["wab", "im%d" % j], [bk])
        for k in MX[a // HALF:(b - 1) // HALF + 1]:
            readers.setdefault(k, []).append(lastw[bk])
        if j + 2 < len(pieces):
            ycopy(j + 2)
        ac(T.sw[:, a:b], o, AF.Copy, [bk], [S6[j]])
        if j == 3:
            numbers(6)
        if j < len(fill):
            fill[j]()

    def column(c, r):
        ts(col(c), pc(P_M), float(r), None, ALU.is_equal, None, ["pfb"], ["col%d" % c])

    def passes(key, out, r, r2, val):
        ts(out[:, r2::16], T.rown[:], float(r), val, ALU.is_equal, ALU.mult, ["rown", "wf"], [key])

    def late_1():
        column(C_ID, R_ID)
        column(C_LEN, R_LEN)
        ts(T.g8[:, 4:8], T.j16[:], pc(P_16), 1.0 / FAM, ALU.add, ALU.mult, ["j16", "pf16"], ["g84"])
        ts(T.rb[:, NT:NU], pc(P_M), 5.0, -2.0, ALU.is_equal, ALU.mult, ["pfb"], ["rbx"])

    def late_2():
        ts(T.g8[:, 1:2], pc(P_H), 4.0, pc(P_Q), ALU.mult, ALU.add, ["pf", "pfb"], ["g81"])
        ts(T.g8[:, 8:16], T.rown[:], float(R_A), -2.0, ALU.is_equal, ALU.mult, ["rown"], ["g88"])

    def late_3():
        ts(T.g8[:, 0:1], pc(P_M), 8.0, T.g8[:, 1:2], ALU.mult, ALU.add, ["g81", "pfb"], ["g80"])
        ts(T.g8[:, 3:4], pc(P_M), -4.0, T.g8[:, 2:3], ALU.mult, ALU.add, ["g82", "pfb"], ["g83"])
        ts(pc(P_2), pc(P_M), 2.0, None, ALU.is_ge, None, ["pfb"], ["pf2up"])
        ts(T.g8[:, 16:24], T.rown[:], float(R_B), None, ALU.is_equal, None, ["rown"], ["g89"])
        mset(T.oa[:, 2:, 0:16], 0, ["pad0"])
        ts(T.gl2[:, 0:1], T.g8[:, 0:1], 63.0, None, ALU.min, None, ["g80"], ["gl2"])
        ts(T.g8[:, 2:3], T.g8[:, 3:4], pc(P_2), T.g8[:, 0:1], ALU.mult, ALU.add, ["g83", "g80", "pf2up"], ["g82"])
        mset(T.oa[:, 2:, 16 + HALF:128], 0, ["pad1"])

    def late_4():
        for j, (w, r) in enumerate(((0, R_HI), (0, R_LO), (1, R_ID), (2, R_LEN))):
            passes(WF8[j], WFV[w], r, r, 1.0)
        ts(T.gl2[:, 2:3], T.g8[:, 2:3], 48.0, HALF - 1.0, ALU.add, ALU.min, ["g82"], ["gl2b"])
        passes("wg", T.wg, 2, R_B, 1.0)
        tt(WFV[0][:, R_B::16], T.g8[:, 8:16], T.g8[:, 16:24], ALU.add, ["g88", "g89", "wf"], [WF8[6]])

    def late_5():
        passes(WF8[4], WFV[3], R_ID, R_ID, 1.0)
        passes(WF8[5], WFV[3], R_LEN, R_LEN, 1.0)

    def late_6():
        ts(col(C_TH), T.thc[:, 0:1], col(C_LEN), None, ALU.add, None, ["thc", "col%d" % C_LEN], ["col%d" % C_TH])

    WFV = [T["wf%d" % j] for j in range(4)]

    chunks = ((0, 2), (2, 6), (6, 10), (10, 14), (14, 16), (16, 20), (20, 24), (24, 28), (28, 30), (30, 32))
    banks = ((4, (3, 7)), (6, (2, 6)), (7, (8, 9)), (3, (0, 4)), (5, (1, 5)), (0, (10, 11)))
    place = {t: (bk, s) for bk, two in banks for s, t in enumerate(two)}

    def ties(bk, two):
        j = 0 if two[1] < 8 else 2
        mm(pb[bk][:, 0:2 * NU], T.idb[:], T.tri[:, j:j + 2, :], True, False, ["idb"] + TRI, ["pb%d" % bk])

    def keyed(h, data, wts, k, last, rd):
        def cols(a, b):
            return slice(a, b) if k is None else slice(a + k, b, 16)
        if h:
            mm(pb[1][0:64, cols(0, 64)], data(32, HALF), wts(0, 4), False, last, rd, ["pb1"])
            mm(pb[1][64:128, cols(0, 64)], data(32, HALF), wts(4, 8), False, last, rd, ["pb1"])
            mm(pb[0][HALF:128, cols(0, 128)], data(0, 32), wts(0, 8), False, last, rd, ["pb0"])
        else:
            mm(pb[0][0:HALF, cols(0, 128)], data(0, HALF), wts(0, 8), False, last, rd, ["pb0"])

    later = [late_1, late_2, late_3, late_4, late_5, late_6]

    def half(t, n, h):
        return t[:, n, HALF * h:HALF * (h + 1)]

    def send_ids(n):
        send(["ids"], [(h, half(T.outI, n, h), half(T.inf, n + 1, there[h])) for h in range(2)], ["inf%d" % (n + 1)])

    def meanwhile():
        if later:
            later.pop(0)()

    for n in range(NR):
        last = n == NR - 1
        an, fn = "al%d" % n, "inf%d" % n
        wn = V + NT * (n + 1)
        AD, YD, SD = (["%s%d" % (s, j) for j in range(n + 1)] + [s + "0b"] for s in ("ad", "yd", "sd"))
        if n > 0:
            copies(2 * n + 1, "a")
            copies(2 * n, "g")
            if not last:
                dma("s", ["c%d" % (2 * n), "c%d" % (2 * n + 1)], ["yd%d" % n], T.yw[:, spare(n)], T.cL[:, 2 * n:2 * n + 2, 0:HALF])
                dma("s", [an], ["ad%d" % n], T.aw[:, spare(n)], T.alL[:, n, :])
            for bk, two in banks:
                if bk:
                    ties(bk, two)
        mm(pb[0][:, 0:128], T.ones[0:1, 0:128], T.kc[0:1, 0:128], True, False, ["ones", "kc"], ["pb0"])
        mm(pb[1][:, 0:64], T.ones[0:1, 0:128], T.kc[0:1, 0:64], True, False, ["ones", "kc"], ["pb1"])
        for h in range(2):
            keyed(h, lambda a, b: T.ones[0:8, a:b], lambda a, b: T.th8[0:8, a:b, :], None, False, ["ones", "th8"])
        lag = 3 if n == 0 else 0
        achunks = ((0, 8), (8, 16), (16, 24)) + (((24, 27), (27, 29)) if lag else ((24, 28), (28, 30), (30, 32)))

        def slot(a):
            return 2 * n + 1 - a // 16

        def offs(a, b):
            return T.off[:, slot(a), 6 * (a % 16):6 * (a % 16 + b - a)]

        def rows_of(a, b):
            return T.sg[:, HALF * a:HALF * b], T.sw[:, 0:V].indirect(offs(a, b))

        def own(j):
            keyed(slot(j) % 2, lambda a, b: T.sg[:, HALF * j + a:HALF * j + b], lambda a, b: T.ws[:, a:b], j % 16, j % 16 == 15,
                  ["sg%d" % j, "ws"])

        for (a, b) in achunks:
            if b <= 32 - lag:
                ac(*rows_of(a, b), AF.Copy, S6 + ["off%d" % slot(a)], ["sg%d" % j for j in range(a, b)])
        jdone = 0
        for (a, b) in chunks:
            s = slot(a)
            cn = "c%d" % s
            if a % 16 == 0:
                keyed(s % 2, lambda a, b: T.cL[:, s, a:b], lambda a, b: T.wsc[:, a:b, :], None, False, [cn, "wsc"])
            ck = [cn] + ([cn + "b"] if b - a > 1 else []) + ([cn + "c"] if b - a > 2 else [])
            tt(T.mx[:, HALF * a:HALF * b], T.xw[:].indirect(offs(a, b)), T.cL[:, s, 0:HALF * (b - a)], ALU.max,
               X3 + ["off%d" % s] + ck, MX[a:b])
            for j in range(a, b):
                keyed(s % 2, lambda a, b: T.mx[:, HALF * j + a:HALF * j + b], lambda a, b: T.wm[:, a:b], j % 16, False, [MX[j], "wm"])
            upto = max([0] + [e for (_, e) in achunks if e + lag <= b])
            for j in range(jdone, upto):
                own(j)
            jdone = upto
            if n == 0 and b == 20:
                for bk, two in banks:
                    if bk:
                        ties(bk, two)
        if lag:
            cp(*rows_of(jdone, 32), S6 + ["off%d" % slot(jdone)], ["sg%d" % j for j in range(jdone, 32)])
            for j in range(jdone, 32):
                own(j)
        meanwhile()
        if n == 0:
            for w in WFV + [T.wg]:
                aset(w[:], T.ones[:, 0:128], 0.0, ["wf"] * (w is T.wg))
        else:
            ac(T.outI[:, n - 1, :], pb[2][:, 0:NT], AF.Copy, ["pb2"], ["ids"])
            send_ids(n - 1)
        ac(T.spc[:, 1, :], T.spc[:, 0, :], AF.Identity, ["spa", "spb", "g84"], ["spc"], scale=1.0 / FAM, bias=T.g8[:, 4 + n:5 + n])
        for bk, a, b in ((1, 128, NT), (0, 0, 128)):
            op("v", ["pb%d" % bk, "rm"], ["scn%d" % bk] + ["r1", "r64"] * bk,
               lambda: vec.tensor_tensor_scan(T.scn[:, a:b], T.rm[:, a:b], pb[bk][:, 0:b - a], 0.0, ALU.mult, ALU.max))
        meanwhile()
        key, r64, r1 = T.scn[:, 15::16], T.scn[:, 14::16], T.scn[:, 13::16]
        SCN = ["scn0", "scn1"]
        ts(r64, key, ROUND_64, ROUND_64, ALU.add, ALU.subtract, SCN, ["r64"])
        ts(r1, key, ROUND_1, ROUND_1, ALU.add, ALU.subtract, SCN, ["r1"])
        ts(T.gi[:], key, 0.5, 1.0 / GS, ALU.add, ALU.mult, SCN, ["gi"])
        tt(row(4), key, r64, ALU.subtract, SCN + ["r64"], ["dl"])
        tt(row(3), r64, r1, ALU.subtract, ["r1", "r64"], ["dh"])
        cp(row(5), T.gi[:], ["gi"], ["dg"])
        DD = DW + ["dh", "dl", "dg", "idb"]

        def turn(o, t0, odd, shift, start, stop, bk):
            c0 = D0 + 32 * t0 + shift - 16 * odd
            p = slice(0, 128) if t0 < 8 else slice(64 * odd, 64 * odd + 64)
            mm(o, T.dd[:, c0:c0 + 128], T.idb[:, p], start, stop, DD, ["pb%d" % bk])

        turn(pb[2][:, 0:128], 0, 0, 0, True, True, 2)
        turn(pb[2][:, 128:256], 4, 1, 0, True, True, 2)
        turn(pb[1][:, 0:128], 0, 0, 3, True, False, 1)
        turn(pb[1][:, 0:128], 4, 1, 3, False, True, 1)
        turn(pb[1][:, 128:NT], 8, 0, 3, True, False, 1)
        turn(pb[1][:, 128:NT], 8, 1, 3, False, True, 1)
        turn(pb[0][:, 0:64], 8, 0, 0, True, True, 0)
        turn(pb[0][:, 64:128], 8, 1, 0, True, True, 0)
        meanwhile()
        ac(T.ll[:, 0:256], pb[2][:, 0:256], AF.Copy, ["pb2"], ["le"])
        cp(T.rb[:, 0:NT], pb[1][:, 0:NT], ["pb1"], ["rb"])
        ac(T.ll[:, 256:2 * NT], pb[0][:, 0:128], AF.Copy, ["pb0"], ["lo"])
        meanwhile()

        def pairs(t):
            bk, s = place[t]
            if s and t >= 8:
                need("p", [lastw["pb%d" % bk][0:2] + ("tile",)])
            p0, c0 = 32 * (t % 4), 128 * (t // 4)
            mm(pb[bk][:, NU * s:NU * (s + 1)], T.ll[p0:p0 + 32, c0:c0 + 128], T.rb[p0:p0 + 32, 0:NU], False, s == 1,
               [("le", "le", "lo")[t // 4], "rb", "rbx"], ["pb%d" % bk])

        parts = ((1, 0, 8, 0), (2, 8, 4, 64))

        def families(j):
            bk, t0, nt, c0 = parts[j]
            c0 += 32 * j * last
            mm(pb[bk][:, 0:8 * nt], T.ones[0:1, 0:128], T.cst[0:1, c0:c0 + 8 * nt], True, False, ["ones"] + CST, ["pb%d" % bk])
            for a in range(8):
                for r in (3, 4):
                    mm(pb[bk][:, nt * a:nt * (a + 1)], T.pick[:, a, :], row(r, t0, t0 + nt), False, False, PK + ["dh", "dl"], ["pb%d" % bk])

        def losses(j):
            bk, t0, nt, c0 = parts[j]
            for a in range(8):
                mm(pb[bk][:, nt * a:nt * (a + 1)], T.pick[:, a, :], T.res[:, t0:t0 + nt], False, a == 7,
                   PK + ["res%d" % t for t in range(t0, t0 + nt)], ["pb%d" % bk])

        def least(j):
            bk, t0, nt, c0 = parts[j]
            tt(T.conv[:, c0:c0 + 8 * nt], pb[bk][:, 0:8 * nt], T.spc[:, 1, c0:c0 + 8 * nt], ALU.min, ["pb%d" % bk, "spc"], ["conv%d" % j])

        LN = ["lst%d_%d" % (n, h) for h in range(2)]

        def columns(h):
            ts(T.lst[:, n, 6 * h:6 * h + 16], T.conv[:, 0:64 + 32 * h].indirect(T.gl2[:, 2 * h:2 * h + 1]), FAM, float(MID), ALU.mult, ALU.add,
               ["conv0", "gl2", "gl2b"] + ["conv1", LN[0]] * h, [LN[h]])

        for t in (0, 4, 3, 7, 1, 5, 2, 6):
            pairs(t)
        pairs(8)
        ties(*banks[5])
        pairs(9)
        pairs(10)
        families(0)
        pairs(11)

        def tile(t):
            bk, s = place[t]
            return pb[bk][:, NU * s:NU * (s + 1)], "pb%d" % bk

        def by_scalar(j):
            t = on_scalar[j]
            src, bk = tile(t)
            a, b = T.sg2[:, 2 * j:2 * j + 1], T.sg2[:, 2 * j + 1:2 * j + 2]
            ac(T.junk[:, 0, 0:NU], src, AF.Sign, [bk], ["junk0", "sa%d" % j], bias=WIN - 0.5, accum_out=a)
            ac(T.junk[:, 1, 0:NU], src, AF.Sign, [bk], ["junk1", "sb%d" % j], scale=-1.0, bias=WIN, accum_out=b)

        def sum_scalar(j):
            t = on_scalar[j]
            ac(T.res[:, t:t + 1], T.sg2[:, 2 * j:2 * j + 1], AF.Identity, ["sa%d" % j, "sb%d" % j], ["res%d" % t],
               bias=T.sg2[:, 2 * j + 1:2 * j + 2])

        def by_vector(t):
            src, bk = tile(t)
            op("v", [bk], ["res%d" % t],
               lambda: vec.tensor_reduce(T.res[:, t:t + 1], src, AX.X, ALU.min, negate=True, apply_absolute_value=True))

        for t in (0, 4, 1, 5, 2, 6):
            by_vector(t)
        by_scalar(0)
        by_scalar(1)
        sum_scalar(0)
        sum_scalar(1)
        ac(T.sw[:, spare(n)], T.inf[:, n, :], AF.Identity, [fn, "col%d" % C_ID], ["sd%d" % n], scale=col(C_ID))
        losses(0)
        families(1)
        by_vector(8)
        by_vector(9)
        if last:
            ac(T.leno[:], T.inf[:, n, :], AF.Identity, [fn, "col%d" % C_LEN], ["leno"], scale=col(C_LEN))
            by_vector(10)
            by_vector(11)
        else:
            by_scalar(2)
            sum_scalar(2)
        least(0)
        meanwhile()
        columns(0)
        if not last:
            by_vector(11)
        meanwhile()
        s0, s1 = 2 * n + 2, 2 * n + 3

        def lh(h):
            return T.lst[:, n, 6 * h:6 * (h + 1)]

        def cut(h):
            return slice(HALF * h, HALF * (h + 1))

        def take_lists(h):
            cp(T.oa[:, s0 + h, 16:16 + HALF], T.aw[:, 0:wn].indirect(lh(h)), ["aw", LN[h]] + AD, ["oa%d" % (s0 + h)])

        def take_features(h):
            ac(half(T.outC, n, h), T.yw[:, 0:wn].indirect(lh(h)), AF.Copy, Y3 + YD + [LN[h]], ["oc%d" % (s0 + h)])

        def take_rows(h):
            ac(T.raw[:, cut(h)], T.sw[:, 0:wn].indirect(lh(h)), AF.Copy, S6 + SD + [LN[h]], ["raw%d" % h])

        def new_rows(h, which):
            o, bk = pb[3 + 2 * h][:, 0:HALF], "pb%d" % (3 + 2 * h)
            if which == 0:
                mm(o, T.wf1[:], half(T.inf, n, h), True, False, WF8 + [fn], [bk])
                mm(o, T.wg[:], T.rb[:, cut(h)], False, False, ["wg", "rb"], [bk])
            elif which == 1:
                mm(o, T.wf0[:], T.raw[:, cut(h)], False, True, WF8 + ["raw%d" % h], [bk])
            else:
                ac(T.vv[:, cut(h)], o, AF.Identity, [bk, "col%d" % C_TH], ["vv%d" % h], bias=col(C_TH))

        def take_ids(h):
            tt(half(T.outI, n, h), T.sw[:, 0:wn].indirect(lh(h)), T.leno[:, cut(h)], ALU.add, S6 + SD + [LN[h], "leno"], ["oi%d" % h])

        if not last:
            take_lists(0)
            take_features(0)
            send(["oc%d" % s0], [(0, half(T.outC, n, 0), T.cL[:, s1, 0:HALF])], ["c%d" % s1])
            new_rows(0, 0)
            losses(1)
            new_rows(1, 0)
            take_rows(0)
            new_rows(0, 1)
            new_rows(0, 2)
            turns(s0, (0,))
            least(1)
            turns(s0, (1,))
            columns(1)
            offsets(s0, T.outO, "oo")
            send(["oo%d" % s0], [(0, T.outO[:, s0, :], T.off[:, s1, :])], ["off%d" % s1])
            take_rows(1)
            new_rows(1, 1)
            take_features(1)
            send(["oc%d" % s1], [(1, half(T.outC, n, 1), T.cL[:, s0, 0:HALF])], ["c%d" % s0])
            new_rows(1, 2)
            take_lists(1)
            cp(T.sw[:, 0:wn].indirect(lh(0)), T.vv[:, cut(0)], ["vv0", LN[0]], S6 + SD)
            turns(s1)
            cp(T.sw[:, 0:wn].indirect(lh(1)), T.vv[:, cut(1)], ["vv1", LN[1]], S6 + SD)
            offsets(s1, T.outO, "oo")
            send(["oo%d" % s1], [(1, T.outO[:, s1, :], T.off[:, s0, :])], ["off%d" % s0])
            if n < NR - 2:
                send(["oa%d" % s0, "oa%d" % s1], [(h, T.oa[:, s0 + h, 16:16 + HALF], half(T.alL, n + 1, there[h])) for h in range(2)],
                     ["al%d" % (n + 1)])
            o = pb[2][:, 0:NT]
            if n:
                mm(o, T.wf2[:], T.inf[:, n, :], True, False, WF8 + [fn], ["pb2"])
            mm(o, T.wf3[:], T.raw[:], n == 0, True, WF8 + ["raw0", "raw1"], ["pb2"])

            def features(a, b, n=n, wn=wn, YD=YD, LN=LN):
                s, c0 = 2 * n + a // 6, 16 * (a % 6)
                cp(T.yw[:, 0:wn].indirect(T.lst[:, n, a:b]), T.cL[:, s, c0:c0 + 16 * (b - a)], ["c%d" % s] + LN, Y3 + YD)

            def applicants(a, b, n=n, wn=wn, AD=AD, LN=LN):
                cp(T.aw[:, 0:wn].indirect(T.lst[:, n, a:b]), T.alL[:, n, 16 * a:16 * b], ["al%d" % n] + LN, ["aw"] + AD)

            if n < NR - 2:
                later += [lambda f=applicants: f(0, 4), lambda f=features: f(4, 6), lambda f=applicants, f2=features: (f(4, 12), f2(0, 2)),
                          lambda f=features: f(6, 12), lambda f=features: f(2, 4), lambda: None]
        else:
            losses(1)
            least(1)
            take_ids(0)
            send(["oi0"], [(0, half(T.outI, n, 0), half(T.inf, NR, flip))], ["end0"])
            columns(1)
            take_ids(1)
            send(["oi1"], [(1, half(T.outI, n, 1), half(T.inf, NR, 1 - flip))], ["end1"])
            cp(T.sw[:, 0:wn].indirect(T.lst[:, n, 0:12]), T.inf[:, n, :], [fn] + LN, S6 + SD)

    dma("s", S6, ["yh"], T.yh[:], T.sw[R_ID::16, 0:V])
    dma("a", ["end0", "end1"], ["yt"], T.yt[:], T.inf[R_ID::16, NR, :])
    dma("s", ["end0", "end1"], ["yl"], T.yl[:], T.inf[R_LEN::16, NR, :])
    need("g", [(sem, val, "end") for sem, val in count.items()])
